import numpy as np
import ml_dtypes


def mxq(x, axis, fmt="e4m3"):
    dtype, down = {"e4m3": (ml_dtypes.float8_e4m3fn, 7), "e5m2": (ml_dtypes.float8_e5m2, 14)}[fmt]
    v = np.moveaxis(np.asarray(x, np.float32).astype(ml_dtypes.bfloat16).astype(np.float64), axis, -1)
    blocks = v.reshape(v.shape[:-1] + (-1, 32))
    amax = np.abs(blocks).max(-1, keepdims=True)
    byte = np.maximum(np.where(amax > 0, np.frexp(amax)[1] - 1 + 127, 0) - down, 1)
    scale = np.exp2(byte - 127.0)
    codes = (blocks / scale).astype(np.float32).astype(dtype).astype(np.float64)
    return np.moveaxis((codes * scale).reshape(v.shape), -1, axis)


WIDE = False


def mx_kscale(k):
    if not WIDE:
        return np.ones(k)
    levels = np.array([10, -10, 5, -5, 0])
    if k % 512:
        return np.exp2(np.random.permutation(np.resize(levels, k // 32))).repeat(32)
    a = np.empty((k // 512, 16))
    for p in range(k // 512):
        a[p, :8] = np.random.permutation(np.resize(levels, 8))
        for g in range(8):
            far = levels[np.abs(levels - a[p, g]) >= 10]
            a[p, g + 8] = far[np.random.randint(len(far))]
    return np.exp2(a.ravel()).repeat(32)


def f64(x):
    return np.asarray(x).astype(np.float64)


def striped(idx):
    return np.tile(idx.reshape(-1, 16).T, (8, 1)).astype(np.uint16)


def unstriped(offs):
    return offs[:16].T.reshape(-1).astype(np.int64)


E2M1 = np.array([0.0, 0.5, 1.0, 1.5, 2.0, 3.0, 4.0, 6.0, -0.0, -0.5, -1.0, -1.5, -2.0, -3.0, -4.0, -6.0])


def pack_weight(w, fmt):
    k, n = w.shape
    w = f64(np.asarray(w, np.float32).astype(ml_dtypes.bfloat16)).reshape(k // 32, 32, n)
    amax = np.abs(w).max(1)
    if fmt == "e4m3":
        byte = np.frexp(amax)[1] - 1 + 127 - 7
    else:
        mant, ex = np.frexp(amax / 6.0)
        byte = np.where(mant > 0.5, ex, ex - 1) + 127
    byte = np.clip(np.where(amax > 0, byte, 1), 1, 254)
    scaled = (w * np.exp2(127.0 - byte)[:, None, :]).reshape(k, n).astype(np.float32)
    by_word = np.ascontiguousarray(scaled.reshape(k // 512, 128, 4, n).transpose(0, 1, 3, 2))
    if fmt == "e4m3":
        words = by_word.astype(ml_dtypes.float8_e4m3fn).view(np.uint8)
    else:
        c = by_word.astype(ml_dtypes.float4_e2m1fn).view(np.uint8) & 0xF
        words = (c[..., 0::2] | (c[..., 1::2] << 4)).reshape(k // 512, 128, 2 * n)
    return np.ascontiguousarray(words), np.ascontiguousarray(byte.astype(np.uint8).reshape(k // 512, 16, n))


def unpack_weight(words, scales, fmt):
    g, _, n = scales.shape
    words = np.ascontiguousarray(words).reshape(g, 128, n, -1)
    if fmt == "e4m3":
        vals = words.view(ml_dtypes.float8_e4m3fn).astype(np.float64)
    else:
        nib = np.empty((g, 128, n, 4), np.uint8)
        nib[..., 0::2] = words & 0xF
        nib[..., 1::2] = words >> 4
        vals = E2M1[nib]
    vals = vals * np.repeat(np.exp2(scales.astype(np.float64) - 127.0), 8, axis=1)[..., None]
    return vals.transpose(0, 1, 3, 2).reshape(g * 512, n)


def gelu(v):
    return 0.5 * v * (1.0 + np.tanh(np.sqrt(2.0 / np.pi) * (v + 0.044715 * v**3)))


K, T, S, H, N, T2 = 1024, 4096, 1024, 512, 1024, 2048

def setup_inputs():
    n = np.random.standard_normal
    s = mx_kscale(K)[:, None]
    u = mx_kscale(H)[:, None]
    tab_words, tab_scales = pack_weight(n((K, T)) * s, "e4m3")
    tab2_words, tab2_scales = pack_weight(n((K, T)) * s, "e4m3")
    w2_words, w2_scales = pack_weight(n((K, H)) / np.sqrt(K) / s * u.T, "e2m1")
    w3_words, w3_scales = pack_weight(n((K, H)) / np.sqrt(K) / s * u.T, "e4m3")
    perm = np.random.permutation(T2)
    return {
        "tab_words": tab_words, "tab_scales": tab_scales,
        "tab2_words": tab2_words, "tab2_scales": tab2_scales,
        "offs": striped(np.random.permutation(T)[:S]),
        "offs2": striped(np.random.permutation(T)[:S]),
        "offs3": striped(perm[:S]), "offs4": striped(perm[S:]),
        "w1": (n((K, H)) / np.sqrt(K) / s * u.T).astype(np.float32),
        "w2_words": w2_words, "w2_scales": w2_scales,
        "w3_words": w3_words, "w3_scales": w3_scales,
        "rate": np.random.uniform(0.3, 0.9, H).astype(np.float32),
        "wall": (n(H) * u[:, 0]).astype(np.float32),
        "wg1": np.exp(0.3 * n((128, S))).astype(np.float32),
        "wg2": np.exp(0.3 * n((128, S))).astype(np.float32),
        "w4": (n((H, N)) / np.sqrt(H) / u).astype(np.float32),
    }

def reference(tab_words, tab_scales, tab2_words, tab2_scales, offs, offs2, offs3, offs4, w1,
              w2_words, w2_scales, w3_words, w3_scales, rate, wall, wg1, wg2, w4):
    v = unpack_weight(tab_words, tab_scales, "e4m3")[:, unstriped(offs)]
    v2 = unpack_weight(tab2_words, tab2_scales, "e4m3")[:, unstriped(offs2)]
    mom = mxq(f64(w1), 0, "e4m3").T @ v
    eq = unpack_weight(w2_words, w2_scales, "e2m1").T @ v
    h1 = mom + f64(rate)[:, None] * (eq - mom)
    h2 = f64(wall)[:, None] - (unpack_weight(w3_words, w3_scales, "e4m3").T @ v2)
    page = np.zeros((H, T2))
    page[:, unstriped(offs3)] = np.tile(f64(wg1), (H // 128, 1)) * h1
    page[:, unstriped(offs4)] = np.tile(f64(wg2), (H // 128, 1)) * h2
    return mxq(f64(w4), 0, "e4m3").T @ mxq(page, 0, "e4m3")

@@ -1,0 +1,351 @@
+from contextlib import ExitStack
+
+import concourse.mybir as mybir
+from concourse.masks import make_identity
+
+K, T, S, H, N, T2 = 1024, 4096, 1024, 512, 1024, 2048
+FLOPS = 2 * (3 * K * H * S + H * N * T2)
+
+F32 = mybir.dt.float32
+BF16 = mybir.dt.bfloat16
+I32 = mybir.dt.int32
+U32 = mybir.dt.uint32
+U16 = mybir.dt.uint16
+U8 = mybir.dt.uint8
+FP8X4 = mybir.dt.float8_e4m3fn_x4
+FP4X4 = mybir.dt.float4_e2m1fn_x4
+MULT = mybir.AluOpType.mult
+COPY = mybir.ActivationFunctionType.Copy
+IDENTITY = mybir.ActivationFunctionType.Identity
+
+P = 128
+PACK = 4
+PASSES = K // (P * PACK)
+BANK = 512
+HALVES = S // BANK
+KIB = 1024
+QUADRANTS = (0, 2, 1, 3)
+PAGE_CHUNKS = ((0, 256), (256, 512), (512, 1024), (1024, 1536), (1536, 2048))
+
+
+def tile_list_lattice_boltzmann_step_kernel(
+    tc, tab_words, tab_scales, tab2_words, tab2_scales, offs, offs2, offs3, offs4, w1,
+    w2_words, w2_scales, w3_words, w3_scales, rate, wall, wg1, wg2, w4, out,
+):
+    nc = tc.nc
+    with ExitStack() as ctx:
+        lists = ctx.enter_context(tc.tile_pool(name="lists", bufs=1))
+        keep = ctx.enter_context(tc.tile_pool(name="keep", bufs=1))
+        arena = ctx.enter_context(tc.tile_pool(name="arena", bufs=1))
+        psum = ctx.enter_context(tc.psum_pool(name="psum", bufs=8))
+
+        def held(name, shape, dtype):
+            return keep.tile(shape, dtype, name=name, align_bytes=64)
+
+        def placed(name, shape, dtype, kib):
+            return arena.tile(shape, dtype, name=name, offset=kib * KIB, align_bytes=64)
+
+        def bank():
+            return psum.tile([P, BANK], F32, name="bank")
+
+        def load_list(name, src):
+            dst = lists.tile([P, S // 16], U16, name=name)
+            nc.sync.dma_start(dst[:], src)
+            return dst
+
+        def load_words(name, words, a, kib):
+            dst = placed(name, [P, T], I32, kib)
+            nc.sync.dma_start(out=dst[:], in_=words[a].rearrange("p t i -> p (t i)").bitcast(I32))
+            return dst
+
+        def load_packed_scales(queue, dst, scales):
+            for q in QUADRANTS:
+                queue.dma_start(
+                    out=dst[32 * q : 32 * q + 8, :], in_=scales.bitcast(I32)[:, 4 * q : 4 * q + 4, :]
+                )
+
+        def load_weights(name, wg, t0, t1):
+            dst = held(name, [P, t1 - t0, S], F32)
+            rows = wg.rearrange("(p t) j -> p t j", t=PACK)
+            for q in QUADRANTS:
+                nc.sync.dma_start(out=dst[32 * q : 32 * q + 32], in_=rows[:, t0:t1, :])
+            return dst
+
+        def gather_scales(name, window, offsets):
+            picked = held(name, [P, S], U8)
+            nc.vector.tensor_copy(picked[:], window[:].bitcast(U8).indirect(offsets[:]))
+            return picked
+
+        def gather_words(dst, window, offsets, j0, j1):
+            nc.vector.tensor_copy(
+                dst[:, j0:j1], window[:].bitcast(U32).indirect(offsets[:, j0 // 16 : j1 // 16])
+            )
+
+        def interleave(engine_copy, dst, src):
+            engine_copy(
+                out=dst.rearrange("p (c i) t -> p c t i", i=4),
+                in_=src.rearrange("p t (c i) -> p c t i", i=4),
+            )
+
+        def quantize(codes, scales, grouped):
+            nc.vector.quantize_mx(
+                out=codes.bitcast(FP8X4), scales=scales, in_=grouped.rearrange("p c t -> p (c t)")
+            )
+
+        window2 = placed("window2", [P, T // 4], I32, 96)
+        window1 = placed("window1", [P, T // 4], I32, 100)
+        w3s_raw = held("w3s_raw", [P, H // 4], I32)
+        w2s = held("w2s", [P, PASSES, H // 4], I32)
+        shifted1 = held("shifted1", [P, S // 4], I32)
+        nc.gpsimd.memset(w3s_raw[:], 0)
+        nc.gpsimd.memset(w2s[:], 0)
+        for filled in (window2, window1, shifted1):
+            nc.vector.memset(filled[:], 0)
+        load_packed_scales(nc.gpsimd, window2, tab2_scales)
+        load_packed_scales(nc.gpsimd, window1, tab_scales)
+        ident = held("ident", [P, P], F32)
+        make_identity(nc, ident[:])
+
+        list2 = load_list("list2", offs2)
+        tab2_sb = [load_words("tab2_0", tab2_words, 0, 0)]
+        list1 = load_list("list1", offs)
+        w3_raw = held("w3_raw", [P, PASSES, H], I32)
+        nc.sync.dma_start(out=w3_raw[:], in_=w3_words.rearrange("a p c i -> p a (c i)").bitcast(I32))
+        load_packed_scales(nc.sync, w3s_raw, w3_scales)
+        tab2_sb.append(load_words("tab2_1", tab2_words, 1, 16))
+        list4 = load_list("list4", offs4)
+        wall_cols = held("wall_cols", [P, PACK], F32)
+        nc.sync.dma_start(out=wall_cols[:], in_=wall.rearrange("(p t) -> p t", t=PACK))
+        wg2_first = load_weights("wg2_0", wg2, 0, 1)
+        tab_sb = [load_words("tab_%d" % a, tab_words, a, 32 + 16 * a) for a in range(PASSES)]
+        wg2_second = load_weights("wg2_1", wg2, 1, 2)
+        w2_sb = held("w2_sb", [P, PASSES, H // 2], I32)
+        nc.sync.dma_start(out=w2_sb[:], in_=w2_words.bitcast(I32).rearrange("a p c -> p a c"))
+        w2s_rows = w2_scales.bitcast(I32).rearrange("a (q r) c -> r q a c", r=4)
+        for r in range(4):
+            nc.sync.dma_start(out=w2s[r:P:32], in_=w2s_rows[r])
+        rate_cols = held("rate_cols", [P, PACK], F32)
+        with nc.allow_non_contiguous_dma(reason="one rate a partition"):
+            nc.sync.dma_start(out=rate_cols[:], in_=rate.rearrange("(c p) -> p c", p=P))
+        w1_raw = []
+        for a in range(PASSES):
+            raw = placed("w1_raw%d" % a, [P, PACK, H], F32, 64 + 8 * a)
+            nc.sync.dma_start(
+                out=raw[:], in_=w1[512 * a : 512 * (a + 1), :].rearrange("(p t) c -> p t c", t=PACK)
+            )
+            w1_raw.append(raw)
+        wg2_late = load_weights("wg2_23", wg2, 2, 4)
+        list3 = load_list("list3", offs3)
+        wg1_sb = load_weights("wg1_sb", wg1, 0, 4)
+        w4_raw = placed("w4_raw", [P, PACK, N], F32, 80)
+        nc.sync.dma_start(out=w4_raw[:], in_=w4.rearrange("(p t) n -> p t n", t=PACK))
+        wg2_rows = [wg2_first[:, 0, :], wg2_second[:, 0, :], wg2_late[:, 0, :], wg2_late[:, 1, :]]
+
+        v2 = [held("v2_0", [P, S], U32), placed("v2_1", [P, S], U32, 100)]
+        gather_words(v2[0], tab2_sb[0], list2, 0, S)
+        v2s = gather_scales("v2s", window2, list2)
+        w3_sb = held("w3_sb", [P, PASSES, H], I32)
+        nc.vector.tensor_copy(
+            out=w3_sb[:].rearrange("p a (t c i) -> p a c t i", t=PACK, i=4),
+            in_=w3_raw[:].rearrange("p a (c i t) -> p a c t i", t=PACK, i=4),
+        )
+        w3s = held("w3s", [P, H], U8)
+        nc.vector.tensor_copy(
+            out=w3s[:].rearrange("p (t m) -> p t m", t=PACK),
+            in_=w3s_raw[:].bitcast(U8).rearrange("p (m t) -> p t m", t=PACK),
+        )
+        v1s_packed = gather_scales("v1s_packed", window1, list1)
+        nc.gpsimd.dma_start(out=shifted1[0:112, :], in_=v1s_packed[4:116, :].bitcast(I32))
+        v1s = [v1s_packed[:], shifted1[:].bitcast(U8)]
+        for h in range(HALVES):
+            gather_words(v2[1], tab2_sb[1], list2, h * BANK, (h + 1) * BANK)
+
+        page = {t: placed("page%d" % t, [P, T2], F32, kib) for t, kib in ((0, 128), (1, 48), (3, 56))}
+        h2 = [held("h2_%d" % t, [P, S], F32) for t in range(PACK)]
+
+        def wall_term(t, h):
+            cols = slice(h * BANK, (h + 1) * BANK)
+            rows = slice(t * P, (t + 1) * P)
+            acc = bank()
+            for a in range(PASSES):
+                nc.tensor.matmul_mx(
+                    out=acc[:],
+                    lhsT=w3_sb[:, a, rows].bitcast(FP8X4),
+                    lhsT_scale=w3s[4 * a : P, rows],
+                    rhs=v2[a][:, cols].bitcast(FP8X4),
+                    rhs_scale=v2s[4 * a : P, cols],
+                    start=(a == 0),
+                    stop=(a == PASSES - 1),
+                )
+            nc.scalar.activation(h2[t][:, cols], acc[:], IDENTITY, bias=wall_cols[:, t : t + 1], scale=-1.0)
+
+        def scatter(t, offsets, j0, j1, values, weights):
+            nc.vector.tensor_tensor(
+                page[t][:].indirect(offsets[:, j0 // 16 : j1 // 16]), values, weights, MULT
+            )
+
+        for t in range(PACK):
+            for h in range(HALVES):
+                wall_term(t, h)
+        for h in range(HALVES):
+            cols = slice(h * BANK, (h + 1) * BANK)
+            scatter(0, list4, h * BANK, (h + 1) * BANK, h2[0][:, cols], wg2_rows[0][:, cols])
+
+        v1 = [held("v1_%d" % a, [P, S], U32) for a in range(PASSES)]
+        for a in range(PASSES):
+            gather_words(v1[a], tab_sb[a], list1, 0, S)
+        scatter(1, list4, 0, S, h2[1][:], wg2_rows[1])
+        w1_codes = held("w1_codes", [P, PASSES, H], U32)
+        w1s = held("w1s", [P, PASSES, H], U8)
+        for a in range(PASSES):
+            grouped = placed("w1_grouped%d" % a, [P, BANK, PACK], BF16, 120 + 4 * a)
+            interleave(nc.scalar.copy, grouped[:], w1_raw[a][:])
+            quantize(w1_codes[:, a, :], w1s[:, a, :], grouped[:])
+        page[2] = placed("page2", [P, T2], F32, 120)
+        for t in range(2, PACK):
+            scatter(t, list4, 0, S, h2[t][:], wg2_rows[t])
+
+        kept_cols = held("kept_cols", [P, PACK], F32)
+        nc.scalar.activation(kept_cols[:], rate_cols[:], COPY, bias=1.0, scale=-1.0)
+        w2_bytes = w2_sb[:].bitcast(U8)
+        w2s_bytes = w2s[:].bitcast(U8)
+
+        def scaled_product(name, kib, weights, weight_scales, h, factor):
+            cols = slice(h * BANK, (h + 1) * BANK)
+            acc = bank()
+            for a in range(PASSES):
+                nc.tensor.matmul_mx(
+                    out=acc[:],
+                    lhsT=weights[a],
+                    lhsT_scale=weight_scales[a],
+                    rhs=v1[a][:, cols].bitcast(FP8X4),
+                    rhs_scale=v1s[a][:, cols],
+                    start=(a == 0),
+                    stop=(a == PASSES - 1),
+                )
+            term = placed(name, [P, BANK], F32, kib)
+            nc.scalar.activation(term[:], acc[:], COPY, scale=factor)
+            return term
+
+        relaxed = {}
+        for h in range(HALVES):
+            for c in range(PACK):
+                relaxed[h, c] = scaled_product(
+                    "relaxed%d%d" % (h, c), 16 * h + 4 * c + 2,
+                    [w2_bytes[:, a, 2 * c * P : 2 * (c + 1) * P].bitcast(FP4X4) for a in range(PASSES)],
+                    [w2s_bytes[:, a, c * P : (c + 1) * P] for a in range(PASSES)],
+                    h, rate_cols[:, c : c + 1],
+                )
+        h1 = []
+        for h in range(HALVES):
+            terms = []
+            for c in range(PACK):
+                kept = scaled_product(
+                    "kept%d%d" % (h, c), 16 * h + 4 * c,
+                    [w1_codes[:, a, c * P : (c + 1) * P].bitcast(FP8X4) for a in range(PASSES)],
+                    [w1s[:, a, c * P : (c + 1) * P] for a in range(PASSES)],
+                    h, kept_cols[:, c : c + 1],
+                )
+                terms.append((kept, relaxed[h, c]))
+            h1_half = placed("h1_%d" % h, [P, PACK, BANK], F32, 64 + 8 * h)
+            for b in range(BANK // P):
+                block = slice(b * P, (b + 1) * P)
+                summed = bank()
+                for c in range(PACK):
+                    for n_term, term in enumerate(terms[c]):
+                        nc.tensor.matmul(
+                            summed[:, c * P : (c + 1) * P], lhsT=term[:, block], rhs=ident[:],
+                            is_transpose=True, start=(n_term == 0), stop=(n_term == 1),
+                        )
+                turned = placed("turned%d%d" % (h, b), [P, PACK, P], F32, 96 + 2 * b)
+                nc.scalar.copy(out=turned[:], in_=summed[:].rearrange("p (m t) -> p t m", t=PACK))
+                back = bank()
+                for t in range(PACK):
+                    nc.tensor.transpose(back[:, t * P : (t + 1) * P], turned[:, t, :], ident[:])
+                nc.scalar.copy(out=h1_half[:, :, block], in_=back[:].rearrange("p (t j) -> p t j", t=PACK))
+            h1.append(h1_half)
+        for h in range(HALVES):
+            cols = slice(h * BANK, (h + 1) * BANK)
+            for t in range(PACK):
+                scatter(t, list3, h * BANK, (h + 1) * BANK, h1[h][:, t, :], wg1_sb[:, t, cols])
+
+        w4_codes = held("w4_codes", [P, N], U32)
+        w4s = held("w4s", [P, N], U8)
+        for n0 in range(0, N, BANK):
+            grouped = placed("w4_grouped%d" % n0, [P, BANK, PACK], BF16, 24 + n0 // 128)
+            interleave(nc.scalar.copy, grouped[:], w4_raw[:, :, n0 : n0 + BANK])
+            quantize(w4_codes[:, n0 : n0 + BANK], w4s[:, n0 : n0 + BANK], grouped[:])
+
+        rounded = [
+            placed("rounded%d" % m0, [P, PACK, m1 - m0], BF16, m0 // 128) for m0, m1 in PAGE_CHUNKS
+        ]
+        for t in range(PACK - 1):
+            for g, (m0, m1) in enumerate(PAGE_CHUNKS):
+                nc.scalar.copy(out=rounded[g][:, t, :], in_=page[t][:, m0:m1])
+        page_codes = placed("page_codes", [P, T2], U32, 96)
+        page_s = held("page_s", [P, T2], U8)
+        for g, (m0, m1) in enumerate(PAGE_CHUNKS):
+            engine_copy = nc.scalar.copy if g == 1 else nc.vector.tensor_copy
+            engine_copy(out=rounded[g][:, PACK - 1, :], in_=page[PACK - 1][:, m0:m1])
+            grouped = placed("page_grouped%d" % m0, [P, m1 - m0, PACK], BF16, 16 + m0 // 128)
+            interleave(engine_copy, grouped[:], rounded[g][:])
+            quantize(page_codes[:, m0:m1], page_s[:, m0:m1], grouped[:])
+
+        staged = [placed("staged%d" % u, [P, 2, T2], F32, (32, 104, 64, 80)[u]) for u in range(4)]
+        out_rows = out.rearrange("(u e p) m -> u p e m", e=2, p=P)
+        emptied = []
+
+        def product(dst, n, m0, m1):
+            nc.tensor.matmul_mx(
+                out=dst,
+                lhsT=w4_codes[:, n * P : (n + 1) * P].bitcast(FP8X4),
+                lhsT_scale=w4s[:, n * P : (n + 1) * P],
+                rhs=page_codes[:, m0:m1].bitcast(FP8X4),
+                rhs_scale=page_s[:, m0:m1],
+                start=True,
+                stop=True,
+            )
+
+        def empty(dst, src):
+            on_vector = len(emptied) >= 14 and len(emptied) % 2 == 1
+            (nc.vector.tensor_copy if on_vector else nc.scalar.copy)(out=dst, in_=src)
+            emptied.append(dst)
+
+        def pair_bank(u, m0, m1):
+            acc = bank()
+            for e in range(2):
+                product(acc[:, e * 256 : (e + 1) * 256], 2 * u + e, m0, m1)
+            empty(staged[u][:, :, m0:m1], acc[:].rearrange("p (e m) -> p e m", e=2))
+
+        def full_bank(n, m0):
+            acc = bank()
+            product(acc[:], n, m0, m0 + BANK)
+            empty(staged[n // 2][:, n % 2, m0 : m0 + BANK], acc[:])
+
+        def store(n, m0, m1):
+            nc.sync.dma_start(out=out_rows[n // 2][:, n % 2, m0:m1], in_=staged[n // 2][:, n % 2, m0:m1])
+
+        for n in range(4):
+            acc = bank()
+            product(acc[:, 0:256], n, 0, 256)
+            empty(staged[n // 2][:, n % 2, 0:256], acc[:, 0:256])
+            store(n, 0, 256)
+        for n in range(4, 8):
+            full_bank(n, 0)
+            store(n, 0, 512)
+        for u in range(2):
+            pair_bank(u, 256, 512)
+            for n in (2 * u, 2 * u + 1):
+                full_bank(n, 512)
+                store(n, 256, 1024)
+        for n in range(4, 8):
+            full_bank(n, 512)
+            full_bank(n, 1024)
+            store(n, 512, 1536)
+        for n in range(4):
+            full_bank(n, 1024)
+            full_bank(n, 1536)
+            store(n, 1024, 2048)
+        for n in range(4, 8):
+            full_bank(n, 1536)
+            store(n, 1536, 2048)

@@ -64,8 +64,7 @@ def tile_list_lattice_boltzmann_step_kernel(
                     out=dst[32 * q : 32 * q + 8, :], in_=scales.bitcast(I32)[:, 4 * q : 4 * q + 4, :]
                 )
 
-        def load_weights(name, wg, t0, t1):
-            dst = held(name, [P, t1 - t0, S], F32)
+        def load_weights(dst, wg, t0, t1):
             rows = wg.rearrange("(p t) j -> p t j", t=PACK)
             for q in QUADRANTS:
                 nc.sync.dma_start(out=dst[32 * q : 32 * q + 32], in_=rows[:, t0:t1, :])
@@ -96,29 +95,34 @@ def tile_list_lattice_boltzmann_step_kernel(
         window1 = placed("window1", [P, T // 4], I32, 100)
         w3s_raw = held("w3s_raw", [P, H // 4], I32)
         w2s = held("w2s", [P, PASSES, H // 4], I32)
-        shifted1 = held("shifted1", [P, S // 4], I32)
-        nc.gpsimd.memset(w3s_raw[:], 0)
-        nc.gpsimd.memset(w2s[:], 0)
-        for filled in (window2, window1, shifted1):
+        v1s_planes = held("v1s_planes", [P, PASSES, S // 4], I32)
+        nc.gpsimd.memset(window1[:], 0)
+        for filled in (window2, w3s_raw, w2s, v1s_planes):
             nc.vector.memset(filled[:], 0)
-        load_packed_scales(nc.gpsimd, window2, tab2_scales)
-        load_packed_scales(nc.gpsimd, window1, tab_scales)
+        warm = held("warm", [P, 2], F32)
+        nc.gpsimd.memset(warm[:], 0.0)
+        nc.scalar.activation(warm[:, 1:2], warm[:, 0:1], IDENTITY, bias=warm[:, 0:1], scale=-1.0)
         ident = held("ident", [P, P], F32)
         make_identity(nc, ident[:])
 
         list2 = load_list("list2", offs2)
         tab2_sb = [load_words("tab2_0", tab2_words, 0, 0)]
-        list1 = load_list("list1", offs)
+        tab2_rows = tab2_scales.bitcast(I32).rearrange("a (q r) t -> a r q t", r=4)
+        for a in range(PASSES):
+            for r in range(4):
+                nc.sync.dma_start(out=window2[4 * a + r : P : 32, :], in_=tab2_rows[a, r])
         w3_raw = held("w3_raw", [P, PASSES, H], I32)
         nc.sync.dma_start(out=w3_raw[:], in_=w3_words.rearrange("a p c i -> p a (c i)").bitcast(I32))
         load_packed_scales(nc.sync, w3s_raw, w3_scales)
+        list1 = load_list("list1", offs)
+        nc.sync.dma_start(out=window1[0:P:4, :], in_=tab_scales.bitcast(I32).rearrange("a q t -> (a q) t"))
         tab2_sb.append(load_words("tab2_1", tab2_words, 1, 16))
         list4 = load_list("list4", offs4)
         wall_cols = held("wall_cols", [P, PACK], F32)
         nc.sync.dma_start(out=wall_cols[:], in_=wall.rearrange("(p t) -> p t", t=PACK))
-        wg2_first = load_weights("wg2_0", wg2, 0, 1)
+        wg2_first = load_weights(held("wg2_0", [P, 1, S], F32), wg2, 0, 1)
         tab_sb = [load_words("tab_%d" % a, tab_words, a, 32 + 16 * a) for a in range(PASSES)]
-        wg2_second = load_weights("wg2_1", wg2, 1, 2)
+        wg2_second = load_weights(held("wg2_1", [P, 1, S], F32), wg2, 1, 2)
         w2_sb = held("w2_sb", [P, PASSES, H // 2], I32)
         nc.sync.dma_start(out=w2_sb[:], in_=w2_words.bitcast(I32).rearrange("a p c -> p a c"))
         w2s_rows = w2_scales.bitcast(I32).rearrange("a (q r) c -> r q a c", r=4)
@@ -134,12 +138,7 @@ def tile_list_lattice_boltzmann_step_kernel(
                 out=raw[:], in_=w1[512 * a : 512 * (a + 1), :].rearrange("(p t) c -> p t c", t=PACK)
             )
             w1_raw.append(raw)
-        wg2_late = load_weights("wg2_23", wg2, 2, 4)
         list3 = load_list("list3", offs3)
-        wg1_sb = load_weights("wg1_sb", wg1, 0, 4)
-        w4_raw = placed("w4_raw", [P, PACK, N], F32, 80)
-        nc.sync.dma_start(out=w4_raw[:], in_=w4.rearrange("(p t) n -> p t n", t=PACK))
-        wg2_rows = [wg2_first[:, 0, :], wg2_second[:, 0, :], wg2_late[:, 0, :], wg2_late[:, 1, :]]
 
         v2 = [held("v2_0", [P, S], U32), placed("v2_1", [P, S], U32, 100)]
         gather_words(v2[0], tab2_sb[0], list2, 0, S)
@@ -154,12 +153,19 @@ def tile_list_lattice_boltzmann_step_kernel(
             out=w3s[:].rearrange("p (t m) -> p t m", t=PACK),
             in_=w3s_raw[:].bitcast(U8).rearrange("p (m t) -> p t m", t=PACK),
         )
-        v1s_packed = gather_scales("v1s_packed", window1, list1)
-        nc.gpsimd.dma_start(out=shifted1[0:112, :], in_=v1s_packed[4:116, :].bitcast(I32))
-        v1s = [v1s_packed[:], shifted1[:].bitcast(U8)]
+        v1s_spread = gather_scales("v1s_spread", window1, list1)
+        for a in range(PASSES):
+            for r in range(4):
+                nc.sync.dma_start(
+                    out=v1s_planes[r:P:32, a, :],
+                    in_=v1s_spread[64 * a + 4 * r : 64 * a + 64 : 16, :].bitcast(I32),
+                )
+        v1s = [v1s_planes[:, a, :].bitcast(U8) for a in range(PASSES)]
         for h in range(HALVES):
             gather_words(v2[1], tab2_sb[1], list2, h * BANK, (h + 1) * BANK)
 
+        wg2_late = load_weights(placed("wg2_23", [P, 2, S], F32, 16), wg2, 2, 4)
+        wg2_rows = [wg2_first[:, 0, :], wg2_second[:, 0, :], wg2_late[:, 0, :], wg2_late[:, 1, :]]
         page = {t: placed("page%d" % t, [P, T2], F32, kib) for t, kib in ((0, 128), (1, 48), (3, 56))}
         h2 = [held("h2_%d" % t, [P, S], F32) for t in range(PACK)]
 
@@ -194,6 +200,7 @@ def tile_list_lattice_boltzmann_step_kernel(
         v1 = [held("v1_%d" % a, [P, S], U32) for a in range(PASSES)]
         for a in range(PASSES):
             gather_words(v1[a], tab_sb[a], list1, 0, S)
+        wg1_sb = load_weights(placed("wg1_sb", [P, PACK, S], F32, 32), wg1, 0, 4)
         scatter(1, list4, 0, S, h2[1][:], wg2_rows[1])
         w1_codes = held("w1_codes", [P, PASSES, H], U32)
         w1s = held("w1s", [P, PASSES, H], U8)
@@ -202,6 +209,8 @@ def tile_list_lattice_boltzmann_step_kernel(
             interleave(nc.scalar.copy, grouped[:], w1_raw[a][:])
             quantize(w1_codes[:, a, :], w1s[:, a, :], grouped[:])
         page[2] = placed("page2", [P, T2], F32, 120)
+        w4_raw = placed("w4_raw", [P, PACK, N], F32, 64)
+        nc.sync.dma_start(out=w4_raw[:], in_=w4.rearrange("(p t) n -> p t n", t=PACK))
         for t in range(2, PACK):
             scatter(t, list4, 0, S, h2[t][:], wg2_rows[t])
 
@@ -231,7 +240,7 @@ def tile_list_lattice_boltzmann_step_kernel(
         for h in range(HALVES):
             for c in range(PACK):
                 relaxed[h, c] = scaled_product(
-                    "relaxed%d%d" % (h, c), 16 * h + 4 * c + 2,
+                    "relaxed%d%d" % (h, c), 136 * h + 4 * c + 2,
                     [w2_bytes[:, a, 2 * c * P : 2 * (c + 1) * P].bitcast(FP4X4) for a in range(PASSES)],
                     [w2s_bytes[:, a, c * P : (c + 1) * P] for a in range(PASSES)],
                     h, rate_cols[:, c : c + 1],
@@ -241,13 +250,13 @@ def tile_list_lattice_boltzmann_step_kernel(
             terms = []
             for c in range(PACK):
                 kept = scaled_product(
-                    "kept%d%d" % (h, c), 16 * h + 4 * c,
+                    "kept%d%d" % (h, c), 136 * h + 4 * c,
                     [w1_codes[:, a, c * P : (c + 1) * P].bitcast(FP8X4) for a in range(PASSES)],
                     [w1s[:, a, c * P : (c + 1) * P] for a in range(PASSES)],
                     h, kept_cols[:, c : c + 1],
                 )
                 terms.append((kept, relaxed[h, c]))
-            h1_half = placed("h1_%d" % h, [P, PACK, BANK], F32, 64 + 8 * h)
+            h1_half = placed("h1_%d" % h, [P, PACK, BANK], F32, 80 + 8 * h)
             for b in range(BANK // P):
                 block = slice(b * P, (b + 1) * P)
                 summed = bank()
@@ -269,36 +278,41 @@ def tile_list_lattice_boltzmann_step_kernel(
             for t in range(PACK):
                 scatter(t, list3, h * BANK, (h + 1) * BANK, h1[h][:, t, :], wg1_sb[:, t, cols])
 
-        w4_codes = held("w4_codes", [P, N], U32)
+        w4_grouped = []
+        for u in range(N // BANK):
+            grouped = placed("w4_grouped%d" % u, [P, BANK, PACK], BF16, 8 + 4 * u)
+            interleave(nc.scalar.copy, grouped[:], w4_raw[:, :, u * BANK : (u + 1) * BANK])
+            w4_grouped.append(grouped)
+        w4_codes = [held("w4_codes0", [P, BANK], U32)]
         w4s = held("w4s", [P, N], U8)
-        for n0 in range(0, N, BANK):
-            grouped = placed("w4_grouped%d" % n0, [P, BANK, PACK], BF16, 24 + n0 // 128)
-            interleave(nc.scalar.copy, grouped[:], w4_raw[:, :, n0 : n0 + BANK])
-            quantize(w4_codes[:, n0 : n0 + BANK], w4s[:, n0 : n0 + BANK], grouped[:])
+        quantize(w4_codes[0][:], w4s[:, 0:BANK], w4_grouped[0][:])
 
         rounded = [
-            placed("rounded%d" % m0, [P, PACK, m1 - m0], BF16, m0 // 128) for m0, m1 in PAGE_CHUNKS
+            placed("rounded%d" % m0, [P, PACK, m1 - m0], BF16, 136 + m0 // 128) for m0, m1 in PAGE_CHUNKS
         ]
         for t in range(PACK - 1):
             for g, (m0, m1) in enumerate(PAGE_CHUNKS):
                 nc.scalar.copy(out=rounded[g][:, t, :], in_=page[t][:, m0:m1])
         page_codes = placed("page_codes", [P, T2], U32, 96)
         page_s = held("page_s", [P, T2], U8)
-        for g, (m0, m1) in enumerate(PAGE_CHUNKS):
-            engine_copy = nc.scalar.copy if g == 1 else nc.vector.tensor_copy
+
+        def round_last_slice(g, engine_copy):
+            m0, m1 = PAGE_CHUNKS[g]
             engine_copy(out=rounded[g][:, PACK - 1, :], in_=page[PACK - 1][:, m0:m1])
+
+        def quantize_page(g):
+            m0, m1 = PAGE_CHUNKS[g]
             grouped = placed("page_grouped%d" % m0, [P, m1 - m0, PACK], BF16, 16 + m0 // 128)
-            interleave(engine_copy, grouped[:], rounded[g][:])
+            interleave(nc.vector.tensor_copy, grouped[:], rounded[g][:])
             quantize(page_codes[:, m0:m1], page_s[:, m0:m1], grouped[:])
 
         staged = [placed("staged%d" % u, [P, 2, T2], F32, (32, 104, 64, 80)[u]) for u in range(4)]
         out_rows = out.rearrange("(u e p) m -> u p e m", e=2, p=P)
-        emptied = []
 
         def product(dst, n, m0, m1):
             nc.tensor.matmul_mx(
                 out=dst,
-                lhsT=w4_codes[:, n * P : (n + 1) * P].bitcast(FP8X4),
+                lhsT=w4_codes[n // 4][:, n % 4 * P : (n % 4 + 1) * P].bitcast(FP8X4),
                 lhsT_scale=w4s[:, n * P : (n + 1) * P],
                 rhs=page_codes[:, m0:m1].bitcast(FP8X4),
                 rhs_scale=page_s[:, m0:m1],
@@ -306,46 +320,57 @@ def tile_list_lattice_boltzmann_step_kernel(
                 stop=True,
             )
 
-        def empty(dst, src):
-            on_vector = len(emptied) >= 14 and len(emptied) % 2 == 1
-            (nc.vector.tensor_copy if on_vector else nc.scalar.copy)(out=dst, in_=src)
-            emptied.append(dst)
+        def half_bank(n, m0, engine_copy):
+            acc = bank()
+            product(acc[:, 0:256], n, m0, m0 + 256)
+            engine_copy(out=staged[n // 2][:, n % 2, m0 : m0 + 256], in_=acc[:, 0:256])
 
-        def pair_bank(u, m0, m1):
+        def pair_bank(u, m0, engine_copy):
             acc = bank()
             for e in range(2):
-                product(acc[:, e * 256 : (e + 1) * 256], 2 * u + e, m0, m1)
-            empty(staged[u][:, :, m0:m1], acc[:].rearrange("p (e m) -> p e m", e=2))
+                product(acc[:, e * 256 : (e + 1) * 256], 2 * u + e, m0, m0 + 256)
+            engine_copy(out=staged[u][:, :, m0 : m0 + 256], in_=acc[:].rearrange("p (e m) -> p e m", e=2))
 
-        def full_bank(n, m0):
+        def full_bank(n, m0, engine_copy):
             acc = bank()
             product(acc[:], n, m0, m0 + BANK)
-            empty(staged[n // 2][:, n % 2, m0 : m0 + BANK], acc[:])
+            engine_copy(out=staged[n // 2][:, n % 2, m0 : m0 + BANK], in_=acc[:])
 
         def store(n, m0, m1):
             nc.sync.dma_start(out=out_rows[n // 2][:, n % 2, m0:m1], in_=staged[n // 2][:, n % 2, m0:m1])
 
+        on_scalar, on_vector = nc.scalar.copy, nc.vector.tensor_copy
+        round_last_slice(0, on_vector)
+        quantize_page(0)
+        w4_codes.append(placed("w4_codes1", [P, BANK], U32, 136))
+        quantize(w4_codes[1][:], w4s[:, BANK:N], w4_grouped[1][:])
+        for g in range(1, 4):
+            round_last_slice(g, on_scalar)
+        for g in range(1, 3):
+            quantize_page(g)
         for n in range(4):
-            acc = bank()
-            product(acc[:, 0:256], n, 0, 256)
-            empty(staged[n // 2][:, n % 2, 0:256], acc[:, 0:256])
+            half_bank(n, 0, on_scalar)
             store(n, 0, 256)
+        round_last_slice(4, on_scalar)
         for n in range(4, 8):
-            full_bank(n, 0)
+            full_bank(n, 0, on_scalar)
             store(n, 0, 512)
         for u in range(2):
-            pair_bank(u, 256, 512)
+            pair_bank(u, 256, on_vector)
             for n in (2 * u, 2 * u + 1):
-                full_bank(n, 512)
+                full_bank(n, 512, on_scalar)
                 store(n, 256, 1024)
+        quantize_page(3)
         for n in range(4, 8):
-            full_bank(n, 512)
-            full_bank(n, 1024)
+            full_bank(n, 512, on_scalar)
+            full_bank(n, 1024, on_scalar if n < 6 else on_vector)
             store(n, 512, 1536)
+            if n == 4:
+                quantize_page(4)
         for n in range(4):
-            full_bank(n, 1024)
-            full_bank(n, 1536)
+            full_bank(n, 1024, on_scalar)
+            full_bank(n, 1536, on_vector)
             store(n, 1024, 2048)
         for n in range(4, 8):
-            full_bank(n, 1536)
+            full_bank(n, 1536, on_vector if n % 2 else on_scalar)
             store(n, 1536, 2048)

@@ -37,7 +37,7 @@ def tile_list_lattice_boltzmann_step_kernel(
         lists = ctx.enter_context(tc.tile_pool(name="lists", bufs=1))
         keep = ctx.enter_context(tc.tile_pool(name="keep", bufs=1))
         arena = ctx.enter_context(tc.tile_pool(name="arena", bufs=1))
-        psum = ctx.enter_context(tc.psum_pool(name="psum", bufs=8))
+        psum = ctx.enter_context(tc.psum_pool(name="psum", bufs=1))
 
         def held(name, shape, dtype):
             return keep.tile(shape, dtype, name=name, align_bytes=64)
@@ -45,8 +45,8 @@ def tile_list_lattice_boltzmann_step_kernel(
         def placed(name, shape, dtype, kib):
             return arena.tile(shape, dtype, name=name, offset=kib * KIB, align_bytes=64)
 
-        def bank():
-            return psum.tile([P, BANK], F32, name="bank")
+        def bank(i):
+            return psum.tile([P, BANK], F32, name="bank%d" % (i % 8))
 
         def load_list(name, src):
             dst = lists.tile([P, S // 16], U16, name=name)
@@ -58,16 +58,16 @@ def tile_list_lattice_boltzmann_step_kernel(
             nc.sync.dma_start(out=dst[:], in_=words[a].rearrange("p t i -> p (t i)").bitcast(I32))
             return dst
 
-        def load_packed_scales(queue, dst, scales):
+        def load_packed_scales(dst, scales):
             for q in QUADRANTS:
-                queue.dma_start(
+                nc.sync.dma_start(
                     out=dst[32 * q : 32 * q + 8, :], in_=scales.bitcast(I32)[:, 4 * q : 4 * q + 4, :]
                 )
 
-        def load_weights(dst, wg, t0, t1):
+        def load_weights(dst, wg, t0, t1, j0, j1):
             rows = wg.rearrange("(p t) j -> p t j", t=PACK)
             for q in QUADRANTS:
-                nc.sync.dma_start(out=dst[32 * q : 32 * q + 32], in_=rows[:, t0:t1, :])
+                nc.sync.dma_start(out=dst[32 * q : 32 * q + 32], in_=rows[:, t0:t1, j0:j1])
             return dst
 
         def gather_scales(name, window, offsets):
@@ -91,58 +91,75 @@ def tile_list_lattice_boltzmann_step_kernel(
                 out=codes.bitcast(FP8X4), scales=scales, in_=grouped.rearrange("p c t -> p (c t)")
             )
 
-        window2 = placed("window2", [P, T // 4], I32, 96)
-        window1 = placed("window1", [P, T // 4], I32, 100)
+        window2 = placed("window2", [P, T // 4], I32, 64)
+        window1 = placed("window1", [P, T // 4], I32, 68)
         w3s_raw = held("w3s_raw", [P, H // 4], I32)
         w2s = held("w2s", [P, PASSES, H // 4], I32)
         v1s_planes = held("v1s_planes", [P, PASSES, S // 4], I32)
-        nc.gpsimd.memset(window1[:], 0)
-        for filled in (window2, w3s_raw, w2s, v1s_planes):
+        for filled in (window2, window1, w3s_raw, w2s, v1s_planes):
             nc.vector.memset(filled[:], 0)
-        warm = held("warm", [P, 2], F32)
-        nc.gpsimd.memset(warm[:], 0.0)
-        nc.scalar.activation(warm[:, 1:2], warm[:, 0:1], IDENTITY, bias=warm[:, 0:1], scale=-1.0)
         ident = held("ident", [P, P], F32)
         make_identity(nc, ident[:])
 
         list2 = load_list("list2", offs2)
-        tab2_sb = [load_words("tab2_0", tab2_words, 0, 0)]
-        tab2_rows = tab2_scales.bitcast(I32).rearrange("a (q r) t -> a r q t", r=4)
-        for a in range(PASSES):
-            for r in range(4):
-                nc.sync.dma_start(out=window2[4 * a + r : P : 32, :], in_=tab2_rows[a, r])
-        w3_raw = held("w3_raw", [P, PASSES, H], I32)
-        nc.sync.dma_start(out=w3_raw[:], in_=w3_words.rearrange("a p c i -> p a (c i)").bitcast(I32))
-        load_packed_scales(nc.sync, w3s_raw, w3_scales)
+        load_packed_scales(window2, tab2_scales)
         list1 = load_list("list1", offs)
         nc.sync.dma_start(out=window1[0:P:4, :], in_=tab_scales.bitcast(I32).rearrange("a q t -> (a q) t"))
+        tab2_sb = [load_words("tab2_0", tab2_words, 0, 0)]
+        w3_raw = held("w3_raw", [P, PASSES, H], I32)
+        nc.sync.dma_start(out=w3_raw[:], in_=w3_words.rearrange("a p c i -> p a (c i)").bitcast(I32))
+        load_packed_scales(w3s_raw, w3_scales)
+        rate_cols = held("rate_cols", [P, PACK], F32)
+        with nc.allow_non_contiguous_dma(reason="one rate a partition"):
+            nc.sync.dma_start(out=rate_cols[:], in_=rate.rearrange("(c p) -> p c", p=P))
         tab2_sb.append(load_words("tab2_1", tab2_words, 1, 16))
         list4 = load_list("list4", offs4)
         wall_cols = held("wall_cols", [P, PACK], F32)
         nc.sync.dma_start(out=wall_cols[:], in_=wall.rearrange("(p t) -> p t", t=PACK))
-        wg2_first = load_weights(held("wg2_0", [P, 1, S], F32), wg2, 0, 1)
-        tab_sb = [load_words("tab_%d" % a, tab_words, a, 32 + 16 * a) for a in range(PASSES)]
-        wg2_second = load_weights(held("wg2_1", [P, 1, S], F32), wg2, 1, 2)
+
+        def load_wg2(t):
+            return load_weights(placed("wg2_%d" % t, [P, 1, S], F32, 104 + 4 * t), wg2, t, t + 1, 0, S)
+
+        wg2_sb = [load_wg2(t) for t in range(2)]
         w2_sb = held("w2_sb", [P, PASSES, H // 2], I32)
         nc.sync.dma_start(out=w2_sb[:], in_=w2_words.bitcast(I32).rearrange("a p c -> p a c"))
         w2s_rows = w2_scales.bitcast(I32).rearrange("a (q r) c -> r q a c", r=4)
         for r in range(4):
             nc.sync.dma_start(out=w2s[r:P:32], in_=w2s_rows[r])
-        rate_cols = held("rate_cols", [P, PACK], F32)
-        with nc.allow_non_contiguous_dma(reason="one rate a partition"):
-            nc.sync.dma_start(out=rate_cols[:], in_=rate.rearrange("(c p) -> p c", p=P))
         w1_raw = []
         for a in range(PASSES):
-            raw = placed("w1_raw%d" % a, [P, PACK, H], F32, 64 + 8 * a)
+            raw = placed("w1_raw%d" % a, [P, PACK, H], F32, 72 + 8 * a)
             nc.sync.dma_start(
                 out=raw[:], in_=w1[512 * a : 512 * (a + 1), :].rearrange("(p t) c -> p t c", t=PACK)
             )
             w1_raw.append(raw)
+        tab_sb = [load_words("tab_%d" % a, tab_words, a, 32 + 16 * a) for a in range(PASSES)]
+        wg2_sb.extend(load_wg2(t) for t in range(2, PACK))
         list3 = load_list("list3", offs3)
 
-        v2 = [held("v2_0", [P, S], U32), placed("v2_1", [P, S], U32, 100)]
-        gather_words(v2[0], tab2_sb[0], list2, 0, S)
+        def load_wg1(j0, j1):
+            dst = placed("wg1_%d" % j0, [P, PACK, j1 - j0], F32, 120 + j0 // 64)
+            return load_weights(dst, wg1, 0, PACK, j0, j1)
+
+        wg1_sb = [load_wg1(0, 256)]
+        w4_raw = placed("w4_raw", [P, PACK, N], F32, 88)
+        nc.sync.dma_start(out=w4_raw[:], in_=w4.rearrange("(p t) n -> p t n", t=PACK))
+        wg1_sb.extend([load_wg1(256, 512), load_wg1(512, 1024)])
+
         v2s = gather_scales("v2s", window2, list2)
+        v1s_spread = gather_scales("v1s_spread", window1, list1)
+        for a in range(PASSES):
+            for r in range(4):
+                nc.gpsimd.dma_start(
+                    out=v1s_planes[r:P:32, a, :],
+                    in_=v1s_spread[64 * a + 4 * r : 64 * a + 64 : 16, :].bitcast(I32),
+                )
+        v1s = [v1s_planes[:, a, :].bitcast(U8) for a in range(PASSES)]
+        kept_cols = held("kept_cols", [P, PACK], F32)
+        nc.scalar.activation(kept_cols[:], rate_cols[:], COPY, bias=1.0, scale=-1.0)
+
+        v2 = [placed("v2_%d" % a, [P, S], U32, 152 + 4 * a) for a in range(PASSES)]
+        gather_words(v2[0], tab2_sb[0], list2, 0, S)
         w3_sb = held("w3_sb", [P, PASSES, H], I32)
         nc.vector.tensor_copy(
             out=w3_sb[:].rearrange("p a (t c i) -> p a c t i", t=PACK, i=4),
@@ -153,26 +170,16 @@ def tile_list_lattice_boltzmann_step_kernel(
             out=w3s[:].rearrange("p (t m) -> p t m", t=PACK),
             in_=w3s_raw[:].bitcast(U8).rearrange("p (m t) -> p t m", t=PACK),
         )
-        v1s_spread = gather_scales("v1s_spread", window1, list1)
-        for a in range(PASSES):
-            for r in range(4):
-                nc.sync.dma_start(
-                    out=v1s_planes[r:P:32, a, :],
-                    in_=v1s_spread[64 * a + 4 * r : 64 * a + 64 : 16, :].bitcast(I32),
-                )
-        v1s = [v1s_planes[:, a, :].bitcast(U8) for a in range(PASSES)]
         for h in range(HALVES):
             gather_words(v2[1], tab2_sb[1], list2, h * BANK, (h + 1) * BANK)
 
-        wg2_late = load_weights(placed("wg2_23", [P, 2, S], F32, 16), wg2, 2, 4)
-        wg2_rows = [wg2_first[:, 0, :], wg2_second[:, 0, :], wg2_late[:, 0, :], wg2_late[:, 1, :]]
-        page = {t: placed("page%d" % t, [P, T2], F32, kib) for t, kib in ((0, 128), (1, 48), (3, 56))}
-        h2 = [held("h2_%d" % t, [P, S], F32) for t in range(PACK)]
+        page = [placed("page%d" % t, [P, T2], F32, 8 * t) for t in range(PACK)]
+        h2 = [placed("h2_%d" % t, [P, S], F32, 136 + 4 * t) for t in range(PACK)]
 
         def wall_term(t, h):
             cols = slice(h * BANK, (h + 1) * BANK)
             rows = slice(t * P, (t + 1) * P)
-            acc = bank()
+            acc = bank((HALVES * t + h) % 3)
             for a in range(PASSES):
                 nc.tensor.matmul_mx(
                     out=acc[:],
@@ -195,33 +202,27 @@ def tile_list_lattice_boltzmann_step_kernel(
                 wall_term(t, h)
         for h in range(HALVES):
             cols = slice(h * BANK, (h + 1) * BANK)
-            scatter(0, list4, h * BANK, (h + 1) * BANK, h2[0][:, cols], wg2_rows[0][:, cols])
+            scatter(0, list4, h * BANK, (h + 1) * BANK, h2[0][:, cols], wg2_sb[0][:, 0, cols])
+        scatter(1, list4, 0, S, h2[1][:], wg2_sb[1][:, 0, :])
 
-        v1 = [held("v1_%d" % a, [P, S], U32) for a in range(PASSES)]
-        for a in range(PASSES):
-            gather_words(v1[a], tab_sb[a], list1, 0, S)
-        wg1_sb = load_weights(placed("wg1_sb", [P, PACK, S], F32, 32), wg1, 0, 4)
-        scatter(1, list4, 0, S, h2[1][:], wg2_rows[1])
         w1_codes = held("w1_codes", [P, PASSES, H], U32)
         w1s = held("w1s", [P, PASSES, H], U8)
         for a in range(PASSES):
-            grouped = placed("w1_grouped%d" % a, [P, BANK, PACK], BF16, 120 + 4 * a)
+            grouped = placed("w1_grouped%d" % a, [P, BANK, PACK], BF16, 64 + 4 * a)
             interleave(nc.scalar.copy, grouped[:], w1_raw[a][:])
             quantize(w1_codes[:, a, :], w1s[:, a, :], grouped[:])
-        page[2] = placed("page2", [P, T2], F32, 120)
-        w4_raw = placed("w4_raw", [P, PACK, N], F32, 64)
-        nc.sync.dma_start(out=w4_raw[:], in_=w4.rearrange("(p t) n -> p t n", t=PACK))
+        v1 = [held("v1_%d" % a, [P, S], U32) for a in range(PASSES)]
+        gather_words(v1[0], tab_sb[0], list1, 0, S)
+        for h in range(HALVES):
+            gather_words(v1[1], tab_sb[1], list1, h * BANK, (h + 1) * BANK)
         for t in range(2, PACK):
-            scatter(t, list4, 0, S, h2[t][:], wg2_rows[t])
+            scatter(t, list4, 0, S, h2[t][:], wg2_sb[t][:, 0, :])
 
-        kept_cols = held("kept_cols", [P, PACK], F32)
-        nc.scalar.activation(kept_cols[:], rate_cols[:], COPY, bias=1.0, scale=-1.0)
         w2_bytes = w2_sb[:].bitcast(U8)
         w2s_bytes = w2s[:].bitcast(U8)
 
-        def scaled_product(name, kib, weights, weight_scales, h, factor):
+        def scaled_product(name, kib, acc, weights, weight_scales, h, factor):
             cols = slice(h * BANK, (h + 1) * BANK)
-            acc = bank()
             for a in range(PASSES):
                 nc.tensor.matmul_mx(
                     out=acc[:],
@@ -236,83 +237,94 @@ def tile_list_lattice_boltzmann_step_kernel(
             nc.scalar.activation(term[:], acc[:], COPY, scale=factor)
             return term
 
-        relaxed = {}
-        for h in range(HALVES):
-            for c in range(PACK):
-                relaxed[h, c] = scaled_product(
-                    "relaxed%d%d" % (h, c), 136 * h + 4 * c + 2,
-                    [w2_bytes[:, a, 2 * c * P : 2 * (c + 1) * P].bitcast(FP4X4) for a in range(PASSES)],
-                    [w2s_bytes[:, a, c * P : (c + 1) * P] for a in range(PASSES)],
-                    h, rate_cols[:, c : c + 1],
-                )
-        h1 = []
-        for h in range(HALVES):
+        def relax_terms(h, kib):
             terms = []
             for c in range(PACK):
                 kept = scaled_product(
-                    "kept%d%d" % (h, c), 136 * h + 4 * c,
+                    "kept%d%d" % (h, c), kib + 4 * c, bank(2 * c % 4),
                     [w1_codes[:, a, c * P : (c + 1) * P].bitcast(FP8X4) for a in range(PASSES)],
                     [w1s[:, a, c * P : (c + 1) * P] for a in range(PASSES)],
                     h, kept_cols[:, c : c + 1],
                 )
-                terms.append((kept, relaxed[h, c]))
-            h1_half = placed("h1_%d" % h, [P, PACK, BANK], F32, 80 + 8 * h)
-            for b in range(BANK // P):
-                block = slice(b * P, (b + 1) * P)
-                summed = bank()
-                for c in range(PACK):
-                    for n_term, term in enumerate(terms[c]):
-                        nc.tensor.matmul(
-                            summed[:, c * P : (c + 1) * P], lhsT=term[:, block], rhs=ident[:],
-                            is_transpose=True, start=(n_term == 0), stop=(n_term == 1),
-                        )
-                turned = placed("turned%d%d" % (h, b), [P, PACK, P], F32, 96 + 2 * b)
-                nc.scalar.copy(out=turned[:], in_=summed[:].rearrange("p (m t) -> p t m", t=PACK))
-                back = bank()
-                for t in range(PACK):
-                    nc.tensor.transpose(back[:, t * P : (t + 1) * P], turned[:, t, :], ident[:])
-                nc.scalar.copy(out=h1_half[:, :, block], in_=back[:].rearrange("p (t j) -> p t j", t=PACK))
-            h1.append(h1_half)
-        for h in range(HALVES):
-            cols = slice(h * BANK, (h + 1) * BANK)
-            for t in range(PACK):
-                scatter(t, list3, h * BANK, (h + 1) * BANK, h1[h][:, t, :], wg1_sb[:, t, cols])
+                relaxed = scaled_product(
+                    "relaxed%d%d" % (h, c), kib + 4 * c + 2, bank((2 * c + 1) % 4),
+                    [w2_bytes[:, a, 2 * c * P : 2 * (c + 1) * P].bitcast(FP4X4) for a in range(PASSES)],
+                    [w2s_bytes[:, a, c * P : (c + 1) * P] for a in range(PASSES)],
+                    h, rate_cols[:, c : c + 1],
+                )
+                terms.append((kept, relaxed))
+            return terms
 
-        w4_grouped = []
-        for u in range(N // BANK):
-            grouped = placed("w4_grouped%d" % u, [P, BANK, PACK], BF16, 8 + 4 * u)
-            interleave(nc.scalar.copy, grouped[:], w4_raw[:, :, u * BANK : (u + 1) * BANK])
-            w4_grouped.append(grouped)
-        w4_codes = [held("w4_codes0", [P, BANK], U32)]
+        def relax_block(h, terms, b, dst):
+            block = slice(b * P, (b + 1) * P)
+            summed = bank(4 + b % 2)
+            for c in range(PACK):
+                for n_term, term in enumerate(terms[c]):
+                    nc.tensor.matmul(
+                        summed[:, c * P : (c + 1) * P], lhsT=term[:, block], rhs=ident[:],
+                        is_transpose=True, start=(n_term == 0), stop=(n_term == 1),
+                    )
+            turned = placed("turned%d%d" % (h, b), [P, PACK, P], F32, 64 + 2 * b)
+            nc.scalar.copy(out=turned[:], in_=summed[:].rearrange("p (m t) -> p t m", t=PACK))
+            back = bank(6 + b % 2)
+            for t in range(PACK):
+                nc.tensor.transpose(back[:, t * P : (t + 1) * P], turned[:, t, :], ident[:])
+            nc.scalar.copy(out=dst, in_=back[:].rearrange("p (t j) -> p t j", t=PACK))
+
+        terms = relax_terms(0, 72)
+        h1_quarters = [placed("h1_q%d" % u, [P, PACK, 2 * P], F32, 48 + 4 * u) for u in range(2)]
+        for b in range(BANK // P):
+            relax_block(0, terms, b, h1_quarters[b // 2][:, :, b % 2 * P : (b % 2 + 1) * P])
+        for u in range(2):
+            cols = slice(u * 2 * P, (u + 1) * 2 * P)
+            for t in range(PACK):
+                scatter(t, list3, cols.start, cols.stop, h1_quarters[u][:, t, :], wg1_sb[u][:, t, :])
+
+        w4_codes = placed("w4_codes", [P, N], U32, 52)
         w4s = held("w4s", [P, N], U8)
-        quantize(w4_codes[0][:], w4s[:, 0:BANK], w4_grouped[0][:])
+        terms = relax_terms(1, 32)
+        h1_half = placed("h1_half", [P, PACK, BANK], F32, 56)
+        for b in range(BANK // P):
+            relax_block(1, terms, b, h1_half[:, :, b * P : (b + 1) * P])
+        for u in range(N // BANK):
+            cols = slice(u * BANK, (u + 1) * BANK)
+            grouped = placed("w4_grouped%d" % u, [P, BANK, PACK], BF16, 160 + 4 * u)
+            for c0 in range(0, BANK, 256):
+                interleave(
+                    nc.scalar.copy, grouped[:, c0 : c0 + 256, :], w4_raw[:, :, u * BANK + c0 : u * BANK + c0 + 256]
+                )
+            quantize(w4_codes[:, cols], w4s[:, cols], grouped[:])
+        for t in range(PACK):
+            scatter(t, list3, BANK, S, h1_half[:, t, :], wg1_sb[2][:, t, :])
 
         rounded = [
-            placed("rounded%d" % m0, [P, PACK, m1 - m0], BF16, 136 + m0 // 128) for m0, m1 in PAGE_CHUNKS
+            placed("rounded%d" % m0, [P, PACK, m1 - m0], BF16, 104 + m0 // 128) for m0, m1 in PAGE_CHUNKS
         ]
         for t in range(PACK - 1):
             for g, (m0, m1) in enumerate(PAGE_CHUNKS):
                 nc.scalar.copy(out=rounded[g][:, t, :], in_=page[t][:, m0:m1])
-        page_codes = placed("page_codes", [P, T2], U32, 96)
+        page_codes = placed("page_codes", [P, T2], U32, 152)
         page_s = held("page_s", [P, T2], U8)
-
-        def round_last_slice(g, engine_copy):
-            m0, m1 = PAGE_CHUNKS[g]
-            engine_copy(out=rounded[g][:, PACK - 1, :], in_=page[PACK - 1][:, m0:m1])
 
         def quantize_page(g):
             m0, m1 = PAGE_CHUNKS[g]
-            grouped = placed("page_grouped%d" % m0, [P, m1 - m0, PACK], BF16, 16 + m0 // 128)
+            nc.vector.tensor_copy(out=rounded[g][:, PACK - 1, :], in_=page[PACK - 1][:, m0:m1])
+            grouped = placed("page_grouped%d" % m0, [P, m1 - m0, PACK], BF16, 136 + m0 // 128)
             interleave(nc.vector.tensor_copy, grouped[:], rounded[g][:])
             quantize(page_codes[:, m0:m1], page_s[:, m0:m1], grouped[:])
 
-        staged = [placed("staged%d" % u, [P, 2, T2], F32, (32, 104, 64, 80)[u]) for u in range(4)]
+        staged = [placed("staged%d" % u, [P, 2, T2], F32, (32, 72, 88, 120)[u]) for u in range(4)]
         out_rows = out.rearrange("(u e p) m -> u p e m", e=2, p=P)
+        used = []
+
+        def fresh_bank():
+            used.append(len(used))
+            return bank(used[-1])
 
         def product(dst, n, m0, m1):
             nc.tensor.matmul_mx(
                 out=dst,
-                lhsT=w4_codes[n // 4][:, n % 4 * P : (n % 4 + 1) * P].bitcast(FP8X4),
+                lhsT=w4_codes[:, n * P : (n + 1) * P].bitcast(FP8X4),
                 lhsT_scale=w4s[:, n * P : (n + 1) * P],
                 rhs=page_codes[:, m0:m1].bitcast(FP8X4),
                 rhs_scale=page_s[:, m0:m1],
@@ -321,18 +333,18 @@ def tile_list_lattice_boltzmann_step_kernel(
             )
 
         def half_bank(n, m0, engine_copy):
-            acc = bank()
+            acc = fresh_bank()
             product(acc[:, 0:256], n, m0, m0 + 256)
             engine_copy(out=staged[n // 2][:, n % 2, m0 : m0 + 256], in_=acc[:, 0:256])
 
         def pair_bank(u, m0, engine_copy):
-            acc = bank()
+            acc = fresh_bank()
             for e in range(2):
                 product(acc[:, e * 256 : (e + 1) * 256], 2 * u + e, m0, m0 + 256)
             engine_copy(out=staged[u][:, :, m0 : m0 + 256], in_=acc[:].rearrange("p (e m) -> p e m", e=2))
 
         def full_bank(n, m0, engine_copy):
-            acc = bank()
+            acc = fresh_bank()
             product(acc[:], n, m0, m0 + BANK)
             engine_copy(out=staged[n // 2][:, n % 2, m0 : m0 + BANK], in_=acc[:])
 
@@ -340,33 +352,23 @@ def tile_list_lattice_boltzmann_step_kernel(
             nc.sync.dma_start(out=out_rows[n // 2][:, n % 2, m0:m1], in_=staged[n // 2][:, n % 2, m0:m1])
 
         on_scalar, on_vector = nc.scalar.copy, nc.vector.tensor_copy
-        round_last_slice(0, on_vector)
-        quantize_page(0)
-        w4_codes.append(placed("w4_codes1", [P, BANK], U32, 136))
-        quantize(w4_codes[1][:], w4s[:, BANK:N], w4_grouped[1][:])
-        for g in range(1, 4):
-            round_last_slice(g, on_scalar)
-        for g in range(1, 3):
+        for g in range(len(PAGE_CHUNKS)):
             quantize_page(g)
         for n in range(4):
             half_bank(n, 0, on_scalar)
             store(n, 0, 256)
-        round_last_slice(4, on_scalar)
         for n in range(4, 8):
             full_bank(n, 0, on_scalar)
             store(n, 0, 512)
         for u in range(2):
-            pair_bank(u, 256, on_vector)
+            pair_bank(u, 256, on_scalar)
             for n in (2 * u, 2 * u + 1):
                 full_bank(n, 512, on_scalar)
                 store(n, 256, 1024)
-        quantize_page(3)
         for n in range(4, 8):
             full_bank(n, 512, on_scalar)
             full_bank(n, 1024, on_scalar if n < 6 else on_vector)
             store(n, 512, 1536)
-            if n == 4:
-                quantize_page(4)
         for n in range(4):
             full_bank(n, 1024, on_scalar)
             full_bank(n, 1536, on_vector)

@@ -26,6 +26,9 @@ HALVES = S // BANK
 KIB = 1024
 QUADRANTS = (0, 2, 1, 3)
 PAGE_CHUNKS = ((0, 256), (256, 512), (512, 1024), (1024, 1536), (1536, 2048))
+WOVEN = 2
+EARLY = 768
+LEAD = 256
 
 
 def tile_list_lattice_boltzmann_step_kernel(
@@ -58,9 +61,9 @@ def tile_list_lattice_boltzmann_step_kernel(
             nc.sync.dma_start(out=dst[:], in_=words[a].rearrange("p t i -> p (t i)").bitcast(I32))
             return dst
 
-        def load_packed_scales(dst, scales):
+        def load_packed_scales(queue, dst, scales):
             for q in QUADRANTS:
-                nc.sync.dma_start(
+                queue.dma_start(
                     out=dst[32 * q : 32 * q + 8, :], in_=scales.bitcast(I32)[:, 4 * q : 4 * q + 4, :]
                 )
 
@@ -96,36 +99,32 @@ def tile_list_lattice_boltzmann_step_kernel(
         w3s_raw = held("w3s_raw", [P, H // 4], I32)
         w2s = held("w2s", [P, PASSES, H // 4], I32)
         v1s_planes = held("v1s_planes", [P, PASSES, S // 4], I32)
-        for filled in (window2, window1, w3s_raw, w2s, v1s_planes):
+        nc.gpsimd.memset(window1[:], 0)
+        for filled in (window2, w3s_raw, w2s, v1s_planes):
             nc.vector.memset(filled[:], 0)
-        ident = held("ident", [P, P], F32)
-        make_identity(nc, ident[:])
 
-        list2 = load_list("list2", offs2)
-        load_packed_scales(window2, tab2_scales)
         list1 = load_list("list1", offs)
-        nc.sync.dma_start(out=window1[0:P:4, :], in_=tab_scales.bitcast(I32).rearrange("a q t -> (a q) t"))
-        tab2_sb = [load_words("tab2_0", tab2_words, 0, 0)]
-        w3_raw = held("w3_raw", [P, PASSES, H], I32)
-        nc.sync.dma_start(out=w3_raw[:], in_=w3_words.rearrange("a p c i -> p a (c i)").bitcast(I32))
-        load_packed_scales(w3s_raw, w3_scales)
-        rate_cols = held("rate_cols", [P, PACK], F32)
-        with nc.allow_non_contiguous_dma(reason="one rate a partition"):
-            nc.sync.dma_start(out=rate_cols[:], in_=rate.rearrange("(c p) -> p c", p=P))
-        tab2_sb.append(load_words("tab2_1", tab2_words, 1, 16))
+        list2 = load_list("list2", offs2)
         list4 = load_list("list4", offs4)
         wall_cols = held("wall_cols", [P, PACK], F32)
         nc.sync.dma_start(out=wall_cols[:], in_=wall.rearrange("(p t) -> p t", t=PACK))
+        nc.sync.dma_start(out=window1[0:P:4, :], in_=tab_scales.bitcast(I32).rearrange("a q t -> (a q) t"))
+        load_packed_scales(nc.sync, window2, tab2_scales)
+        tab2_sb = [load_words("tab2_0", tab2_words, 0, 0)]
+        w3_raw = held("w3_raw", [P, PASSES, H], I32)
+        nc.sync.dma_start(out=w3_raw[:], in_=w3_words.rearrange("a p c i -> p a (c i)").bitcast(I32))
+        load_packed_scales(nc.sync, w3s_raw, w3_scales)
+        tab2_sb.append(load_words("tab2_1", tab2_words, 1, 16))
 
-        def load_wg2(t):
-            return load_weights(placed("wg2_%d" % t, [P, 1, S], F32, 104 + 4 * t), wg2, t, t + 1, 0, S)
+        def load_wg2(t, j0, j1):
+            dst = placed("wg2_%d_%d" % (t, j0), [P, 1, j1 - j0], F32, 104 + 4 * t + j0 // 256)
+            return load_weights(dst, wg2, t, t + 1, j0, j1)
 
-        wg2_sb = [load_wg2(t) for t in range(2)]
-        w2_sb = held("w2_sb", [P, PASSES, H // 2], I32)
-        nc.sync.dma_start(out=w2_sb[:], in_=w2_words.bitcast(I32).rearrange("a p c -> p a c"))
-        w2s_rows = w2_scales.bitcast(I32).rearrange("a (q r) c -> r q a c", r=4)
-        for r in range(4):
-            nc.sync.dma_start(out=w2s[r:P:32], in_=w2s_rows[r])
+        wg2_first = load_wg2(0, 0, S)
+        rate_cols = held("rate_cols", [P, PACK], F32)
+        with nc.allow_non_contiguous_dma(reason="one rate a partition"):
+            nc.sync.dma_start(out=rate_cols[:], in_=rate.rearrange("(c p) -> p c", p=P))
+        wg2_second = [load_wg2(1, 0, EARLY)]
         w1_raw = []
         for a in range(PASSES):
             raw = placed("w1_raw%d" % a, [P, PACK, H], F32, 72 + 8 * a)
@@ -134,7 +133,13 @@ def tile_list_lattice_boltzmann_step_kernel(
             )
             w1_raw.append(raw)
         tab_sb = [load_words("tab_%d" % a, tab_words, a, 32 + 16 * a) for a in range(PASSES)]
-        wg2_sb.extend(load_wg2(t) for t in range(2, PACK))
+        w2_sb = held("w2_sb", [P, PASSES, H // 2], I32)
+        nc.sync.dma_start(out=w2_sb[:], in_=w2_words.bitcast(I32).rearrange("a p c -> p a c"))
+        w2s_rows = w2_scales.bitcast(I32).rearrange("a (q r) c -> r q a c", r=4)
+        for r in range(4):
+            nc.sync.dma_start(out=w2s[r:P:32], in_=w2s_rows[r])
+        wg2_second.append(load_wg2(1, EARLY, S))
+        wg2_late = [load_wg2(t, 0, S) for t in range(2, PACK)]
         list3 = load_list("list3", offs3)
 
         def load_wg1(j0, j1):
@@ -146,7 +151,9 @@ def tile_list_lattice_boltzmann_step_kernel(
         nc.sync.dma_start(out=w4_raw[:], in_=w4.rearrange("(p t) n -> p t n", t=PACK))
         wg1_sb.extend([load_wg1(256, 512), load_wg1(512, 1024)])
 
-        v2s = gather_scales("v2s", window2, list2)
+        ident = held("ident", [P, P], F32)
+        make_identity(nc, ident[:])
+
         v1s_spread = gather_scales("v1s_spread", window1, list1)
         for a in range(PASSES):
             for r in range(4):
@@ -154,6 +161,7 @@ def tile_list_lattice_boltzmann_step_kernel(
                     out=v1s_planes[r:P:32, a, :],
                     in_=v1s_spread[64 * a + 4 * r : 64 * a + 64 : 16, :].bitcast(I32),
                 )
+        v2s = gather_scales("v2s", window2, list2)
         v1s = [v1s_planes[:, a, :].bitcast(U8) for a in range(PASSES)]
         kept_cols = held("kept_cols", [P, PACK], F32)
         nc.scalar.activation(kept_cols[:], rate_cols[:], COPY, bias=1.0, scale=-1.0)
@@ -176,13 +184,13 @@ def tile_list_lattice_boltzmann_step_kernel(
         page = [placed("page%d" % t, [P, T2], F32, 8 * t) for t in range(PACK)]
         h2 = [placed("h2_%d" % t, [P, S], F32, 136 + 4 * t) for t in range(PACK)]
 
-        def wall_term(t, h):
-            cols = slice(h * BANK, (h + 1) * BANK)
+        def wall_term(t, j0, j1, turn):
+            cols = slice(j0, j1)
             rows = slice(t * P, (t + 1) * P)
-            acc = bank((HALVES * t + h) % 3)
+            acc = bank(turn % 3)[:, 0 : j1 - j0]
             for a in range(PASSES):
                 nc.tensor.matmul_mx(
-                    out=acc[:],
+                    out=acc,
                     lhsT=w3_sb[:, a, rows].bitcast(FP8X4),
                     lhsT_scale=w3s[4 * a : P, rows],
                     rhs=v2[a][:, cols].bitcast(FP8X4),
@@ -190,21 +198,21 @@ def tile_list_lattice_boltzmann_step_kernel(
                     start=(a == 0),
                     stop=(a == PASSES - 1),
                 )
-            nc.scalar.activation(h2[t][:, cols], acc[:], IDENTITY, bias=wall_cols[:, t : t + 1], scale=-1.0)
+            nc.scalar.activation(h2[t][:, cols], acc, IDENTITY, bias=wall_cols[:, t : t + 1], scale=-1.0)
 
         def scatter(t, offsets, j0, j1, values, weights):
             nc.vector.tensor_tensor(
                 page[t][:].indirect(offsets[:, j0 // 16 : j1 // 16]), values, weights, MULT
             )
 
-        for t in range(PACK):
-            for h in range(HALVES):
-                wall_term(t, h)
-        for h in range(HALVES):
-            cols = slice(h * BANK, (h + 1) * BANK)
-            scatter(0, list4, h * BANK, (h + 1) * BANK, h2[0][:, cols], wg2_sb[0][:, 0, cols])
-        scatter(1, list4, 0, S, h2[1][:], wg2_sb[1][:, 0, :])
+        pieces = [(0, 0, LEAD), (0, LEAD, BANK), (0, BANK, S)]
+        pieces.extend((t, h * BANK, (h + 1) * BANK) for t in range(1, PACK) for h in range(HALVES))
+        for turn, (t, j0, j1) in enumerate(pieces):
+            wall_term(t, j0, j1, turn)
+        for j0, j1 in ((0, LEAD), (LEAD, S)):
+            scatter(0, list4, j0, j1, h2[0][:, j0:j1], wg2_first[:, 0, j0:j1])
 
+        scatter(1, list4, 0, EARLY, h2[1][:, 0:EARLY], wg2_second[0][:, 0, :])
         w1_codes = held("w1_codes", [P, PASSES, H], U32)
         w1s = held("w1s", [P, PASSES, H], U8)
         for a in range(PASSES):
@@ -215,8 +223,9 @@ def tile_list_lattice_boltzmann_step_kernel(
         gather_words(v1[0], tab_sb[0], list1, 0, S)
         for h in range(HALVES):
             gather_words(v1[1], tab_sb[1], list1, h * BANK, (h + 1) * BANK)
+        scatter(1, list4, EARLY, S, h2[1][:, EARLY:S], wg2_second[1][:, 0, :])
         for t in range(2, PACK):
-            scatter(t, list4, 0, S, h2[t][:], wg2_sb[t][:, 0, :])
+            scatter(t, list4, 0, S, h2[t][:], wg2_late[t - 2][:, 0, :])
 
         w2_bytes = w2_sb[:].bitcast(U8)
         w2s_bytes = w2s[:].bitcast(U8)
@@ -280,37 +289,46 @@ def tile_list_lattice_boltzmann_step_kernel(
             for t in range(PACK):
                 scatter(t, list3, cols.start, cols.stop, h1_quarters[u][:, t, :], wg1_sb[u][:, t, :])
 
-        w4_codes = placed("w4_codes", [P, N], U32, 52)
-        w4s = held("w4s", [P, N], U8)
         terms = relax_terms(1, 32)
         h1_half = placed("h1_half", [P, PACK, BANK], F32, 56)
         for b in range(BANK // P):
             relax_block(1, terms, b, h1_half[:, :, b * P : (b + 1) * P])
-        for u in range(N // BANK):
-            cols = slice(u * BANK, (u + 1) * BANK)
-            grouped = placed("w4_grouped%d" % u, [P, BANK, PACK], BF16, 160 + 4 * u)
-            for c0 in range(0, BANK, 256):
-                interleave(
-                    nc.scalar.copy, grouped[:, c0 : c0 + 256, :], w4_raw[:, :, u * BANK + c0 : u * BANK + c0 + 256]
-                )
-            quantize(w4_codes[:, cols], w4s[:, cols], grouped[:])
+        w4_grouped = [placed("w4_grouped%d" % u, [P, BANK, PACK], BF16, 160 + 4 * u) for u in range(2)]
+        for c0 in range(0, N, 256):
+            interleave(
+                nc.scalar.copy, w4_grouped[c0 // BANK][:, c0 % BANK : c0 % BANK + 256, :], w4_raw[:, :, c0 : c0 + 256]
+            )
+        w4s = held("w4s", [P, N], U8)
+        w4_codes = [placed("w4_codes0", [P, BANK], U32, 52)]
+        quantize(w4_codes[0][:], w4s[:, 0:BANK], w4_grouped[0][:])
         for t in range(PACK):
             scatter(t, list3, BANK, S, h1_half[:, t, :], wg1_sb[2][:, t, :])
 
-        rounded = [
-            placed("rounded%d" % m0, [P, PACK, m1 - m0], BF16, 104 + m0 // 128) for m0, m1 in PAGE_CHUNKS
-        ]
+        woven = {
+            m0: placed("page_grouped%d" % m0, [P, m1 - m0, PACK], BF16, 136 + m0 // 128)
+            for m0, m1 in PAGE_CHUNKS[:WOVEN]
+        }
+        rounded = {
+            m0: placed("rounded%d" % m0, [P, PACK, m1 - m0], BF16, 104 + m0 // 128) for m0, m1 in PAGE_CHUNKS[WOVEN:]
+        }
         for t in range(PACK - 1):
-            for g, (m0, m1) in enumerate(PAGE_CHUNKS):
-                nc.scalar.copy(out=rounded[g][:, t, :], in_=page[t][:, m0:m1])
+            for m0, m1 in PAGE_CHUNKS[:WOVEN]:
+                if t < PACK - 2:
+                    nc.scalar.copy(out=woven[m0][:, :, t], in_=page[t][:, m0:m1])
+                else:
+                    nc.scalar.copy(
+                        out=woven[m0][:, :, t:PACK],
+                        in_=page[t][:, m0:m1].unsqueeze(2).to_broadcast([P, m1 - m0, 2]),
+                    )
+            for m0, m1 in PAGE_CHUNKS[WOVEN:]:
+                nc.scalar.copy(out=rounded[m0][:, t, :], in_=page[t][:, m0:m1])
         page_codes = placed("page_codes", [P, T2], U32, 152)
         page_s = held("page_s", [P, T2], U8)
 
-        def quantize_page(g):
-            m0, m1 = PAGE_CHUNKS[g]
-            nc.vector.tensor_copy(out=rounded[g][:, PACK - 1, :], in_=page[PACK - 1][:, m0:m1])
+        def quantize_page(m0, m1):
+            nc.vector.tensor_copy(out=rounded[m0][:, PACK - 1, :], in_=page[PACK - 1][:, m0:m1])
             grouped = placed("page_grouped%d" % m0, [P, m1 - m0, PACK], BF16, 136 + m0 // 128)
-            interleave(nc.vector.tensor_copy, grouped[:], rounded[g][:])
+            interleave(nc.vector.tensor_copy, grouped[:], rounded[m0][:])
             quantize(page_codes[:, m0:m1], page_s[:, m0:m1], grouped[:])
 
         staged = [placed("staged%d" % u, [P, 2, T2], F32, (32, 72, 88, 120)[u]) for u in range(4)]
@@ -324,7 +342,7 @@ def tile_list_lattice_boltzmann_step_kernel(
         def product(dst, n, m0, m1):
             nc.tensor.matmul_mx(
                 out=dst,
-                lhsT=w4_codes[:, n * P : (n + 1) * P].bitcast(FP8X4),
+                lhsT=w4_codes[n // 4][:, n % 4 * P : (n % 4 + 1) * P].bitcast(FP8X4),
                 lhsT_scale=w4s[:, n * P : (n + 1) * P],
                 rhs=page_codes[:, m0:m1].bitcast(FP8X4),
                 rhs_scale=page_s[:, m0:m1],
@@ -352,8 +370,14 @@ def tile_list_lattice_boltzmann_step_kernel(
             nc.sync.dma_start(out=out_rows[n // 2][:, n % 2, m0:m1], in_=staged[n // 2][:, n % 2, m0:m1])
 
         on_scalar, on_vector = nc.scalar.copy, nc.vector.tensor_copy
-        for g in range(len(PAGE_CHUNKS)):
-            quantize_page(g)
+        for m0, m1 in PAGE_CHUNKS[:WOVEN]:
+            nc.vector.tensor_copy(out=woven[m0][:, :, PACK - 1], in_=page[PACK - 1][:, m0:m1])
+        for m0, m1 in PAGE_CHUNKS[:WOVEN]:
+            quantize(page_codes[:, m0:m1], page_s[:, m0:m1], woven[m0][:])
+        w4_codes.append(placed("w4_codes1", [P, BANK], U32, 136))
+        quantize(w4_codes[1][:], w4s[:, BANK:N], w4_grouped[1][:])
+        for m0, m1 in PAGE_CHUNKS[WOVEN:]:
+            quantize_page(m0, m1)
         for n in range(4):
             half_bank(n, 0, on_scalar)
             store(n, 0, 256)

@@ -27,7 +27,6 @@ KIB = 1024
 QUADRANTS = (0, 2, 1, 3)
 PAGE_CHUNKS = ((0, 256), (256, 512), (512, 1024), (1024, 1536), (1536, 2048))
 WOVEN = 2
-EARLY = 768
 LEAD = 256
 
 
@@ -111,20 +110,24 @@ def tile_list_lattice_boltzmann_step_kernel(
         nc.sync.dma_start(out=window1[0:P:4, :], in_=tab_scales.bitcast(I32).rearrange("a q t -> (a q) t"))
         load_packed_scales(nc.sync, window2, tab2_scales)
         tab2_sb = [load_words("tab2_0", tab2_words, 0, 0)]
+        wg2_rows = placed("wg2_rows", [P, S], F32, 160)
+        nc.sync.dma_start(out=wg2_rows[:], in_=wg2)
         w3_raw = held("w3_raw", [P, PASSES, H], I32)
         nc.sync.dma_start(out=w3_raw[:], in_=w3_words.rearrange("a p c i -> p a (c i)").bitcast(I32))
         load_packed_scales(nc.sync, w3s_raw, w3_scales)
         tab2_sb.append(load_words("tab2_1", tab2_words, 1, 16))
 
-        def load_wg2(t, j0, j1):
-            dst = placed("wg2_%d_%d" % (t, j0), [P, 1, j1 - j0], F32, 104 + 4 * t + j0 // 256)
-            return load_weights(dst, wg2, t, t + 1, j0, j1)
+        v1s_spread = gather_scales("v1s_spread", window1, list1)
+        v2s = gather_scales("v2s", window2, list2)
+        v1s = [v1s_planes[:, a, :].bitcast(U8) for a in range(PASSES)]
 
-        wg2_first = load_wg2(0, 0, S)
-        rate_cols = held("rate_cols", [P, PACK], F32)
-        with nc.allow_non_contiguous_dma(reason="one rate a partition"):
-            nc.sync.dma_start(out=rate_cols[:], in_=rate.rearrange("(c p) -> p c", p=P))
-        wg2_second = [load_wg2(1, 0, EARLY)]
+        def move_scale_rows(n0, n1):
+            for a, r in [divmod(n, 4) for n in range(n0, n1)]:
+                nc.sync.dma_start(
+                    out=v1s_planes[r:P:32, a, :],
+                    in_=v1s_spread[64 * a + 4 * r : 64 * a + 64 : 16, :].bitcast(I32),
+                )
+
         w1_raw = []
         for a in range(PASSES):
             raw = placed("w1_raw%d" % a, [P, PACK, H], F32, 72 + 8 * a)
@@ -132,14 +135,18 @@ def tile_list_lattice_boltzmann_step_kernel(
                 out=raw[:], in_=w1[512 * a : 512 * (a + 1), :].rearrange("(p t) c -> p t c", t=PACK)
             )
             w1_raw.append(raw)
-        tab_sb = [load_words("tab_%d" % a, tab_words, a, 32 + 16 * a) for a in range(PASSES)]
+            move_scale_rows(3 * a, 3 * a + 3)
+        tab_sb = [load_words("tab_0", tab_words, 0, 32)]
+        move_scale_rows(6, 8)
+        rate_cols = held("rate_cols", [P, PACK], F32)
+        with nc.allow_non_contiguous_dma(reason="one rate a partition"):
+            nc.sync.dma_start(out=rate_cols[:], in_=rate.rearrange("(c p) -> p c", p=P))
+        tab_sb.append(load_words("tab_1", tab_words, 1, 48))
         w2_sb = held("w2_sb", [P, PASSES, H // 2], I32)
         nc.sync.dma_start(out=w2_sb[:], in_=w2_words.bitcast(I32).rearrange("a p c -> p a c"))
         w2s_rows = w2_scales.bitcast(I32).rearrange("a (q r) c -> r q a c", r=4)
         for r in range(4):
             nc.sync.dma_start(out=w2s[r:P:32], in_=w2s_rows[r])
-        wg2_second.append(load_wg2(1, EARLY, S))
-        wg2_late = [load_wg2(t, 0, S) for t in range(2, PACK)]
         list3 = load_list("list3", offs3)
 
         def load_wg1(j0, j1):
@@ -147,22 +154,31 @@ def tile_list_lattice_boltzmann_step_kernel(
             return load_weights(dst, wg1, 0, PACK, j0, j1)
 
         wg1_sb = [load_wg1(0, 256)]
-        w4_raw = placed("w4_raw", [P, PACK, N], F32, 88)
-        nc.sync.dma_start(out=w4_raw[:], in_=w4.rearrange("(p t) n -> p t n", t=PACK))
-        wg1_sb.extend([load_wg1(256, 512), load_wg1(512, 1024)])
 
         ident = held("ident", [P, P], F32)
         make_identity(nc, ident[:])
+        wg2_turned = []
+        for h in range(HALVES):
+            acc = bank(4 + h)
+            for b in range(BANK // P):
+                j0 = h * BANK + b * P
+                nc.tensor.transpose(acc[:, b * P : (b + 1) * P], wg2_rows[:, j0 : j0 + P], ident[:])
+            for b in range(BANK // P):
+                turned = placed("wg2_turned%d%d" % (h, b), [P, PACK, 4, 32], F32, 88 + 8 * h + 2 * b)
+                rows = acc[:, b * P : (b + 1) * P].rearrange("p (m t) -> p t m", t=PACK)
+                nc.scalar.copy(out=turned[:], in_=rows.unsqueeze(2).to_broadcast([P, PACK, 4, 32]))
+                wg2_turned.append(turned)
 
-        v1s_spread = gather_scales("v1s_spread", window1, list1)
-        for a in range(PASSES):
-            for r in range(4):
-                nc.gpsimd.dma_start(
-                    out=v1s_planes[r:P:32, a, :],
-                    in_=v1s_spread[64 * a + 4 * r : 64 * a + 64 : 16, :].bitcast(I32),
-                )
-        v2s = gather_scales("v2s", window2, list2)
-        v1s = [v1s_planes[:, a, :].bitcast(U8) for a in range(PASSES)]
+        def deal_wg2(t, banks):
+            dealt = placed("wg2_%d" % t, [P, S], F32, 104 + 4 * t)
+            for h in range(HALVES):
+                acc = bank(banks[h])
+                for b in range(BANK // P):
+                    source = wg2_turned[4 * h + b][:, t].rearrange("p q m -> p (q m)")
+                    nc.tensor.transpose(acc[:, b * P : (b + 1) * P], source, ident[:])
+                nc.scalar.copy(out=dealt[:, h * BANK : (h + 1) * BANK], in_=acc[:])
+            return dealt
+
         kept_cols = held("kept_cols", [P, PACK], F32)
         nc.scalar.activation(kept_cols[:], rate_cols[:], COPY, bias=1.0, scale=-1.0)
 
@@ -181,7 +197,7 @@ def tile_list_lattice_boltzmann_step_kernel(
         for h in range(HALVES):
             gather_words(v2[1], tab2_sb[1], list2, h * BANK, (h + 1) * BANK)
 
-        page = [placed("page%d" % t, [P, T2], F32, 8 * t) for t in range(PACK)]
+        page = [placed("page%d" % t, [P, T2], F32, (0, 8, 48, 56)[t]) for t in range(PACK)]
         h2 = [placed("h2_%d" % t, [P, S], F32, 136 + 4 * t) for t in range(PACK)]
 
         def wall_term(t, j0, j1, turn):
@@ -207,12 +223,21 @@ def tile_list_lattice_boltzmann_step_kernel(
 
         pieces = [(0, 0, LEAD), (0, LEAD, BANK), (0, BANK, S)]
         pieces.extend((t, h * BANK, (h + 1) * BANK) for t in range(1, PACK) for h in range(HALVES))
-        for turn, (t, j0, j1) in enumerate(pieces):
+        wg2_sb = [deal_wg2(0, (6, 7))]
+        turn = 0
+        for t, j0, j1 in pieces:
+            if t > 0 and j0 == 0:
+                wg2_sb.append(deal_wg2(t, (turn % 3, (turn + 1) % 3)))
+                turn = turn + 2
             wall_term(t, j0, j1, turn)
+            turn = turn + 1
+        w4_raw = placed("w4_raw", [P, PACK, N], F32, 88)
+        nc.sync.dma_start(out=w4_raw[:], in_=w4.rearrange("(p t) n -> p t n", t=PACK))
+        wg1_sb.extend([load_wg1(256, 512), load_wg1(512, 1024)])
         for j0, j1 in ((0, LEAD), (LEAD, S)):
-            scatter(0, list4, j0, j1, h2[0][:, j0:j1], wg2_first[:, 0, j0:j1])
+            scatter(0, list4, j0, j1, h2[0][:, j0:j1], wg2_sb[0][:, j0:j1])
+        scatter(1, list4, 0, S, h2[1][:], wg2_sb[1][:])
 
-        scatter(1, list4, 0, EARLY, h2[1][:, 0:EARLY], wg2_second[0][:, 0, :])
         w1_codes = held("w1_codes", [P, PASSES, H], U32)
         w1s = held("w1s", [P, PASSES, H], U8)
         for a in range(PASSES):
@@ -223,9 +248,8 @@ def tile_list_lattice_boltzmann_step_kernel(
         gather_words(v1[0], tab_sb[0], list1, 0, S)
         for h in range(HALVES):
             gather_words(v1[1], tab_sb[1], list1, h * BANK, (h + 1) * BANK)
-        scatter(1, list4, EARLY, S, h2[1][:, EARLY:S], wg2_second[1][:, 0, :])
         for t in range(2, PACK):
-            scatter(t, list4, 0, S, h2[t][:], wg2_late[t - 2][:, 0, :])
+            scatter(t, list4, 0, S, h2[t][:], wg2_sb[t][:])
 
         w2_bytes = w2_sb[:].bitcast(U8)
         w2s_bytes = w2s[:].bitcast(U8)
@@ -281,7 +305,7 @@ def tile_list_lattice_boltzmann_step_kernel(
             nc.scalar.copy(out=dst, in_=back[:].rearrange("p (t j) -> p t j", t=PACK))
 
         terms = relax_terms(0, 72)
-        h1_quarters = [placed("h1_q%d" % u, [P, PACK, 2 * P], F32, 48 + 4 * u) for u in range(2)]
+        h1_quarters = [placed("h1_q%d" % u, [P, PACK, 2 * P], F32, 16 + 4 * u) for u in range(2)]
         for b in range(BANK // P):
             relax_block(0, terms, b, h1_quarters[b // 2][:, :, b % 2 * P : (b % 2 + 1) * P])
         for u in range(2):
@@ -290,7 +314,7 @@ def tile_list_lattice_boltzmann_step_kernel(
                 scatter(t, list3, cols.start, cols.stop, h1_quarters[u][:, t, :], wg1_sb[u][:, t, :])
 
         terms = relax_terms(1, 32)
-        h1_half = placed("h1_half", [P, PACK, BANK], F32, 56)
+        h1_half = placed("h1_half", [P, PACK, BANK], F32, 24)
         for b in range(BANK // P):
             relax_block(1, terms, b, h1_half[:, :, b * P : (b + 1) * P])
         w4_grouped = [placed("w4_grouped%d" % u, [P, BANK, PACK], BF16, 160 + 4 * u) for u in range(2)]
@@ -299,7 +323,7 @@ def tile_list_lattice_boltzmann_step_kernel(
                 nc.scalar.copy, w4_grouped[c0 // BANK][:, c0 % BANK : c0 % BANK + 256, :], w4_raw[:, :, c0 : c0 + 256]
             )
         w4s = held("w4s", [P, N], U8)
-        w4_codes = [placed("w4_codes0", [P, BANK], U32, 52)]
+        w4_codes = [placed("w4_codes0", [P, BANK], U32, 20)]
         quantize(w4_codes[0][:], w4s[:, 0:BANK], w4_grouped[0][:])
         for t in range(PACK):
             scatter(t, list3, BANK, S, h1_half[:, t, :], wg1_sb[2][:, t, :])

@@ -102,20 +102,20 @@ def tile_list_lattice_boltzmann_step_kernel(
         for filled in (window2, w3s_raw, w2s, v1s_planes):
             nc.vector.memset(filled[:], 0)
 
-        list1 = load_list("list1", offs)
         list2 = load_list("list2", offs2)
-        list4 = load_list("list4", offs4)
-        wall_cols = held("wall_cols", [P, PACK], F32)
-        nc.sync.dma_start(out=wall_cols[:], in_=wall.rearrange("(p t) -> p t", t=PACK))
-        nc.sync.dma_start(out=window1[0:P:4, :], in_=tab_scales.bitcast(I32).rearrange("a q t -> (a q) t"))
-        load_packed_scales(nc.sync, window2, tab2_scales)
         tab2_sb = [load_words("tab2_0", tab2_words, 0, 0)]
         wg2_rows = placed("wg2_rows", [P, S], F32, 160)
         nc.sync.dma_start(out=wg2_rows[:], in_=wg2)
+        list1 = load_list("list1", offs)
+        nc.sync.dma_start(out=window1[0:P:4, :], in_=tab_scales.bitcast(I32).rearrange("a q t -> (a q) t"))
+        load_packed_scales(nc.sync, window2, tab2_scales)
         w3_raw = held("w3_raw", [P, PASSES, H], I32)
         nc.sync.dma_start(out=w3_raw[:], in_=w3_words.rearrange("a p c i -> p a (c i)").bitcast(I32))
         load_packed_scales(nc.sync, w3s_raw, w3_scales)
         tab2_sb.append(load_words("tab2_1", tab2_words, 1, 16))
+        list4 = load_list("list4", offs4)
+        wall_cols = held("wall_cols", [P, PACK], F32)
+        nc.sync.dma_start(out=wall_cols[:], in_=wall.rearrange("(p t) -> p t", t=PACK))
 
         v1s_spread = gather_scales("v1s_spread", window1, list1)
         v2s = gather_scales("v2s", window2, list2)
@@ -224,8 +224,12 @@ def tile_list_lattice_boltzmann_step_kernel(
         pieces = [(0, 0, LEAD), (0, LEAD, BANK), (0, BANK, S)]
         pieces.extend((t, h * BANK, (h + 1) * BANK) for t in range(1, PACK) for h in range(HALVES))
         wg2_sb = [deal_wg2(0, (6, 7))]
+        w1_grouped = [placed("w1_grouped%d" % a, [P, BANK, PACK], BF16, 64 + 4 * a) for a in range(PASSES)]
         turn = 0
         for t, j0, j1 in pieces:
+            if t == 2 and j0 == 0:
+                for a in range(PASSES):
+                    interleave(nc.scalar.copy, w1_grouped[a][:], w1_raw[a][:])
             if t > 0 and j0 == 0:
                 wg2_sb.append(deal_wg2(t, (turn % 3, (turn + 1) % 3)))
                 turn = turn + 2
@@ -241,9 +245,7 @@ def tile_list_lattice_boltzmann_step_kernel(
         w1_codes = held("w1_codes", [P, PASSES, H], U32)
         w1s = held("w1s", [P, PASSES, H], U8)
         for a in range(PASSES):
-            grouped = placed("w1_grouped%d" % a, [P, BANK, PACK], BF16, 64 + 4 * a)
-            interleave(nc.scalar.copy, grouped[:], w1_raw[a][:])
-            quantize(w1_codes[:, a, :], w1s[:, a, :], grouped[:])
+            quantize(w1_codes[:, a, :], w1s[:, a, :], w1_grouped[a][:])
         v1 = [held("v1_%d" % a, [P, S], U32) for a in range(PASSES)]
         gather_words(v1[0], tab_sb[0], list1, 0, S)
         for h in range(HALVES):
@@ -323,7 +325,7 @@ def tile_list_lattice_boltzmann_step_kernel(
                 nc.scalar.copy, w4_grouped[c0 // BANK][:, c0 % BANK : c0 % BANK + 256, :], w4_raw[:, :, c0 : c0 + 256]
             )
         w4s = held("w4s", [P, N], U8)
-        w4_codes = [placed("w4_codes0", [P, BANK], U32, 20)]
+        w4_codes = [held("w4_codes0", [P, BANK], U32)]
         quantize(w4_codes[0][:], w4s[:, 0:BANK], w4_grouped[0][:])
         for t in range(PACK):
             scatter(t, list3, BANK, S, h1_half[:, t, :], wg1_sb[2][:, t, :])
@@ -400,8 +402,7 @@ def tile_list_lattice_boltzmann_step_kernel(
             quantize(page_codes[:, m0:m1], page_s[:, m0:m1], woven[m0][:])
         w4_codes.append(placed("w4_codes1", [P, BANK], U32, 136))
         quantize(w4_codes[1][:], w4s[:, BANK:N], w4_grouped[1][:])
-        for m0, m1 in PAGE_CHUNKS[WOVEN:]:
-            quantize_page(m0, m1)
+        quantize_page(*PAGE_CHUNKS[2])
         for n in range(4):
             half_bank(n, 0, on_scalar)
             store(n, 0, 256)
@@ -409,10 +410,12 @@ def tile_list_lattice_boltzmann_step_kernel(
             full_bank(n, 0, on_scalar)
             store(n, 0, 512)
         for u in range(2):
-            pair_bank(u, 256, on_scalar)
+            pair_bank(u, 256, on_vector)
             for n in (2 * u, 2 * u + 1):
                 full_bank(n, 512, on_scalar)
                 store(n, 256, 1024)
+        quantize_page(*PAGE_CHUNKS[3])
+        quantize_page(*PAGE_CHUNKS[4])
         for n in range(4, 8):
             full_bank(n, 512, on_scalar)
             full_bank(n, 1024, on_scalar if n < 6 else on_vector)

@@ -45,7 +45,7 @@ def tile_list_lattice_boltzmann_step_kernel(
             return keep.tile(shape, dtype, name=name, align_bytes=64)
 
         def placed(name, shape, dtype, kib):
-            return arena.tile(shape, dtype, name=name, offset=kib * KIB, align_bytes=64)
+            return arena.tile(shape, dtype, name=name, offset=int(kib * KIB), align_bytes=64)
 
         def bank(i):
             return psum.tile([P, BANK], F32, name="bank%d" % (i % 8))
@@ -72,14 +72,14 @@ def tile_list_lattice_boltzmann_step_kernel(
                 nc.sync.dma_start(out=dst[32 * q : 32 * q + 32], in_=rows[:, t0:t1, j0:j1])
             return dst
 
-        def gather_scales(name, window, offsets):
-            picked = held(name, [P, S], U8)
+        def gather_scales(name, kib, window, offsets):
+            picked = placed(name, [P, S], U8, kib)
             nc.vector.tensor_copy(picked[:], window[:].bitcast(U8).indirect(offsets[:]))
             return picked
 
         def gather_words(dst, window, offsets, j0, j1):
             nc.vector.tensor_copy(
-                dst[:, j0:j1], window[:].bitcast(U32).indirect(offsets[:, j0 // 16 : j1 // 16])
+                dst, window[:].bitcast(U32).indirect(offsets[:, j0 // 16 : j1 // 16])
             )
 
         def interleave(engine_copy, dst, src):
@@ -93,41 +93,60 @@ def tile_list_lattice_boltzmann_step_kernel(
                 out=codes.bitcast(FP8X4), scales=scales, in_=grouped.rearrange("p c t -> p (c t)")
             )
 
-        window2 = placed("window2", [P, T // 4], I32, 64)
-        window1 = placed("window1", [P, T // 4], I32, 68)
-        w3s_raw = held("w3s_raw", [P, H // 4], I32)
-        w2s = held("w2s", [P, PASSES, H // 4], I32)
+        window2 = placed("window2", [P, T // 4], I32, 172)
+        window1 = placed("window1", [P, T // 4], I32, 168)
+        v2s_planes = held("v2s_planes", [P, PASSES, S // 4], I32)
         v1s_planes = held("v1s_planes", [P, PASSES, S // 4], I32)
         nc.gpsimd.memset(window1[:], 0)
-        for filled in (window2, w3s_raw, w2s, v1s_planes):
+        for filled in (window2, v2s_planes, v1s_planes):
             nc.vector.memset(filled[:], 0)
+        ident = held("ident", [P, P], F32)
+        make_identity(nc, ident[:])
+        w3s_raw = held("w3s_raw", [P, H // 4], I32)
+        nc.vector.memset(w3s_raw[:], 0)
 
-        list2 = load_list("list2", offs2)
-        tab2_sb = [load_words("tab2_0", tab2_words, 0, 0)]
+        def load_spread(window, scales):
+            nc.sync.dma_start(out=window[0:P:4, :], in_=scales.bitcast(I32).rearrange("a q t -> q a t"))
+
+        def move_scale_rows(planes, spread):
+            for q in range(4):
+                nc.sync.dma_start(
+                    out=planes[32 * q : 32 * q + 4], in_=spread[32 * q : 32 * q + 32 : 4, :].bitcast(I32)
+                )
+
         wg2_rows = placed("wg2_rows", [P, S], F32, 160)
         nc.sync.dma_start(out=wg2_rows[:], in_=wg2)
+        list2 = load_list("list2", offs2)
         list1 = load_list("list1", offs)
-        nc.sync.dma_start(out=window1[0:P:4, :], in_=tab_scales.bitcast(I32).rearrange("a q t -> (a q) t"))
-        load_packed_scales(nc.sync, window2, tab2_scales)
-        w3_raw = held("w3_raw", [P, PASSES, H], I32)
-        nc.sync.dma_start(out=w3_raw[:], in_=w3_words.rearrange("a p c i -> p a (c i)").bitcast(I32))
+        list3 = load_list("list3", offs3)
+        load_spread(window2, tab2_scales)
+        load_spread(window1, tab_scales)
+        tab2_sb = [load_words("tab2_0", tab2_words, 0, 0)]
         load_packed_scales(nc.sync, w3s_raw, w3_scales)
         tab2_sb.append(load_words("tab2_1", tab2_words, 1, 16))
+        w3_raw = placed("w3_raw", [P, PASSES, H], I32, 164)
+        nc.sync.dma_start(out=w3_raw[:], in_=w3_words.rearrange("a p c i -> p a (c i)").bitcast(I32))
         list4 = load_list("list4", offs4)
         wall_cols = held("wall_cols", [P, PACK], F32)
         nc.sync.dma_start(out=wall_cols[:], in_=wall.rearrange("(p t) -> p t", t=PACK))
 
-        v1s_spread = gather_scales("v1s_spread", window1, list1)
-        v2s = gather_scales("v2s", window2, list2)
+        v2s_spread = gather_scales("v2s_spread", 79.5, window2, list2)
+        v1s_spread = gather_scales("v1s_spread", 48, window1, list1)
+        v2s = [v2s_planes[:, a, :].bitcast(U8) for a in range(PASSES)]
         v1s = [v1s_planes[:, a, :].bitcast(U8) for a in range(PASSES)]
-
-        def move_scale_rows(n0, n1):
-            for a, r in [divmod(n, 4) for n in range(n0, n1)]:
-                nc.sync.dma_start(
-                    out=v1s_planes[r:P:32, a, :],
-                    in_=v1s_spread[64 * a + 4 * r : 64 * a + 64 : 16, :].bitcast(I32),
-                )
-
+        move_scale_rows(v2s_planes, v2s_spread)
+        tab_sb = [load_words("tab_0", tab_words, 0, 175)]
+        w2_sb = placed("w2_sb", [P, PASSES, H // 2], I32, 168)
+        nc.sync.dma_start(out=w2_sb[:], in_=w2_words.bitcast(I32).rearrange("a p c -> p a c"))
+        rate_cols = placed("rate_cols", [P, PACK], F32, 170)
+        with nc.allow_non_contiguous_dma(reason="one rate a partition"):
+            nc.sync.dma_start(out=rate_cols[:], in_=rate.rearrange("(c p) -> p c", p=P))
+        move_scale_rows(v1s_planes, v1s_spread)
+        w2s = placed("w2s", [P, PASSES, H // 4], I32, 171)
+        nc.gpsimd.memset(w2s[:], 0)
+        w2s_rows = w2_scales.bitcast(I32).rearrange("a (q r) c -> r q a c", r=4)
+        for r in range(4):
+            nc.sync.dma_start(out=w2s[r:P:32], in_=w2s_rows[r])
         w1_raw = []
         for a in range(PASSES):
             raw = placed("w1_raw%d" % a, [P, PACK, H], F32, 72 + 8 * a)
@@ -135,67 +154,56 @@ def tile_list_lattice_boltzmann_step_kernel(
                 out=raw[:], in_=w1[512 * a : 512 * (a + 1), :].rearrange("(p t) c -> p t c", t=PACK)
             )
             w1_raw.append(raw)
-            move_scale_rows(3 * a, 3 * a + 3)
-        tab_sb = [load_words("tab_0", tab_words, 0, 32)]
-        move_scale_rows(6, 8)
-        rate_cols = held("rate_cols", [P, PACK], F32)
-        with nc.allow_non_contiguous_dma(reason="one rate a partition"):
-            nc.sync.dma_start(out=rate_cols[:], in_=rate.rearrange("(c p) -> p c", p=P))
         tab_sb.append(load_words("tab_1", tab_words, 1, 48))
-        w2_sb = held("w2_sb", [P, PASSES, H // 2], I32)
-        nc.sync.dma_start(out=w2_sb[:], in_=w2_words.bitcast(I32).rearrange("a p c -> p a c"))
-        w2s_rows = w2_scales.bitcast(I32).rearrange("a (q r) c -> r q a c", r=4)
-        for r in range(4):
-            nc.sync.dma_start(out=w2s[r:P:32], in_=w2s_rows[r])
-        list3 = load_list("list3", offs3)
 
         def load_wg1(j0, j1):
-            dst = placed("wg1_%d" % j0, [P, PACK, j1 - j0], F32, 120 + j0 // 64)
+            dst = placed("wg1_%d" % j0, [P, PACK, j1 - j0], F32, 72 + j0 // 64)
             return load_weights(dst, wg1, 0, PACK, j0, j1)
 
-        wg1_sb = [load_wg1(0, 256)]
-
-        ident = held("ident", [P, P], F32)
-        make_identity(nc, ident[:])
         wg2_turned = []
-        for h in range(HALVES):
-            acc = bank(4 + h)
+
+        def turn_wg2(h, turn):
+            acc = bank(turn)
             for b in range(BANK // P):
-                j0 = h * BANK + b * P
-                nc.tensor.transpose(acc[:, b * P : (b + 1) * P], wg2_rows[:, j0 : j0 + P], ident[:])
+                nc.tensor.transpose(acc[:, b * P : (b + 1) * P], wg2_rows[:, h * BANK + b * P : h * BANK + (b + 1) * P], ident[:])
             for b in range(BANK // P):
                 turned = placed("wg2_turned%d%d" % (h, b), [P, PACK, 4, 32], F32, 88 + 8 * h + 2 * b)
                 rows = acc[:, b * P : (b + 1) * P].rearrange("p (m t) -> p t m", t=PACK)
                 nc.scalar.copy(out=turned[:], in_=rows.unsqueeze(2).to_broadcast([P, PACK, 4, 32]))
                 wg2_turned.append(turned)
 
-        def deal_wg2(t, banks):
-            dealt = placed("wg2_%d" % t, [P, S], F32, 104 + 4 * t)
-            for h in range(HALVES):
-                acc = bank(banks[h])
-                for b in range(BANK // P):
-                    source = wg2_turned[4 * h + b][:, t].rearrange("p q m -> p (q m)")
-                    nc.tensor.transpose(acc[:, b * P : (b + 1) * P], source, ident[:])
-                nc.scalar.copy(out=dealt[:, h * BANK : (h + 1) * BANK], in_=acc[:])
-            return dealt
+        wg2_sb = [placed("wg2_%d" % t, [P, S], F32, 104 + 4 * t) for t in range(PACK)]
+
+        def deal_wg2(t, h, turn):
+            acc = bank(turn)
+            for b in range(BANK // P):
+                source = wg2_turned[4 * h + b][:, t].rearrange("p q m -> p (q m)")
+                nc.tensor.transpose(acc[:, b * P : (b + 1) * P], source, ident[:])
+            nc.scalar.copy(out=wg2_sb[t][:, h * BANK : (h + 1) * BANK], in_=acc[:])
 
         kept_cols = held("kept_cols", [P, PACK], F32)
         nc.scalar.activation(kept_cols[:], rate_cols[:], COPY, bias=1.0, scale=-1.0)
 
-        v2 = [placed("v2_%d" % a, [P, S], U32, 152 + 4 * a) for a in range(PASSES)]
-        gather_words(v2[0], tab2_sb[0], list2, 0, S)
-        w3_sb = held("w3_sb", [P, PASSES, H], I32)
-        nc.vector.tensor_copy(
-            out=w3_sb[:].rearrange("p a (t c i) -> p a c t i", t=PACK, i=4),
-            in_=w3_raw[:].rearrange("p a (c i t) -> p a c t i", t=PACK, i=4),
-        )
+        v2_0 = placed("v2_0", [P, S], U32, 152)
+        gather_words(v2_0[:], tab2_sb[0], list2, 0, S)
         w3s = held("w3s", [P, H], U8)
         nc.vector.tensor_copy(
             out=w3s[:].rearrange("p (t m) -> p t m", t=PACK),
             in_=w3s_raw[:].bitcast(U8).rearrange("p (m t) -> p t m", t=PACK),
         )
-        for h in range(HALVES):
-            gather_words(v2[1], tab2_sb[1], list2, h * BANK, (h + 1) * BANK)
+        v2_10 = placed("v2_10", [P, BANK], U32, 156)
+        gather_words(v2_10[:], tab2_sb[1], list2, 0, BANK)
+        w3_columns = w3_raw[:].rearrange("p a (c i t) -> p a c t i", t=PACK, i=4)
+        w3_first = held("w3_first", [P, PASSES, P], I32)
+        nc.vector.tensor_copy(out=w3_first[:].rearrange("p a (c i) -> p a c i", i=4), in_=w3_columns[:, :, :, 0, :])
+        w3_rest = held("w3_rest", [P, PASSES, (PACK - 1) * P], I32)
+        nc.vector.tensor_copy(
+            out=w3_rest[:].rearrange("p a (t c i) -> p a c t i", t=PACK - 1, i=4), in_=w3_columns[:, :, :, 1:PACK, :]
+        )
+        w3_sb = [w3_first[:]] + [w3_rest[:, :, t * P : (t + 1) * P] for t in range(PACK - 1)]
+        v2_11 = placed("v2_11", [P, BANK], U32, 164)
+        gather_words(v2_11[:], tab2_sb[1], list2, BANK, S)
+        v2 = [[v2_0[:, 0:BANK], v2_0[:, BANK:S]], [v2_10[:], v2_11[:]]]
 
         page = [placed("page%d" % t, [P, T2], F32, (0, 8, 48, 56)[t]) for t in range(PACK)]
         h2 = [placed("h2_%d" % t, [P, S], F32, 136 + 4 * t) for t in range(PACK)]
@@ -203,14 +211,14 @@ def tile_list_lattice_boltzmann_step_kernel(
         def wall_term(t, j0, j1, turn):
             cols = slice(j0, j1)
             rows = slice(t * P, (t + 1) * P)
-            acc = bank(turn % 3)[:, 0 : j1 - j0]
+            acc = bank(turn)[:, 0 : j1 - j0]
             for a in range(PASSES):
                 nc.tensor.matmul_mx(
                     out=acc,
-                    lhsT=w3_sb[:, a, rows].bitcast(FP8X4),
+                    lhsT=w3_sb[t][:, a, :].bitcast(FP8X4),
                     lhsT_scale=w3s[4 * a : P, rows],
-                    rhs=v2[a][:, cols].bitcast(FP8X4),
-                    rhs_scale=v2s[4 * a : P, cols],
+                    rhs=v2[a][j0 // BANK][:, j0 % BANK : j0 % BANK + j1 - j0].bitcast(FP8X4),
+                    rhs_scale=v2s[a][:, cols],
                     start=(a == 0),
                     stop=(a == PASSES - 1),
                 )
@@ -221,35 +229,41 @@ def tile_list_lattice_boltzmann_step_kernel(
                 page[t][:].indirect(offsets[:, j0 // 16 : j1 // 16]), values, weights, MULT
             )
 
-        pieces = [(0, 0, LEAD), (0, LEAD, BANK), (0, BANK, S)]
-        pieces.extend((t, h * BANK, (h + 1) * BANK) for t in range(1, PACK) for h in range(HALVES))
-        wg2_sb = [deal_wg2(0, (6, 7))]
-        w1_grouped = [placed("w1_grouped%d" % a, [P, BANK, PACK], BF16, 64 + 4 * a) for a in range(PASSES)]
+        for h in range(HALVES):
+            turn_wg2(h, 4 + h)
+        for t in range(2):
+            for h in range(HALVES):
+                deal_wg2(t, h, 6 + h)
+        wall_term(0, 0, LEAD, 0)
+        wall_term(1, 0, BANK, 1)
+        wall_term(0, LEAD, BANK, 2)
+        for t in range(2):
+            wall_term(t, BANK, S, t)
         turn = 0
-        for t, j0, j1 in pieces:
-            if t == 2 and j0 == 0:
-                for a in range(PASSES):
-                    interleave(nc.scalar.copy, w1_grouped[a][:], w1_raw[a][:])
-            if t > 0 and j0 == 0:
-                wg2_sb.append(deal_wg2(t, (turn % 3, (turn + 1) % 3)))
+        for t in range(2, PACK):
+            for h in range(HALVES):
+                deal_wg2(t, h, (2 + turn) % 3)
+                wall_term(t, h * BANK, (h + 1) * BANK, turn % 3)
                 turn = turn + 2
-            wall_term(t, j0, j1, turn)
-            turn = turn + 1
-        w4_raw = placed("w4_raw", [P, PACK, N], F32, 88)
-        nc.sync.dma_start(out=w4_raw[:], in_=w4.rearrange("(p t) n -> p t n", t=PACK))
-        wg1_sb.extend([load_wg1(256, 512), load_wg1(512, 1024)])
-        for j0, j1 in ((0, LEAD), (LEAD, S)):
-            scatter(0, list4, j0, j1, h2[0][:, j0:j1], wg2_sb[0][:, j0:j1])
-        scatter(1, list4, 0, S, h2[1][:], wg2_sb[1][:])
+        w1_grouped = [placed("w1_grouped%d" % a, [P, BANK, PACK], BF16, 96 + 4 * a) for a in range(PASSES)]
+        for a in range(PASSES):
+            interleave(nc.scalar.copy, w1_grouped[a][:], w1_raw[a][:])
+        for t, j0, j1 in ((0, 0, LEAD), (1, 0, BANK), (0, LEAD, S), (1, BANK, S)):
+            if t < 2:
+                scatter(t, list4, j0, j1, h2[t][:, j0:j1], wg2_sb[t][:, j0:j1])
 
         w1_codes = held("w1_codes", [P, PASSES, H], U32)
         w1s = held("w1s", [P, PASSES, H], U8)
         for a in range(PASSES):
             quantize(w1_codes[:, a, :], w1s[:, a, :], w1_grouped[a][:])
+        wg1_sb = [load_wg1(0, 256)]
+        w4_raw = placed("w4_raw", [P, PACK, N], F32, 88)
+        nc.sync.dma_start(out=w4_raw[:], in_=w4.rearrange("(p t) n -> p t n", t=PACK))
+        wg1_sb.append(load_wg1(LEAD, S))
         v1 = [held("v1_%d" % a, [P, S], U32) for a in range(PASSES)]
-        gather_words(v1[0], tab_sb[0], list1, 0, S)
+        gather_words(v1[0][:], tab_sb[0], list1, 0, S)
         for h in range(HALVES):
-            gather_words(v1[1], tab_sb[1], list1, h * BANK, (h + 1) * BANK)
+            gather_words(v1[1][:, h * BANK : (h + 1) * BANK], tab_sb[1], list1, h * BANK, (h + 1) * BANK)
         for t in range(2, PACK):
             scatter(t, list4, 0, S, h2[t][:], wg2_sb[t][:])
 
@@ -306,19 +320,25 @@ def tile_list_lattice_boltzmann_step_kernel(
                 nc.tensor.transpose(back[:, t * P : (t + 1) * P], turned[:, t, :], ident[:])
             nc.scalar.copy(out=dst, in_=back[:].rearrange("p (t j) -> p t j", t=PACK))
 
-        terms = relax_terms(0, 72)
-        h1_quarters = [placed("h1_q%d" % u, [P, PACK, 2 * P], F32, 16 + 4 * u) for u in range(2)]
+        terms = relax_terms(0, 120)
+        h1_first = placed("h1_first", [P, PACK, LEAD], F32, 16)
+        h1_rest = placed("h1_rest", [P, PACK, S - LEAD], F32, 20)
         for b in range(BANK // P):
-            relax_block(0, terms, b, h1_quarters[b // 2][:, :, b % 2 * P : (b % 2 + 1) * P])
-        for u in range(2):
-            cols = slice(u * 2 * P, (u + 1) * 2 * P)
-            for t in range(PACK):
-                scatter(t, list3, cols.start, cols.stop, h1_quarters[u][:, t, :], wg1_sb[u][:, t, :])
+            dst = h1_first if b * P < LEAD else h1_rest
+            relax_block(0, terms, b, dst[:, :, b * P % LEAD : b * P % LEAD + P])
+        for t in range(PACK):
+            scatter(t, list3, 0, LEAD, h1_first[:, t, :], wg1_sb[0][:, t, :])
 
+        def scatter_rest(t, j0, j1):
+            cols = slice(j0 - LEAD, j1 - LEAD)
+            scatter(t, list3, j0, j1, h1_rest[:, t, cols], wg1_sb[1][:, t, cols])
+
+        for t in range(PACK - 1):
+            scatter_rest(t, LEAD, BANK)
         terms = relax_terms(1, 32)
-        h1_half = placed("h1_half", [P, PACK, BANK], F32, 24)
         for b in range(BANK // P):
-            relax_block(1, terms, b, h1_half[:, :, b * P : (b + 1) * P])
+            j0 = BANK - LEAD + b * P
+            relax_block(1, terms, b, h1_rest[:, :, j0 : j0 + P])
         w4_grouped = [placed("w4_grouped%d" % u, [P, BANK, PACK], BF16, 160 + 4 * u) for u in range(2)]
         for c0 in range(0, N, 256):
             interleave(
@@ -327,35 +347,38 @@ def tile_list_lattice_boltzmann_step_kernel(
         w4s = held("w4s", [P, N], U8)
         w4_codes = [held("w4_codes0", [P, BANK], U32)]
         quantize(w4_codes[0][:], w4s[:, 0:BANK], w4_grouped[0][:])
-        for t in range(PACK):
-            scatter(t, list3, BANK, S, h1_half[:, t, :], wg1_sb[2][:, t, :])
+        for t in range(PACK - 1):
+            scatter_rest(t, BANK, S)
+        scatter_rest(PACK - 1, LEAD, S)
 
         woven = {
             m0: placed("page_grouped%d" % m0, [P, m1 - m0, PACK], BF16, 136 + m0 // 128)
             for m0, m1 in PAGE_CHUNKS[:WOVEN]
         }
-        rounded = {
-            m0: placed("rounded%d" % m0, [P, PACK, m1 - m0], BF16, 104 + m0 // 128) for m0, m1 in PAGE_CHUNKS[WOVEN:]
+        paired = {
+            m0: placed("paired%d" % m0, [P, 2, m1 - m0, 2], BF16, 104 + m0 // 128) for m0, m1 in PAGE_CHUNKS[WOVEN:]
         }
         for t in range(PACK - 1):
-            for m0, m1 in PAGE_CHUNKS[:WOVEN]:
+            for m0, m1 in PAGE_CHUNKS:
+                dst = woven[m0][:, :, t : t + 2] if m0 in woven else paired[m0][:, t // 2, :, :]
                 if t < PACK - 2:
-                    nc.scalar.copy(out=woven[m0][:, :, t], in_=page[t][:, m0:m1])
+                    nc.scalar.copy(out=dst[:, :, 0 if m0 in woven else t], in_=page[t][:, m0:m1])
                 else:
-                    nc.scalar.copy(
-                        out=woven[m0][:, :, t:PACK],
-                        in_=page[t][:, m0:m1].unsqueeze(2).to_broadcast([P, m1 - m0, 2]),
-                    )
-            for m0, m1 in PAGE_CHUNKS[WOVEN:]:
-                nc.scalar.copy(out=rounded[m0][:, t, :], in_=page[t][:, m0:m1])
+                    nc.scalar.copy(out=dst, in_=page[t][:, m0:m1].unsqueeze(2).to_broadcast([P, m1 - m0, 2]))
         page_codes = placed("page_codes", [P, T2], U32, 152)
         page_s = held("page_s", [P, T2], U8)
+        merged = {}
+
+        def pair_last(m0, m1):
+            nc.vector.tensor_copy(out=paired[m0][:, 1, :, 1], in_=page[PACK - 1][:, m0:m1])
+
+        def merge_pairs(m0, m1):
+            merged[m0] = placed("page_grouped%d" % m0, [P, m1 - m0, PACK], BF16, 136 + m0 // 128)
+            words = paired[m0][:].rearrange("p u m e -> p u (m e)").bitcast(I32)
+            interleave(nc.vector.tensor_copy, merged[m0][:].bitcast(I32), words)
 
         def quantize_page(m0, m1):
-            nc.vector.tensor_copy(out=rounded[m0][:, PACK - 1, :], in_=page[PACK - 1][:, m0:m1])
-            grouped = placed("page_grouped%d" % m0, [P, m1 - m0, PACK], BF16, 136 + m0 // 128)
-            interleave(nc.vector.tensor_copy, grouped[:], rounded[m0][:])
-            quantize(page_codes[:, m0:m1], page_s[:, m0:m1], grouped[:])
+            quantize(page_codes[:, m0:m1], page_s[:, m0:m1], merged[m0][:])
 
         staged = [placed("staged%d" % u, [P, 2, T2], F32, (32, 72, 88, 120)[u]) for u in range(4)]
         out_rows = out.rearrange("(u e p) m -> u p e m", e=2, p=P)
@@ -400,9 +423,18 @@ def tile_list_lattice_boltzmann_step_kernel(
             nc.vector.tensor_copy(out=woven[m0][:, :, PACK - 1], in_=page[PACK - 1][:, m0:m1])
         for m0, m1 in PAGE_CHUNKS[:WOVEN]:
             quantize(page_codes[:, m0:m1], page_s[:, m0:m1], woven[m0][:])
+        first, second, third = PAGE_CHUNKS[WOVEN:]
+        pair_last(*first)
         w4_codes.append(placed("w4_codes1", [P, BANK], U32, 136))
         quantize(w4_codes[1][:], w4s[:, BANK:N], w4_grouped[1][:])
-        quantize_page(*PAGE_CHUNKS[2])
+        merge_pairs(*first)
+        pair_last(*second)
+        quantize_page(*first)
+        merge_pairs(*second)
+        pair_last(*third)
+        quantize_page(*second)
+        merge_pairs(*third)
+        quantize_page(*third)
         for n in range(4):
             half_bank(n, 0, on_scalar)
             store(n, 0, 256)
@@ -410,20 +442,15 @@ def tile_list_lattice_boltzmann_step_kernel(
             full_bank(n, 0, on_scalar)
             store(n, 0, 512)
         for u in range(2):
-            pair_bank(u, 256, on_vector)
+            pair_bank(u, 256, on_scalar)
             for n in (2 * u, 2 * u + 1):
                 full_bank(n, 512, on_scalar)
                 store(n, 256, 1024)
-        quantize_page(*PAGE_CHUNKS[3])
-        quantize_page(*PAGE_CHUNKS[4])
         for n in range(4, 8):
-            full_bank(n, 512, on_scalar)
-            full_bank(n, 1024, on_scalar if n < 6 else on_vector)
-            store(n, 512, 1536)
+            for c, m0 in enumerate((512, 1024, 1536)):
+                full_bank(n, m0, on_vector if (n + c) % 2 == 0 else on_scalar)
+            store(n, 512, 2048)
         for n in range(4):
             full_bank(n, 1024, on_scalar)
             full_bank(n, 1536, on_vector)
             store(n, 1024, 2048)
-        for n in range(4, 8):
-            full_bank(n, 1536, on_vector if n % 2 else on_scalar)
-            store(n, 1536, 2048)

@@ -345,8 +345,6 @@ def tile_list_lattice_boltzmann_step_kernel(
                 nc.scalar.copy, w4_grouped[c0 // BANK][:, c0 % BANK : c0 % BANK + 256, :], w4_raw[:, :, c0 : c0 + 256]
             )
         w4s = held("w4s", [P, N], U8)
-        w4_codes = [held("w4_codes0", [P, BANK], U32)]
-        quantize(w4_codes[0][:], w4s[:, 0:BANK], w4_grouped[0][:])
         for t in range(PACK - 1):
             scatter_rest(t, BANK, S)
         scatter_rest(PACK - 1, LEAD, S)
@@ -419,6 +417,8 @@ def tile_list_lattice_boltzmann_step_kernel(
             nc.sync.dma_start(out=out_rows[n // 2][:, n % 2, m0:m1], in_=staged[n // 2][:, n % 2, m0:m1])
 
         on_scalar, on_vector = nc.scalar.copy, nc.vector.tensor_copy
+        w4_codes = [placed("w4_codes0", [P, BANK], U32, 0)]
+        quantize(w4_codes[0][:], w4s[:, 0:BANK], w4_grouped[0][:])
         for m0, m1 in PAGE_CHUNKS[:WOVEN]:
             nc.vector.tensor_copy(out=woven[m0][:, :, PACK - 1], in_=page[PACK - 1][:, m0:m1])
         for m0, m1 in PAGE_CHUNKS[:WOVEN]:

@@ -27,6 +27,7 @@ KIB = 1024
 QUADRANTS = (0, 2, 1, 3)
 PAGE_CHUNKS = ((0, 256), (256, 512), (512, 1024), (1024, 1536), (1536, 2048))
 WOVEN = 2
+NARROW = PAGE_CHUNKS[0][1]
 LEAD = 256
 
 
@@ -60,27 +61,13 @@ def tile_list_lattice_boltzmann_step_kernel(
             nc.sync.dma_start(out=dst[:], in_=words[a].rearrange("p t i -> p (t i)").bitcast(I32))
             return dst
 
-        def load_packed_scales(queue, dst, scales):
-            for q in QUADRANTS:
-                queue.dma_start(
-                    out=dst[32 * q : 32 * q + 8, :], in_=scales.bitcast(I32)[:, 4 * q : 4 * q + 4, :]
-                )
-
-        def load_weights(dst, wg, t0, t1, j0, j1):
-            rows = wg.rearrange("(p t) j -> p t j", t=PACK)
-            for q in QUADRANTS:
-                nc.sync.dma_start(out=dst[32 * q : 32 * q + 32], in_=rows[:, t0:t1, j0:j1])
-            return dst
-
         def gather_scales(name, kib, window, offsets):
             picked = placed(name, [P, S], U8, kib)
             nc.vector.tensor_copy(picked[:], window[:].bitcast(U8).indirect(offsets[:]))
             return picked
 
         def gather_words(dst, window, offsets, j0, j1):
-            nc.vector.tensor_copy(
-                dst, window[:].bitcast(U32).indirect(offsets[:, j0 // 16 : j1 // 16])
-            )
+            nc.vector.tensor_copy(dst, window[:].bitcast(U32).indirect(offsets[:, j0 // 16 : j1 // 16]))
 
         def interleave(engine_copy, dst, src):
             engine_copy(
@@ -97,8 +84,7 @@ def tile_list_lattice_boltzmann_step_kernel(
         window1 = placed("window1", [P, T // 4], I32, 168)
         v2s_planes = held("v2s_planes", [P, PASSES, S // 4], I32)
         v1s_planes = held("v1s_planes", [P, PASSES, S // 4], I32)
-        nc.gpsimd.memset(window1[:], 0)
-        for filled in (window2, v2s_planes, v1s_planes):
+        for filled in (window2, window1, v2s_planes, v1s_planes):
             nc.vector.memset(filled[:], 0)
         ident = held("ident", [P, P], F32)
         make_identity(nc, ident[:])
@@ -122,7 +108,10 @@ def tile_list_lattice_boltzmann_step_kernel(
         load_spread(window2, tab2_scales)
         load_spread(window1, tab_scales)
         tab2_sb = [load_words("tab2_0", tab2_words, 0, 0)]
-        load_packed_scales(nc.sync, w3s_raw, w3_scales)
+        for q in QUADRANTS:
+            nc.sync.dma_start(
+                out=w3s_raw[32 * q : 32 * q + 8, :], in_=w3_scales.bitcast(I32)[:, 4 * q : 4 * q + 4, :]
+            )
         tab2_sb.append(load_words("tab2_1", tab2_words, 1, 16))
         w3_raw = placed("w3_raw", [P, PASSES, H], I32, 164)
         nc.sync.dma_start(out=w3_raw[:], in_=w3_words.rearrange("a p c i -> p a (c i)").bitcast(I32))
@@ -158,24 +147,31 @@ def tile_list_lattice_boltzmann_step_kernel(
 
         def load_wg1(j0, j1):
             dst = placed("wg1_%d" % j0, [P, PACK, j1 - j0], F32, 72 + j0 // 64)
-            return load_weights(dst, wg1, 0, PACK, j0, j1)
+            rows = wg1.rearrange("(p t) j -> p t j", t=PACK)
+            for q in QUADRANTS:
+                nc.sync.dma_start(out=dst[32 * q : 32 * q + 32], in_=rows[:, 0:PACK, j0:j1])
+            return dst
 
         wg2_turned = []
 
-        def turn_wg2(h, turn):
-            acc = bank(turn)
+        def turn_wg2(h, i_bank):
+            acc = bank(i_bank)
             for b in range(BANK // P):
-                nc.tensor.transpose(acc[:, b * P : (b + 1) * P], wg2_rows[:, h * BANK + b * P : h * BANK + (b + 1) * P], ident[:])
+                j0 = h * BANK + b * P
+                nc.tensor.transpose(acc[:, b * P : (b + 1) * P], wg2_rows[:, j0 : j0 + P], ident[:])
             for b in range(BANK // P):
                 turned = placed("wg2_turned%d%d" % (h, b), [P, PACK, 4, 32], F32, 88 + 8 * h + 2 * b)
-                rows = acc[:, b * P : (b + 1) * P].rearrange("p (m t) -> p t m", t=PACK)
-                nc.scalar.copy(out=turned[:], in_=rows.unsqueeze(2).to_broadcast([P, PACK, 4, 32]))
+                rows = acc[:, b * P : (b + 1) * P].rearrange("p (m u e) -> p u m e", u=2, e=2)
+                nc.scalar.copy(
+                    out=turned[:].rearrange("p (u e) q m -> p u q m e", e=2),
+                    in_=rows.unsqueeze(2).to_broadcast([P, 2, 4, 32, 2]),
+                )
                 wg2_turned.append(turned)
 
         wg2_sb = [placed("wg2_%d" % t, [P, S], F32, 104 + 4 * t) for t in range(PACK)]
 
-        def deal_wg2(t, h, turn):
-            acc = bank(turn)
+        def deal_wg2(t, h, i_bank):
+            acc = bank(i_bank)
             for b in range(BANK // P):
                 source = wg2_turned[4 * h + b][:, t].rearrange("p q m -> p (q m)")
                 nc.tensor.transpose(acc[:, b * P : (b + 1) * P], source, ident[:])
@@ -208,10 +204,10 @@ def tile_list_lattice_boltzmann_step_kernel(
         page = [placed("page%d" % t, [P, T2], F32, (0, 8, 48, 56)[t]) for t in range(PACK)]
         h2 = [placed("h2_%d" % t, [P, S], F32, 136 + 4 * t) for t in range(PACK)]
 
-        def wall_term(t, j0, j1, turn):
+        def wall_term(t, j0, j1, i_bank):
             cols = slice(j0, j1)
             rows = slice(t * P, (t + 1) * P)
-            acc = bank(turn)[:, 0 : j1 - j0]
+            acc = bank(i_bank)[:, 0 : j1 - j0]
             for a in range(PASSES):
                 nc.tensor.matmul_mx(
                     out=acc,
@@ -239,24 +235,20 @@ def tile_list_lattice_boltzmann_step_kernel(
         wall_term(0, LEAD, BANK, 2)
         for t in range(2):
             wall_term(t, BANK, S, t)
-        turn = 0
-        for t in range(2, PACK):
-            for h in range(HALVES):
-                deal_wg2(t, h, (2 + turn) % 3)
-                wall_term(t, h * BANK, (h + 1) * BANK, turn % 3)
-                turn = turn + 2
+        for step, (t, h) in enumerate((t, h) for t in range(2, PACK) for h in range(HALVES)):
+            deal_wg2(t, h, (2 * step + 2) % 3)
+            wall_term(t, h * BANK, (h + 1) * BANK, 2 * step % 3)
         w1_grouped = [placed("w1_grouped%d" % a, [P, BANK, PACK], BF16, 96 + 4 * a) for a in range(PASSES)]
         for a in range(PASSES):
             interleave(nc.scalar.copy, w1_grouped[a][:], w1_raw[a][:])
         for t, j0, j1 in ((0, 0, LEAD), (1, 0, BANK), (0, LEAD, S), (1, BANK, S)):
-            if t < 2:
-                scatter(t, list4, j0, j1, h2[t][:, j0:j1], wg2_sb[t][:, j0:j1])
+            scatter(t, list4, j0, j1, h2[t][:, j0:j1], wg2_sb[t][:, j0:j1])
 
         w1_codes = held("w1_codes", [P, PASSES, H], U32)
         w1s = held("w1s", [P, PASSES, H], U8)
         for a in range(PASSES):
             quantize(w1_codes[:, a, :], w1s[:, a, :], w1_grouped[a][:])
-        wg1_sb = [load_wg1(0, 256)]
+        wg1_sb = [load_wg1(0, LEAD)]
         w4_raw = placed("w4_raw", [P, PACK, N], F32, 88)
         nc.sync.dma_start(out=w4_raw[:], in_=w4.rearrange("(p t) n -> p t n", t=PACK))
         wg1_sb.append(load_wg1(LEAD, S))
@@ -314,7 +306,10 @@ def tile_list_lattice_boltzmann_step_kernel(
                         is_transpose=True, start=(n_term == 0), stop=(n_term == 1),
                     )
             turned = placed("turned%d%d" % (h, b), [P, PACK, P], F32, 64 + 2 * b)
-            nc.scalar.copy(out=turned[:], in_=summed[:].rearrange("p (m t) -> p t m", t=PACK))
+            nc.scalar.copy(
+                out=turned[:].rearrange("p (u e) m -> p u m e", e=2),
+                in_=summed[:].rearrange("p (m u e) -> p u m e", u=2, e=2),
+            )
             back = bank(6 + b % 2)
             for t in range(PACK):
                 nc.tensor.transpose(back[:, t * P : (t + 1) * P], turned[:, t, :], ident[:])
@@ -340,10 +335,10 @@ def tile_list_lattice_boltzmann_step_kernel(
             j0 = BANK - LEAD + b * P
             relax_block(1, terms, b, h1_rest[:, :, j0 : j0 + P])
         w4_grouped = [placed("w4_grouped%d" % u, [P, BANK, PACK], BF16, 160 + 4 * u) for u in range(2)]
-        for c0 in range(0, N, 256):
-            interleave(
-                nc.scalar.copy, w4_grouped[c0 // BANK][:, c0 % BANK : c0 % BANK + 256, :], w4_raw[:, :, c0 : c0 + 256]
-            )
+        quarter = N // 4
+        for c0 in range(0, N, quarter):
+            dst = w4_grouped[c0 // BANK][:, c0 % BANK : c0 % BANK + quarter, :]
+            interleave(nc.scalar.copy, dst, w4_raw[:, :, c0 : c0 + quarter])
         w4s = held("w4s", [P, N], U8)
         for t in range(PACK - 1):
             scatter_rest(t, BANK, S)
@@ -399,14 +394,14 @@ def tile_list_lattice_boltzmann_step_kernel(
 
         def half_bank(n, m0, engine_copy):
             acc = fresh_bank()
-            product(acc[:, 0:256], n, m0, m0 + 256)
-            engine_copy(out=staged[n // 2][:, n % 2, m0 : m0 + 256], in_=acc[:, 0:256])
+            product(acc[:, 0:NARROW], n, m0, m0 + NARROW)
+            engine_copy(out=staged[n // 2][:, n % 2, m0 : m0 + NARROW], in_=acc[:, 0:NARROW])
 
         def pair_bank(u, m0, engine_copy):
             acc = fresh_bank()
             for e in range(2):
-                product(acc[:, e * 256 : (e + 1) * 256], 2 * u + e, m0, m0 + 256)
-            engine_copy(out=staged[u][:, :, m0 : m0 + 256], in_=acc[:].rearrange("p (e m) -> p e m", e=2))
+                product(acc[:, e * NARROW : (e + 1) * NARROW], 2 * u + e, m0, m0 + NARROW)
+            engine_copy(out=staged[u][:, :, m0 : m0 + NARROW], in_=acc[:].rearrange("p (e m) -> p e m", e=2))
 
         def full_bank(n, m0, engine_copy):
             acc = fresh_bank()
@@ -435,22 +430,23 @@ def tile_list_lattice_boltzmann_step_kernel(
         quantize_page(*second)
         merge_pairs(*third)
         quantize_page(*third)
-        for n in range(4):
+        low, high = range(N // P // 2), range(N // P // 2, N // P)
+        for n in low:
             half_bank(n, 0, on_scalar)
-            store(n, 0, 256)
-        for n in range(4, 8):
+            store(n, 0, NARROW)
+        for n in high:
             full_bank(n, 0, on_scalar)
-            store(n, 0, 512)
-        for u in range(2):
-            pair_bank(u, 256, on_scalar)
+            store(n, 0, BANK)
+        for u in range(len(low) // 2):
+            pair_bank(u, NARROW, on_scalar)
             for n in (2 * u, 2 * u + 1):
-                full_bank(n, 512, on_scalar)
-                store(n, 256, 1024)
-        for n in range(4, 8):
-            for c, m0 in enumerate((512, 1024, 1536)):
+                full_bank(n, BANK, on_scalar)
+                store(n, NARROW, 2 * BANK)
+        for n in high:
+            for c, m0 in enumerate(range(BANK, T2, BANK)):
                 full_bank(n, m0, on_vector if (n + c) % 2 == 0 else on_scalar)
-            store(n, 512, 2048)
-        for n in range(4):
-            full_bank(n, 1024, on_scalar)
-            full_bank(n, 1536, on_vector)
-            store(n, 1024, 2048)
+            store(n, BANK, T2)
+        for n in low:
+            full_bank(n, 2 * BANK, on_scalar)
+            full_bank(n, 3 * BANK, on_vector)
+            store(n, 2 * BANK, T2)

@@ -80,8 +80,8 @@ def tile_list_lattice_boltzmann_step_kernel(
                 out=codes.bitcast(FP8X4), scales=scales, in_=grouped.rearrange("p c t -> p (c t)")
             )
 
-        window2 = placed("window2", [P, T // 4], I32, 172)
-        window1 = placed("window1", [P, T // 4], I32, 168)
+        window2 = placed("window2", [P, T // 4], I32, 124)
+        window1 = placed("window1", [P, T // 4], I32, 120)
         v2s_planes = held("v2s_planes", [P, PASSES, S // 4], I32)
         v1s_planes = held("v1s_planes", [P, PASSES, S // 4], I32)
         for filled in (window2, window1, v2s_planes, v1s_planes):
@@ -90,14 +90,16 @@ def tile_list_lattice_boltzmann_step_kernel(
         make_identity(nc, ident[:])
         w3s_raw = held("w3s_raw", [P, H // 4], I32)
         nc.vector.memset(w3s_raw[:], 0)
+        w2s = held("w2s", [P, PASSES, H // 4], I32)
+        nc.vector.memset(w2s[:], 0)
 
         def load_spread(window, scales):
             nc.sync.dma_start(out=window[0:P:4, :], in_=scales.bitcast(I32).rearrange("a q t -> q a t"))
 
         def move_scale_rows(planes, spread):
-            for q in range(4):
+            for q in QUADRANTS:
                 nc.sync.dma_start(
-                    out=planes[32 * q : 32 * q + 4], in_=spread[32 * q : 32 * q + 32 : 4, :].bitcast(I32)
+                    out=planes[32 * q : 32 * q + 4], in_=spread[32 * q : 32 * q + 32 : 4, 0:S].bitcast(I32)
                 )
 
         wg2_rows = placed("wg2_rows", [P, S], F32, 160)
@@ -119,34 +121,33 @@ def tile_list_lattice_boltzmann_step_kernel(
         wall_cols = held("wall_cols", [P, PACK], F32)
         nc.sync.dma_start(out=wall_cols[:], in_=wall.rearrange("(p t) -> p t", t=PACK))
 
-        v2s_spread = gather_scales("v2s_spread", 79.5, window2, list2)
+        v2s_spread = placed("v2s_spread", [P, 39 * KIB], U8, 168)
+        nc.vector.tensor_copy(v2s_spread[:, 0:S], window2[:].bitcast(U8).indirect(list2[:]))
         v1s_spread = gather_scales("v1s_spread", 48, window1, list1)
         v2s = [v2s_planes[:, a, :].bitcast(U8) for a in range(PASSES)]
         v1s = [v1s_planes[:, a, :].bitcast(U8) for a in range(PASSES)]
         move_scale_rows(v2s_planes, v2s_spread)
-        tab_sb = [load_words("tab_0", tab_words, 0, 175)]
-        w2_sb = placed("w2_sb", [P, PASSES, H // 2], I32, 168)
-        nc.sync.dma_start(out=w2_sb[:], in_=w2_words.bitcast(I32).rearrange("a p c -> p a c"))
-        rate_cols = placed("rate_cols", [P, PACK], F32, 170)
-        with nc.allow_non_contiguous_dma(reason="one rate a partition"):
-            nc.sync.dma_start(out=rate_cols[:], in_=rate.rearrange("(c p) -> p c", p=P))
         move_scale_rows(v1s_planes, v1s_spread)
-        w2s = placed("w2s", [P, PASSES, H // 4], I32, 171)
-        nc.gpsimd.memset(w2s[:], 0)
-        w2s_rows = w2_scales.bitcast(I32).rearrange("a (q r) c -> r q a c", r=4)
-        for r in range(4):
-            nc.sync.dma_start(out=w2s[r:P:32], in_=w2s_rows[r])
         w1_raw = []
         for a in range(PASSES):
-            raw = placed("w1_raw%d" % a, [P, PACK, H], F32, 72 + 8 * a)
+            raw = placed("w1_raw%d" % a, [P, PACK, H], F32, 191 + 8 * a)
             nc.sync.dma_start(
                 out=raw[:], in_=w1[512 * a : 512 * (a + 1), :].rearrange("(p t) c -> p t c", t=PACK)
             )
             w1_raw.append(raw)
+        tab_sb = [load_words("tab_0", tab_words, 0, 175)]
+        w2_sb = placed("w2_sb", [P, PASSES, H // 2], I32, 168)
+        nc.sync.dma_start(out=w2_sb[:], in_=w2_words.bitcast(I32).rearrange("a p c -> p a c"))
+        w2s_rows = w2_scales.bitcast(I32).rearrange("a (q r) c -> r q a c", r=4)
+        for r in range(4):
+            nc.sync.dma_start(out=w2s[r:P:32], in_=w2s_rows[r])
+        rate_cols = placed("rate_cols", [P, PACK], F32, 170)
+        with nc.allow_non_contiguous_dma(reason="one rate a partition"):
+            nc.sync.dma_start(out=rate_cols[:], in_=rate.rearrange("(c p) -> p c", p=P))
         tab_sb.append(load_words("tab_1", tab_words, 1, 48))
 
         def load_wg1(j0, j1):
-            dst = placed("wg1_%d" % j0, [P, PACK, j1 - j0], F32, 72 + j0 // 64)
+            dst = placed("wg1_%d" % j0, [P, PACK, j1 - j0], F32, 191 + j0 // 64)
             rows = wg1.rearrange("(p t) j -> p t j", t=PACK)
             for q in QUADRANTS:
                 nc.sync.dma_start(out=dst[32 * q : 32 * q + 32], in_=rows[:, 0:PACK, j0:j1])
@@ -177,8 +178,6 @@ def tile_list_lattice_boltzmann_step_kernel(
                 nc.tensor.transpose(acc[:, b * P : (b + 1) * P], source, ident[:])
             nc.scalar.copy(out=wg2_sb[t][:, h * BANK : (h + 1) * BANK], in_=acc[:])
 
-        kept_cols = held("kept_cols", [P, PACK], F32)
-        nc.scalar.activation(kept_cols[:], rate_cols[:], COPY, bias=1.0, scale=-1.0)
 
         v2_0 = placed("v2_0", [P, S], U32, 152)
         gather_words(v2_0[:], tab2_sb[0], list2, 0, S)
@@ -227,20 +226,20 @@ def tile_list_lattice_boltzmann_step_kernel(
 
         for h in range(HALVES):
             turn_wg2(h, 4 + h)
-        for t in range(2):
-            for h in range(HALVES):
-                deal_wg2(t, h, 6 + h)
+        for step, (t, h) in enumerate((t, h) for t in range(PACK) for h in range(HALVES)):
+            deal_wg2(t, h, 4 + step % 4)
         wall_term(0, 0, LEAD, 0)
         wall_term(1, 0, BANK, 1)
         wall_term(0, LEAD, BANK, 2)
         for t in range(2):
             wall_term(t, BANK, S, t)
         for step, (t, h) in enumerate((t, h) for t in range(2, PACK) for h in range(HALVES)):
-            deal_wg2(t, h, (2 * step + 2) % 3)
-            wall_term(t, h * BANK, (h + 1) * BANK, 2 * step % 3)
+            wall_term(t, h * BANK, (h + 1) * BANK, (step + 2) % 3)
         w1_grouped = [placed("w1_grouped%d" % a, [P, BANK, PACK], BF16, 96 + 4 * a) for a in range(PASSES)]
         for a in range(PASSES):
             interleave(nc.scalar.copy, w1_grouped[a][:], w1_raw[a][:])
+        kept_cols = held("kept_cols", [P, PACK], F32)
+        nc.scalar.activation(kept_cols[:], rate_cols[:], COPY, bias=1.0, scale=-1.0)
         for t, j0, j1 in ((0, 0, LEAD), (1, 0, BANK), (0, LEAD, S), (1, BANK, S)):
             scatter(t, list4, j0, j1, h2[t][:, j0:j1], wg2_sb[t][:, j0:j1])
 
@@ -334,7 +333,7 @@ def tile_list_lattice_boltzmann_step_kernel(
         for b in range(BANK // P):
             j0 = BANK - LEAD + b * P
             relax_block(1, terms, b, h1_rest[:, :, j0 : j0 + P])
-        w4_grouped = [placed("w4_grouped%d" % u, [P, BANK, PACK], BF16, 160 + 4 * u) for u in range(2)]
+        w4_grouped = [placed("w4_grouped%d" % u, [P, BANK, PACK], BF16, 64 + 4 * u) for u in range(2)]
         quarter = N // 4
         for c0 in range(0, N, quarter):
             dst = w4_grouped[c0 // BANK][:, c0 % BANK : c0 % BANK + quarter, :]

@@ -15,6 +15,7 @@ U8 = mybir.dt.uint8
 FP8X4 = mybir.dt.float8_e4m3fn_x4
 FP4X4 = mybir.dt.float4_e2m1fn_x4
 MULT = mybir.AluOpType.mult
+ADD = mybir.AluOpType.add
 COPY = mybir.ActivationFunctionType.Copy
 IDENTITY = mybir.ActivationFunctionType.Identity
 
@@ -22,13 +23,13 @@ P = 128
 PACK = 4
 PASSES = K // (P * PACK)
 BANK = 512
-HALVES = S // BANK
 KIB = 1024
 QUADRANTS = (0, 2, 1, 3)
 PAGE_CHUNKS = ((0, 256), (256, 512), (512, 1024), (1024, 1536), (1536, 2048))
-WOVEN = 2
 NARROW = PAGE_CHUNKS[0][1]
 LEAD = 256
+REST = S - LEAD
+STAGE = S + H
 
 
 def tile_list_lattice_boltzmann_step_kernel(
@@ -61,10 +62,15 @@ def tile_list_lattice_boltzmann_step_kernel(
             nc.sync.dma_start(out=dst[:], in_=words[a].rearrange("p t i -> p (t i)").bitcast(I32))
             return dst
 
-        def gather_scales(name, kib, window, offsets):
-            picked = placed(name, [P, S], U8, kib)
-            nc.vector.tensor_copy(picked[:], window[:].bitcast(U8).indirect(offsets[:]))
-            return picked
+        def load_spread(dst, scales):
+            nc.sync.dma_start(out=dst, in_=scales.bitcast(I32).rearrange("a q t -> q a t"))
+
+        def load_dealt(name, kib, weights, t0, t1, j0, j1):
+            dst = placed(name, [P, t1 - t0, j1 - j0], F32, kib)
+            rows = weights.rearrange("(p t) j -> p t j", t=PACK)
+            for q in QUADRANTS:
+                nc.sync.dma_start(out=dst[32 * q : 32 * q + 32], in_=rows[:, t0:t1, j0:j1])
+            return dst
 
         def gather_words(dst, window, offsets, j0, j1):
             nc.vector.tensor_copy(dst, window[:].bitcast(U32).indirect(offsets[:, j0 // 16 : j1 // 16]))
@@ -80,310 +86,270 @@ def tile_list_lattice_boltzmann_step_kernel(
                 out=codes.bitcast(FP8X4), scales=scales, in_=grouped.rearrange("p c t -> p (c t)")
             )
 
-        window2 = placed("window2", [P, T // 4], I32, 124)
-        window1 = placed("window1", [P, T // 4], I32, 120)
-        v2s_planes = held("v2s_planes", [P, PASSES, S // 4], I32)
-        v1s_planes = held("v1s_planes", [P, PASSES, S // 4], I32)
-        for filled in (window2, window1, v2s_planes, v1s_planes):
-            nc.vector.memset(filled[:], 0)
+        X, Y, Z = 32, 72, 96
+
+        window2 = placed("window2", [P, T // 4], I32, Y + 11)
+        window1 = placed("window1", [P, T // 4], I32, Y + 20)
+        weight_rows = held("weight_rows", [P, 2, H // 4], I32)
+        planes2 = placed("planes2", [P, PASSES, STAGE // 4], I32, Y + 8)
+        planes1 = held("planes1", [P, PASSES, STAGE // 4], I32)
         ident = held("ident", [P, P], F32)
-        make_identity(nc, ident[:])
-        w3s_raw = held("w3s_raw", [P, H // 4], I32)
-        nc.vector.memset(w3s_raw[:], 0)
-        w2s = held("w2s", [P, PASSES, H // 4], I32)
-        nc.vector.memset(w2s[:], 0)
+        for filled in (window2, window1, weight_rows, ident, planes2, planes1):
+            nc.vector.memset(filled[:], 0)
+        make_identity(nc, ident[:], nomemset=True)
 
-        def load_spread(window, scales):
-            nc.sync.dma_start(out=window[0:P:4, :], in_=scales.bitcast(I32).rearrange("a q t -> q a t"))
-
-        def move_scale_rows(planes, spread):
-            for q in QUADRANTS:
-                nc.sync.dma_start(
-                    out=planes[32 * q : 32 * q + 4], in_=spread[32 * q : 32 * q + 32 : 4, 0:S].bitcast(I32)
-                )
-
-        wg2_rows = placed("wg2_rows", [P, S], F32, 160)
-        nc.sync.dma_start(out=wg2_rows[:], in_=wg2)
         list2 = load_list("list2", offs2)
-        list1 = load_list("list1", offs)
-        list3 = load_list("list3", offs3)
-        load_spread(window2, tab2_scales)
-        load_spread(window1, tab_scales)
-        tab2_sb = [load_words("tab2_0", tab2_words, 0, 0)]
-        for q in QUADRANTS:
-            nc.sync.dma_start(
-                out=w3s_raw[32 * q : 32 * q + 8, :], in_=w3_scales.bitcast(I32)[:, 4 * q : 4 * q + 4, :]
-            )
-        tab2_sb.append(load_words("tab2_1", tab2_words, 1, 16))
-        w3_raw = placed("w3_raw", [P, PASSES, H], I32, 164)
+        w3_raw = held("w3_raw", [P, PASSES, H], I32)
         nc.sync.dma_start(out=w3_raw[:], in_=w3_words.rearrange("a p c i -> p a (c i)").bitcast(I32))
+        list1 = load_list("list1", offs)
+        wg2_rows = held("wg2_rows", [P, LEAD], F32)
+        nc.sync.dma_start(out=wg2_rows[:], in_=wg2[:, 0:LEAD])
+        load_spread(window2[0:P:4, :], tab2_scales)
+        load_spread(window1[0:P:4, :], tab_scales)
+        load_spread(weight_rows[0:P:4, 0, :], w3_scales)
+        load_spread(weight_rows[0:P:4, 1, :], w2_scales)
+        tab2_sb = [load_words("tab2_%d" % a, tab2_words, a, 16 * a) for a in range(PASSES)]
         list4 = load_list("list4", offs4)
         wall_cols = held("wall_cols", [P, PACK], F32)
         nc.sync.dma_start(out=wall_cols[:], in_=wall.rearrange("(p t) -> p t", t=PACK))
+        list3 = load_list("list3", offs3)
 
-        v2s_spread = placed("v2s_spread", [P, 39 * KIB], U8, 168)
-        nc.vector.tensor_copy(v2s_spread[:, 0:S], window2[:].bitcast(U8).indirect(list2[:]))
-        v1s_spread = gather_scales("v1s_spread", 48, window1, list1)
-        v2s = [v2s_planes[:, a, :].bitcast(U8) for a in range(PASSES)]
-        v1s = [v1s_planes[:, a, :].bitcast(U8) for a in range(PASSES)]
-        move_scale_rows(v2s_planes, v2s_spread)
-        move_scale_rows(v1s_planes, v1s_spread)
+        def stage_scales(name, kib, window, offsets, weight, planes):
+            picked = held(name + "_picked", [P, S], U8)
+            nc.vector.tensor_copy(picked[:], window[:].bitcast(U8).indirect(offsets[:]))
+            stage = placed(name, [P, STAGE], U8, kib)
+            nc.vector.tensor_copy(out=stage[:, 0:S].bitcast(I32), in_=picked[:].bitcast(I32))
+            nc.gpsimd.tensor_copy(
+                out=stage[:, S:STAGE].rearrange("p (t m) -> p t m", t=PACK),
+                in_=weight_rows[:, weight, :].bitcast(U8).rearrange("p (m t) -> p t m", t=PACK),
+            )
+            for q in QUADRANTS:
+                nc.sync.dma_start(
+                    out=planes[32 * q : 32 * q + 4], in_=stage[32 * q : 32 * q + 32 : 4, :].bitcast(I32)
+                )
+            return [planes[:, a, :].bitcast(U8) for a in range(PASSES)]
+
+        w3_sb = placed("w3_sb", [P, PASSES, H], U32, Y + 4)
+        nc.scalar.copy(
+            out=w3_sb[:].rearrange("p a (t c i) -> p a c t i", t=PACK, i=4),
+            in_=w3_raw[:].bitcast(U32).rearrange("p a (c i t) -> p a c t i", t=PACK, i=4),
+        )
+        scales2 = stage_scales("stage2", X + 5.5, window2, list2, 0, planes2)
+        scales1 = stage_scales("stage1", X + 21.5, window1, list1, 1, planes1)
+
+        wg2_front = load_dealt("wg2_front", X, wg2, 0, 2, LEAD, S)
+        rate_cols = placed("rate_cols", [P, PACK], F32, X + 6)
+        nc.sync.dma_start(out=rate_cols[:], in_=rate.rearrange("(p t) -> p t", t=PACK))
         w1_raw = []
         for a in range(PASSES):
-            raw = placed("w1_raw%d" % a, [P, PACK, H], F32, 191 + 8 * a)
+            raw = placed("w1_raw%d" % a, [P, PACK, H], F32, X + 6.25 + 8 * a)
             nc.sync.dma_start(
                 out=raw[:], in_=w1[512 * a : 512 * (a + 1), :].rearrange("(p t) c -> p t c", t=PACK)
             )
             w1_raw.append(raw)
-        tab_sb = [load_words("tab_0", tab_words, 0, 175)]
-        w2_sb = placed("w2_sb", [P, PASSES, H // 2], I32, 168)
-        nc.sync.dma_start(out=w2_sb[:], in_=w2_words.bitcast(I32).rearrange("a p c -> p a c"))
-        w2s_rows = w2_scales.bitcast(I32).rearrange("a (q r) c -> r q a c", r=4)
-        for r in range(4):
-            nc.sync.dma_start(out=w2s[r:P:32], in_=w2s_rows[r])
-        rate_cols = placed("rate_cols", [P, PACK], F32, 170)
-        with nc.allow_non_contiguous_dma(reason="one rate a partition"):
-            nc.sync.dma_start(out=rate_cols[:], in_=rate.rearrange("(c p) -> p c", p=P))
-        tab_sb.append(load_words("tab_1", tab_words, 1, 48))
+        tab_sb = [load_words("tab_0", tab_words, 0, X + 22.25)]
 
-        def load_wg1(j0, j1):
-            dst = placed("wg1_%d" % j0, [P, PACK, j1 - j0], F32, 191 + j0 // 64)
-            rows = wg1.rearrange("(p t) j -> p t j", t=PACK)
-            for q in QUADRANTS:
-                nc.sync.dma_start(out=dst[32 * q : 32 * q + 32], in_=rows[:, 0:PACK, j0:j1])
-            return dst
-
-        wg2_turned = []
-
-        def turn_wg2(h, i_bank):
-            acc = bank(i_bank)
-            for b in range(BANK // P):
-                j0 = h * BANK + b * P
-                nc.tensor.transpose(acc[:, b * P : (b + 1) * P], wg2_rows[:, j0 : j0 + P], ident[:])
-            for b in range(BANK // P):
-                turned = placed("wg2_turned%d%d" % (h, b), [P, PACK, 4, 32], F32, 88 + 8 * h + 2 * b)
-                rows = acc[:, b * P : (b + 1) * P].rearrange("p (m u e) -> p u m e", u=2, e=2)
-                nc.scalar.copy(
-                    out=turned[:].rearrange("p (u e) q m -> p u q m e", e=2),
-                    in_=rows.unsqueeze(2).to_broadcast([P, 2, 4, 32, 2]),
-                )
-                wg2_turned.append(turned)
-
-        wg2_sb = [placed("wg2_%d" % t, [P, S], F32, 104 + 4 * t) for t in range(PACK)]
-
-        def deal_wg2(t, h, i_bank):
-            acc = bank(i_bank)
-            for b in range(BANK // P):
-                source = wg2_turned[4 * h + b][:, t].rearrange("p q m -> p (q m)")
-                nc.tensor.transpose(acc[:, b * P : (b + 1) * P], source, ident[:])
-            nc.scalar.copy(out=wg2_sb[t][:, h * BANK : (h + 1) * BANK], in_=acc[:])
-
-
-        v2_0 = placed("v2_0", [P, S], U32, 152)
-        gather_words(v2_0[:], tab2_sb[0], list2, 0, S)
-        w3s = held("w3s", [P, H], U8)
-        nc.vector.tensor_copy(
-            out=w3s[:].rearrange("p (t m) -> p t m", t=PACK),
-            in_=w3s_raw[:].bitcast(U8).rearrange("p (m t) -> p t m", t=PACK),
-        )
-        v2_10 = placed("v2_10", [P, BANK], U32, 156)
-        gather_words(v2_10[:], tab2_sb[1], list2, 0, BANK)
-        w3_columns = w3_raw[:].rearrange("p a (c i t) -> p a c t i", t=PACK, i=4)
-        w3_first = held("w3_first", [P, PASSES, P], I32)
-        nc.vector.tensor_copy(out=w3_first[:].rearrange("p a (c i) -> p a c i", i=4), in_=w3_columns[:, :, :, 0, :])
-        w3_rest = held("w3_rest", [P, PASSES, (PACK - 1) * P], I32)
-        nc.vector.tensor_copy(
-            out=w3_rest[:].rearrange("p a (t c i) -> p a c t i", t=PACK - 1, i=4), in_=w3_columns[:, :, :, 1:PACK, :]
-        )
-        w3_sb = [w3_first[:]] + [w3_rest[:, :, t * P : (t + 1) * P] for t in range(PACK - 1)]
-        v2_11 = placed("v2_11", [P, BANK], U32, 164)
-        gather_words(v2_11[:], tab2_sb[1], list2, BANK, S)
-        v2 = [[v2_0[:, 0:BANK], v2_0[:, BANK:S]], [v2_10[:], v2_11[:]]]
-
-        page = [placed("page%d" % t, [P, T2], F32, (0, 8, 48, 56)[t]) for t in range(PACK)]
-        h2 = [placed("h2_%d" % t, [P, S], F32, 136 + 4 * t) for t in range(PACK)]
-
-        def wall_term(t, j0, j1, i_bank):
-            cols = slice(j0, j1)
-            rows = slice(t * P, (t + 1) * P)
-            acc = bank(i_bank)[:, 0 : j1 - j0]
-            for a in range(PASSES):
-                nc.tensor.matmul_mx(
-                    out=acc,
-                    lhsT=w3_sb[t][:, a, :].bitcast(FP8X4),
-                    lhsT_scale=w3s[4 * a : P, rows],
-                    rhs=v2[a][j0 // BANK][:, j0 % BANK : j0 % BANK + j1 - j0].bitcast(FP8X4),
-                    rhs_scale=v2s[a][:, cols],
-                    start=(a == 0),
-                    stop=(a == PASSES - 1),
-                )
-            nc.scalar.activation(h2[t][:, cols], acc, IDENTITY, bias=wall_cols[:, t : t + 1], scale=-1.0)
-
-        def scatter(t, offsets, j0, j1, values, weights):
-            nc.vector.tensor_tensor(
-                page[t][:].indirect(offsets[:, j0 // 16 : j1 // 16]), values, weights, MULT
-            )
-
-        for h in range(HALVES):
-            turn_wg2(h, 4 + h)
-        for step, (t, h) in enumerate((t, h) for t in range(PACK) for h in range(HALVES)):
-            deal_wg2(t, h, 4 + step % 4)
-        wall_term(0, 0, LEAD, 0)
-        wall_term(1, 0, BANK, 1)
-        wall_term(0, LEAD, BANK, 2)
-        for t in range(2):
-            wall_term(t, BANK, S, t)
-        for step, (t, h) in enumerate((t, h) for t in range(2, PACK) for h in range(HALVES)):
-            wall_term(t, h * BANK, (h + 1) * BANK, (step + 2) % 3)
-        w1_grouped = [placed("w1_grouped%d" % a, [P, BANK, PACK], BF16, 96 + 4 * a) for a in range(PASSES)]
-        for a in range(PASSES):
-            interleave(nc.scalar.copy, w1_grouped[a][:], w1_raw[a][:])
-        kept_cols = held("kept_cols", [P, PACK], F32)
-        nc.scalar.activation(kept_cols[:], rate_cols[:], COPY, bias=1.0, scale=-1.0)
-        for t, j0, j1 in ((0, 0, LEAD), (1, 0, BANK), (0, LEAD, S), (1, BANK, S)):
-            scatter(t, list4, j0, j1, h2[t][:, j0:j1], wg2_sb[t][:, j0:j1])
-
-        w1_codes = held("w1_codes", [P, PASSES, H], U32)
-        w1s = held("w1s", [P, PASSES, H], U8)
-        for a in range(PASSES):
-            quantize(w1_codes[:, a, :], w1s[:, a, :], w1_grouped[a][:])
-        wg1_sb = [load_wg1(0, LEAD)]
-        w4_raw = placed("w4_raw", [P, PACK, N], F32, 88)
-        nc.sync.dma_start(out=w4_raw[:], in_=w4.rearrange("(p t) n -> p t n", t=PACK))
-        wg1_sb.append(load_wg1(LEAD, S))
-        v1 = [held("v1_%d" % a, [P, S], U32) for a in range(PASSES)]
-        gather_words(v1[0][:], tab_sb[0], list1, 0, S)
-        for h in range(HALVES):
-            gather_words(v1[1][:, h * BANK : (h + 1) * BANK], tab_sb[1], list1, h * BANK, (h + 1) * BANK)
-        for t in range(2, PACK):
-            scatter(t, list4, 0, S, h2[t][:], wg2_sb[t][:])
-
-        w2_bytes = w2_sb[:].bitcast(U8)
-        w2s_bytes = w2s[:].bitcast(U8)
-
-        def scaled_product(name, kib, acc, weights, weight_scales, h, factor):
-            cols = slice(h * BANK, (h + 1) * BANK)
-            for a in range(PASSES):
-                nc.tensor.matmul_mx(
-                    out=acc[:],
-                    lhsT=weights[a],
-                    lhsT_scale=weight_scales[a],
-                    rhs=v1[a][:, cols].bitcast(FP8X4),
-                    rhs_scale=v1s[a][:, cols],
-                    start=(a == 0),
-                    stop=(a == PASSES - 1),
-                )
-            term = placed(name, [P, BANK], F32, kib)
-            nc.scalar.activation(term[:], acc[:], COPY, scale=factor)
-            return term
-
-        def relax_terms(h, kib):
-            terms = []
-            for c in range(PACK):
-                kept = scaled_product(
-                    "kept%d%d" % (h, c), kib + 4 * c, bank(2 * c % 4),
-                    [w1_codes[:, a, c * P : (c + 1) * P].bitcast(FP8X4) for a in range(PASSES)],
-                    [w1s[:, a, c * P : (c + 1) * P] for a in range(PASSES)],
-                    h, kept_cols[:, c : c + 1],
-                )
-                relaxed = scaled_product(
-                    "relaxed%d%d" % (h, c), kib + 4 * c + 2, bank((2 * c + 1) % 4),
-                    [w2_bytes[:, a, 2 * c * P : 2 * (c + 1) * P].bitcast(FP4X4) for a in range(PASSES)],
-                    [w2s_bytes[:, a, c * P : (c + 1) * P] for a in range(PASSES)],
-                    h, rate_cols[:, c : c + 1],
-                )
-                terms.append((kept, relaxed))
-            return terms
-
-        def relax_block(h, terms, b, dst):
-            block = slice(b * P, (b + 1) * P)
-            summed = bank(4 + b % 2)
-            for c in range(PACK):
-                for n_term, term in enumerate(terms[c]):
-                    nc.tensor.matmul(
-                        summed[:, c * P : (c + 1) * P], lhsT=term[:, block], rhs=ident[:],
-                        is_transpose=True, start=(n_term == 0), stop=(n_term == 1),
-                    )
-            turned = placed("turned%d%d" % (h, b), [P, PACK, P], F32, 64 + 2 * b)
+        wg2_lead = held("wg2_lead", [P, PACK, LEAD], F32)
+        acc = bank(4)
+        turned = []
+        for b in range(LEAD // P):
+            nc.tensor.transpose(acc[:, b * P : (b + 1) * P], wg2_rows[:, b * P : (b + 1) * P], ident[:])
+        for b in range(LEAD // P):
+            sorted_rows = held("wg2_turned%d" % b, [P, PACK, 4, 32], F32)
+            rows = acc[:, b * P : (b + 1) * P].rearrange("p (m u e) -> p u m e", u=2, e=2)
             nc.scalar.copy(
-                out=turned[:].rearrange("p (u e) m -> p u m e", e=2),
-                in_=summed[:].rearrange("p (m u e) -> p u m e", u=2, e=2),
+                out=sorted_rows[:].rearrange("p (u e) q m -> p u q m e", e=2),
+                in_=rows.unsqueeze(2).to_broadcast([P, 2, 4, 32, 2]),
             )
-            back = bank(6 + b % 2)
-            for t in range(PACK):
-                nc.tensor.transpose(back[:, t * P : (t + 1) * P], turned[:, t, :], ident[:])
-            nc.scalar.copy(out=dst, in_=back[:].rearrange("p (t j) -> p t j", t=PACK))
+            turned.append(sorted_rows)
+        for u in range(2):
+            acc = bank(5 + u)
+            for e in range(2):
+                for b in range(LEAD // P):
+                    j0 = e * LEAD + b * P
+                    source = turned[b][:, 2 * u + e].rearrange("p q m -> p (q m)")
+                    nc.tensor.transpose(acc[:, j0 : j0 + P], source, ident[:])
+            nc.scalar.copy(
+                out=wg2_lead[:, 2 * u : 2 * u + 2, :], in_=acc[:].rearrange("p (e j) -> p e j", e=2)
+            )
 
-        terms = relax_terms(0, 120)
-        h1_first = placed("h1_first", [P, PACK, LEAD], F32, 16)
-        h1_rest = placed("h1_rest", [P, PACK, S - LEAD], F32, 20)
-        for b in range(BANK // P):
-            dst = h1_first if b * P < LEAD else h1_rest
-            relax_block(0, terms, b, dst[:, :, b * P % LEAD : b * P % LEAD + P])
-        for t in range(PACK):
-            scatter(t, list3, 0, LEAD, h1_first[:, t, :], wg1_sb[0][:, t, :])
+        v2 = [placed("v2_%d" % a, [P, S], U32, Y + 16 * a) for a in range(PASSES)]
+        gather_words(v2[0][:], tab2_sb[0], list2, 0, S)
+        gather_words(v2[1][:, 0:LEAD], tab2_sb[1], list2, 0, LEAD)
+        gather_words(v2[1][:, LEAD:S], tab2_sb[1], list2, LEAD, S)
 
-        def scatter_rest(t, j0, j1):
-            cols = slice(j0 - LEAD, j1 - LEAD)
-            scatter(t, list3, j0, j1, h1_rest[:, t, cols], wg1_sb[1][:, t, cols])
-
-        for t in range(PACK - 1):
-            scatter_rest(t, LEAD, BANK)
-        terms = relax_terms(1, 32)
-        for b in range(BANK // P):
-            j0 = BANK - LEAD + b * P
-            relax_block(1, terms, b, h1_rest[:, :, j0 : j0 + P])
-        w4_grouped = [placed("w4_grouped%d" % u, [P, BANK, PACK], BF16, 64 + 4 * u) for u in range(2)]
-        quarter = N // 4
-        for c0 in range(0, N, quarter):
-            dst = w4_grouped[c0 // BANK][:, c0 % BANK : c0 % BANK + quarter, :]
-            interleave(nc.scalar.copy, dst, w4_raw[:, :, c0 : c0 + quarter])
-        w4s = held("w4s", [P, N], U8)
-        for t in range(PACK - 1):
-            scatter_rest(t, BANK, S)
-        scatter_rest(PACK - 1, LEAD, S)
-
-        woven = {
-            m0: placed("page_grouped%d" % m0, [P, m1 - m0, PACK], BF16, 136 + m0 // 128)
-            for m0, m1 in PAGE_CHUNKS[:WOVEN]
-        }
-        paired = {
-            m0: placed("paired%d" % m0, [P, 2, m1 - m0, 2], BF16, 104 + m0 // 128) for m0, m1 in PAGE_CHUNKS[WOVEN:]
-        }
-        for t in range(PACK - 1):
-            for m0, m1 in PAGE_CHUNKS:
-                dst = woven[m0][:, :, t : t + 2] if m0 in woven else paired[m0][:, t // 2, :, :]
-                if t < PACK - 2:
-                    nc.scalar.copy(out=dst[:, :, 0 if m0 in woven else t], in_=page[t][:, m0:m1])
-                else:
-                    nc.scalar.copy(out=dst, in_=page[t][:, m0:m1].unsqueeze(2).to_broadcast([P, m1 - m0, 2]))
-        page_codes = placed("page_codes", [P, T2], U32, 152)
-        page_s = held("page_s", [P, T2], U8)
-        merged = {}
-
-        def pair_last(m0, m1):
-            nc.vector.tensor_copy(out=paired[m0][:, 1, :, 1], in_=page[PACK - 1][:, m0:m1])
-
-        def merge_pairs(m0, m1):
-            merged[m0] = placed("page_grouped%d" % m0, [P, m1 - m0, PACK], BF16, 136 + m0 // 128)
-            words = paired[m0][:].rearrange("p u m e -> p u (m e)").bitcast(I32)
-            interleave(nc.vector.tensor_copy, merged[m0][:].bitcast(I32), words)
-
-        def quantize_page(m0, m1):
-            quantize(page_codes[:, m0:m1], page_s[:, m0:m1], merged[m0][:])
-
-        staged = [placed("staged%d" % u, [P, 2, T2], F32, (32, 72, 88, 120)[u]) for u in range(4)]
-        out_rows = out.rearrange("(u e p) m -> u p e m", e=2, p=P)
+        page = [placed("page%d" % t, [P, T2], F32, 8 * t) for t in range(PACK)]
+        h2 = [placed("h2_%d" % t, [P, S], F32, Z + 4 * t) for t in range(PACK)]
         used = []
 
         def fresh_bank():
             used.append(len(used))
             return bank(used[-1])
 
-        def product(dst, n, m0, m1):
+        def product(acc, weights, weight_scales, values, value_scales, j0, j1):
+            for a in range(PASSES):
+                nc.tensor.matmul_mx(
+                    out=acc,
+                    lhsT=weights[a],
+                    lhsT_scale=weight_scales[a],
+                    rhs=values[a][:, j0:j1].bitcast(FP8X4),
+                    rhs_scale=value_scales[a][:, j0:j1],
+                    start=(a == 0),
+                    stop=(a == PASSES - 1),
+                )
+
+        def wall_term(t, j0, j1):
+            acc = fresh_bank()[:, 0 : j1 - j0]
+            product(
+                acc,
+                [w3_sb[:, a, t * P : (t + 1) * P].bitcast(FP8X4) for a in range(PASSES)],
+                [scales2[a][:, S + t * P : S + (t + 1) * P] for a in range(PASSES)],
+                v2, scales2, j0, j1,
+            )
+            nc.scalar.activation(h2[t][:, j0:j1], acc, IDENTITY, bias=wall_cols[:, t : t + 1], scale=-1.0)
+
+        def scatter_weighted(t, offsets, j0, j1, values, weights):
+            nc.vector.tensor_tensor(
+                page[t][:].indirect(offsets[:, j0 // 16 : j1 // 16]), values, weights, MULT
+            )
+
+        def scatter(t, offsets, j0, j1, values):
+            nc.vector.tensor_copy(page[t][:].indirect(offsets[:, j0 // 16 : j1 // 16]), values)
+
+        for t in range(PACK):
+            wall_term(t, 0, LEAD)
+        for t in range(PACK):
+            wall_term(t, LEAD, BANK)
+            wall_term(t, BANK, S)
+        for t in range(PACK):
+            scatter_weighted(t, list4, 0, LEAD, h2[t][:, 0:LEAD], wg2_lead[:, t, :])
+        for t in range(2):
+            scatter_weighted(t, list4, LEAD, S, h2[t][:, LEAD:S], wg2_front[:, t, :])
+
+        w2_raw = placed("w2_raw", [P, PASSES, H // 2], I32, Y)
+        nc.sync.dma_start(out=w2_raw[:], in_=w2_words.bitcast(I32).rearrange("a p c -> p a c"))
+        tab_sb.append(load_words("tab_1", tab_words, 1, Y + 2))
+        wg2_back = load_dealt("wg2_back", Y + 18, wg2, 2, PACK, LEAD, S)
+
+        w1_grouped = [placed("w1_grouped%d" % a, [P, H, PACK], BF16, 166 + 8 * a) for a in range(PASSES)]
+        for a in range(PASSES):
+            nc.scalar.copy(
+                out=w1_grouped[a][:].rearrange("p (t m) i -> p m t i", t=PACK),
+                in_=w1_raw[a][:].rearrange("p i (m t) -> p m t i", t=PACK),
+            )
+        kept_cols = held("kept_cols", [P, PACK], F32)
+        nc.scalar.activation(kept_cols[:], rate_cols[:], COPY, bias=1.0, scale=-1.0)
+        w2_sb = held("w2_sb", [P, PASSES, H], U16)
+        nc.scalar.copy(
+            out=w2_sb[:].rearrange("p a (t m) -> p a m t", t=PACK),
+            in_=w2_raw[:].bitcast(U16).rearrange("p a (m t) -> p a m t", t=PACK),
+        )
+        w1_codes = held("w1_codes", [P, PASSES, H], U32)
+        w1s = held("w1s", [P, PASSES, H], U8)
+        for a in range(PASSES):
+            quantize(w1_codes[:, a, :], w1s[:, a, :], w1_grouped[a][:])
+        wg1_sb = [load_dealt("wg1_0", 160, wg1, 0, 2, 0, S), load_dealt("wg1_1", 168, wg1, 2, PACK, 0, S)]
+        w4_raw = placed("w4_raw", [P, PACK, N], F32, 176)
+        nc.sync.dma_start(out=w4_raw[:], in_=w4.rearrange("(p t) n -> p t n", t=PACK))
+
+        v1 = [placed("v1_%d" % a, [P, S], U32, Z + 4 - 4 * a) for a in range(PASSES)]
+        gather_words(v1[0][:], tab_sb[0], list1, 0, S)
+        for j0 in range(0, S, BANK):
+            gather_words(v1[1][:, j0 : j0 + BANK], tab_sb[1], list1, j0, j0 + BANK)
+        for t in range(2, PACK):
+            weighted = placed("weighted%d" % t, [P, REST], F32, X + 3 * (t - 2))
+            nc.gpsimd.tensor_tensor(weighted[:], h2[t][:, LEAD:S], wg2_back[:, t - 2, :], MULT)
+            scatter(t, list4, LEAD, S, weighted[:])
+
+        w2_bytes = w2_sb[:].bitcast(U8)
+        kept = [placed("kept%d" % t, [P, S], F32, X + 22.25 + 4 * t) for t in range(PACK)]
+        relaxed = [placed("relaxed%d" % t, [P, S], F32, (Y + 18, Z + 8, Z + 12, Y + 2)[t]) for t in range(PACK)]
+        for t in range(PACK):
+            rows = slice(t * P, (t + 1) * P)
+            for j0 in range(0, S, BANK):
+                step = 2 * (2 * t + j0 // BANK)
+                acc = bank(step % 3)
+                product(
+                    acc[:], [w1_codes[:, a, rows].bitcast(FP8X4) for a in range(PASSES)],
+                    [w1s[:, a, rows] for a in range(PASSES)], v1, scales1, j0, j0 + BANK,
+                )
+                nc.scalar.activation(kept[t][:, j0 : j0 + BANK], acc[:], COPY, scale=kept_cols[:, t : t + 1])
+                acc = bank((step + 1) % 3)
+                product(
+                    acc[:], [w2_bytes[:, a, 2 * t * P : 2 * (t + 1) * P].bitcast(FP4X4) for a in range(PASSES)],
+                    [scales1[a][:, S + t * P : S + (t + 1) * P] for a in range(PASSES)], v1, scales1, j0, j0 + BANK,
+                )
+                nc.scalar.activation(relaxed[t][:, j0 : j0 + BANK], acc[:], COPY, scale=rate_cols[:, t : t + 1])
+
+        def add_terms(t, j0, j1, kib):
+            summed = placed("summed%d_%d" % (t, j0), [P, j1 - j0], F32, kib)
+            nc.gpsimd.tensor_tensor(summed[:], kept[t][:, j0:j1], relaxed[t][:, j0:j1], ADD)
+            return summed
+
+        def weigh(t, j0, j1, summed):
+            nc.gpsimd.tensor_tensor(kept[t][:, j0:j1], summed, wg1_sb[t // 2][:, t % 2, j0:j1], MULT)
+
+        halves = [add_terms(0, j0, j0 + BANK, 112 + j0 // 256) for j0 in range(0, S, BANK)]
+        for h in range(2):
+            weigh(0, h * BANK, (h + 1) * BANK, halves[h][:])
+        middle = [add_terms(1, 0, S, 112), add_terms(2, 0, S, Z + 8)]
+        for t in (1, 2):
+            weigh(t, 0, S, middle[t - 1][:])
+        weigh(3, 0, S, add_terms(3, 0, S, 112)[:])
+        for t in range(PACK):
+            scatter(t, list3, 0, S, kept[t][:])
+
+        w4_grouped = [placed("w4_grouped%d" % u, [P, BANK, PACK], BF16, Z + 4 * u) for u in range(2)]
+        for u in range(2):
+            interleave(nc.scalar.copy, w4_grouped[u][:], w4_raw[:, :, u * BANK : (u + 1) * BANK])
+
+        grouped = {
+            m0: placed("page_grouped%d" % m0, [P, m1 - m0, PACK], BF16, 176 + m0 // 128) for m0, m1 in PAGE_CHUNKS
+        }
+        for t in range(PACK - 2):
+            for m0, m1 in PAGE_CHUNKS:
+                nc.scalar.copy(out=grouped[m0][:, :, t], in_=page[t][:, m0:m1])
+        for m0, m1 in PAGE_CHUNKS:
+            both = page[2][:, m0:m1].unsqueeze(2).to_broadcast([P, m1 - m0, 2])
+            nc.scalar.copy(out=grouped[m0][:, :, 2:4], in_=both)
+        page_codes = held("page_codes", [P, T2], U32)
+        page_s = held("page_s", [P, T2], U8)
+        w4_codes = {}
+        w4s = held("w4s", [P, N], U8)
+
+        def quantize_w4(n0, n1, kib):
+            u = n0 // BANK
+            codes = placed("w4_codes%d" % n0, [P, n1 - n0], U32, kib)
+            for n in range(n0, n1, P):
+                w4_codes[n // P] = codes[:, n - n0 : n - n0 + P]
+            quantize(codes[:], w4s[:, n0:n1], w4_grouped[u][:, n0 - u * BANK : n1 - u * BANK, :])
+
+        def place_last(m0, m1):
+            nc.vector.tensor_copy(out=grouped[m0][:, :, PACK - 1], in_=page[PACK - 1][:, m0:m1])
+
+        def quantize_page(m0, m1):
+            quantize(page_codes[:, m0:m1], page_s[:, m0:m1], grouped[m0][:])
+
+        quantize_w4(0, 256, 112)
+        for chunk in PAGE_CHUNKS[:2]:
+            place_last(*chunk)
+        quantize_page(*PAGE_CHUNKS[0])
+        quantize_w4(256, 512, 176)
+        quantize_page(*PAGE_CHUNKS[1])
+        quantize_w4(512, 1024, 178)
+        place_last(*PAGE_CHUNKS[2])
+        for c in range(2, len(PAGE_CHUNKS) - 1):
+            place_last(*PAGE_CHUNKS[c + 1])
+            quantize_page(*PAGE_CHUNKS[c])
+        quantize_page(*PAGE_CHUNKS[-1])
+
+        staged = [placed("staged%d" % u, [P, 2, T2], F32, (128, 144, X + 6.25, Y + 2)[u]) for u in range(4)]
+        out_rows = out.rearrange("(u e p) m -> u p e m", e=2, p=P)
+
+        def last_product(dst, n, m0, m1):
             nc.tensor.matmul_mx(
                 out=dst,
-                lhsT=w4_codes[n // 4][:, n % 4 * P : (n % 4 + 1) * P].bitcast(FP8X4),
+                lhsT=w4_codes[n].bitcast(FP8X4),
                 lhsT_scale=w4s[:, n * P : (n + 1) * P],
                 rhs=page_codes[:, m0:m1].bitcast(FP8X4),
                 rhs_scale=page_s[:, m0:m1],
@@ -393,42 +359,24 @@ def tile_list_lattice_boltzmann_step_kernel(
 
         def half_bank(n, m0, engine_copy):
             acc = fresh_bank()
-            product(acc[:, 0:NARROW], n, m0, m0 + NARROW)
+            last_product(acc[:, 0:NARROW], n, m0, m0 + NARROW)
             engine_copy(out=staged[n // 2][:, n % 2, m0 : m0 + NARROW], in_=acc[:, 0:NARROW])
 
         def pair_bank(u, m0, engine_copy):
             acc = fresh_bank()
             for e in range(2):
-                product(acc[:, e * NARROW : (e + 1) * NARROW], 2 * u + e, m0, m0 + NARROW)
+                last_product(acc[:, e * NARROW : (e + 1) * NARROW], 2 * u + e, m0, m0 + NARROW)
             engine_copy(out=staged[u][:, :, m0 : m0 + NARROW], in_=acc[:].rearrange("p (e m) -> p e m", e=2))
 
         def full_bank(n, m0, engine_copy):
             acc = fresh_bank()
-            product(acc[:], n, m0, m0 + BANK)
+            last_product(acc[:], n, m0, m0 + BANK)
             engine_copy(out=staged[n // 2][:, n % 2, m0 : m0 + BANK], in_=acc[:])
 
         def store(n, m0, m1):
             nc.sync.dma_start(out=out_rows[n // 2][:, n % 2, m0:m1], in_=staged[n // 2][:, n % 2, m0:m1])
 
         on_scalar, on_vector = nc.scalar.copy, nc.vector.tensor_copy
-        w4_codes = [placed("w4_codes0", [P, BANK], U32, 0)]
-        quantize(w4_codes[0][:], w4s[:, 0:BANK], w4_grouped[0][:])
-        for m0, m1 in PAGE_CHUNKS[:WOVEN]:
-            nc.vector.tensor_copy(out=woven[m0][:, :, PACK - 1], in_=page[PACK - 1][:, m0:m1])
-        for m0, m1 in PAGE_CHUNKS[:WOVEN]:
-            quantize(page_codes[:, m0:m1], page_s[:, m0:m1], woven[m0][:])
-        first, second, third = PAGE_CHUNKS[WOVEN:]
-        pair_last(*first)
-        w4_codes.append(placed("w4_codes1", [P, BANK], U32, 136))
-        quantize(w4_codes[1][:], w4s[:, BANK:N], w4_grouped[1][:])
-        merge_pairs(*first)
-        pair_last(*second)
-        quantize_page(*first)
-        merge_pairs(*second)
-        pair_last(*third)
-        quantize_page(*second)
-        merge_pairs(*third)
-        quantize_page(*third)
         low, high = range(N // P // 2), range(N // P // 2, N // P)
         for n in low:
             half_bank(n, 0, on_scalar)

@@ -89,12 +89,11 @@ def tile_list_lattice_boltzmann_step_kernel(
         X, Y, Z = 32, 72, 96
 
         window2 = placed("window2", [P, T // 4], I32, Y + 11)
-        window1 = placed("window1", [P, T // 4], I32, Y + 20)
+        window1 = placed("window1", [P, T // 4], I32, X + 4)
         weight_rows = held("weight_rows", [P, 2, H // 4], I32)
-        planes2 = placed("planes2", [P, PASSES, STAGE // 4], I32, Y + 8)
-        planes1 = held("planes1", [P, PASSES, STAGE // 4], I32)
+        planes = held("planes", [P, PASSES, STAGE // 4], I32)
         ident = held("ident", [P, P], F32)
-        for filled in (window2, window1, weight_rows, ident, planes2, planes1):
+        for filled in (window2, window1, weight_rows, ident, planes):
             nc.vector.memset(filled[:], 0)
         make_identity(nc, ident[:], nomemset=True)
 
@@ -114,39 +113,39 @@ def tile_list_lattice_boltzmann_step_kernel(
         nc.sync.dma_start(out=wall_cols[:], in_=wall.rearrange("(p t) -> p t", t=PACK))
         list3 = load_list("list3", offs3)
 
-        def stage_scales(name, kib, window, offsets, weight, planes):
-            picked = held(name + "_picked", [P, S], U8)
+        def stage_scales(name, picked, window, offsets, weight):
             nc.vector.tensor_copy(picked[:], window[:].bitcast(U8).indirect(offsets[:]))
-            stage = placed(name, [P, STAGE], U8, kib)
+            stage = held(name, [P, STAGE], U8)
             nc.vector.tensor_copy(out=stage[:, 0:S].bitcast(I32), in_=picked[:].bitcast(I32))
             nc.gpsimd.tensor_copy(
                 out=stage[:, S:STAGE].rearrange("p (t m) -> p t m", t=PACK),
                 in_=weight_rows[:, weight, :].bitcast(U8).rearrange("p (m t) -> p t m", t=PACK),
             )
+            return stage
+
+        def move_scales(stage):
             for q in QUADRANTS:
                 nc.sync.dma_start(
                     out=planes[32 * q : 32 * q + 4], in_=stage[32 * q : 32 * q + 32 : 4, :].bitcast(I32)
                 )
-            return [planes[:, a, :].bitcast(U8) for a in range(PASSES)]
 
+        scales = [planes[:, a, :].bitcast(U8) for a in range(PASSES)]
         w3_sb = placed("w3_sb", [P, PASSES, H], U32, Y + 4)
         nc.scalar.copy(
             out=w3_sb[:].rearrange("p a (t c i) -> p a c t i", t=PACK, i=4),
             in_=w3_raw[:].bitcast(U32).rearrange("p a (c i t) -> p a c t i", t=PACK, i=4),
         )
-        scales2 = stage_scales("stage2", X + 5.5, window2, list2, 0, planes2)
-        scales1 = stage_scales("stage1", X + 21.5, window1, list1, 1, planes1)
+        move_scales(stage_scales("stage2", held("picked2", [P, S], U8), window2, list2, 0))
+        stage1 = stage_scales("stage1", placed("picked1", [P, S], U8, X + 22), window1, list1, 1)
 
         wg2_front = load_dealt("wg2_front", X, wg2, 0, 2, LEAD, S)
         rate_cols = placed("rate_cols", [P, PACK], F32, X + 6)
         nc.sync.dma_start(out=rate_cols[:], in_=rate.rearrange("(p t) -> p t", t=PACK))
-        w1_raw = []
+        w1_raw = placed("w1_raw", [P, PASSES, PACK, H], F32, X + 6.25)
         for a in range(PASSES):
-            raw = placed("w1_raw%d" % a, [P, PACK, H], F32, X + 6.25 + 8 * a)
             nc.sync.dma_start(
-                out=raw[:], in_=w1[512 * a : 512 * (a + 1), :].rearrange("(p t) c -> p t c", t=PACK)
+                out=w1_raw[:, a], in_=w1[512 * a : 512 * (a + 1), :].rearrange("(p t) c -> p t c", t=PACK)
             )
-            w1_raw.append(raw)
         tab_sb = [load_words("tab_0", tab_words, 0, X + 22.25)]
 
         wg2_lead = held("wg2_lead", [P, PACK, LEAD], F32)
@@ -203,8 +202,8 @@ def tile_list_lattice_boltzmann_step_kernel(
             product(
                 acc,
                 [w3_sb[:, a, t * P : (t + 1) * P].bitcast(FP8X4) for a in range(PASSES)],
-                [scales2[a][:, S + t * P : S + (t + 1) * P] for a in range(PASSES)],
-                v2, scales2, j0, j1,
+                [scales[a][:, S + t * P : S + (t + 1) * P] for a in range(PASSES)],
+                v2, scales, j0, j1,
             )
             nc.scalar.activation(h2[t][:, j0:j1], acc, IDENTITY, bias=wall_cols[:, t : t + 1], scale=-1.0)
 
@@ -226,16 +225,17 @@ def tile_list_lattice_boltzmann_step_kernel(
         for t in range(2):
             scatter_weighted(t, list4, LEAD, S, h2[t][:, LEAD:S], wg2_front[:, t, :])
 
-        w2_raw = placed("w2_raw", [P, PASSES, H // 2], I32, Y)
-        nc.sync.dma_start(out=w2_raw[:], in_=w2_words.bitcast(I32).rearrange("a p c -> p a c"))
         tab_sb.append(load_words("tab_1", tab_words, 1, Y + 2))
         wg2_back = load_dealt("wg2_back", Y + 18, wg2, 2, PACK, LEAD, S)
+        move_scales(stage1)
+        w2_raw = placed("w2_raw", [P, PASSES, H // 2], I32, Y)
+        nc.sync.dma_start(out=w2_raw[:], in_=w2_words.bitcast(I32).rearrange("a p c -> p a c"))
 
         w1_grouped = [placed("w1_grouped%d" % a, [P, H, PACK], BF16, 166 + 8 * a) for a in range(PASSES)]
         for a in range(PASSES):
             nc.scalar.copy(
                 out=w1_grouped[a][:].rearrange("p (t m) i -> p m t i", t=PACK),
-                in_=w1_raw[a][:].rearrange("p i (m t) -> p m t i", t=PACK),
+                in_=w1_raw[:, a].rearrange("p i (m t) -> p m t i", t=PACK),
             )
         kept_cols = held("kept_cols", [P, PACK], F32)
         nc.scalar.activation(kept_cols[:], rate_cols[:], COPY, bias=1.0, scale=-1.0)
@@ -271,13 +271,13 @@ def tile_list_lattice_boltzmann_step_kernel(
                 acc = bank(step % 3)
                 product(
                     acc[:], [w1_codes[:, a, rows].bitcast(FP8X4) for a in range(PASSES)],
-                    [w1s[:, a, rows] for a in range(PASSES)], v1, scales1, j0, j0 + BANK,
+                    [w1s[:, a, rows] for a in range(PASSES)], v1, scales, j0, j0 + BANK,
                 )
                 nc.scalar.activation(kept[t][:, j0 : j0 + BANK], acc[:], COPY, scale=kept_cols[:, t : t + 1])
                 acc = bank((step + 1) % 3)
                 product(
                     acc[:], [w2_bytes[:, a, 2 * t * P : 2 * (t + 1) * P].bitcast(FP4X4) for a in range(PASSES)],
-                    [scales1[a][:, S + t * P : S + (t + 1) * P] for a in range(PASSES)], v1, scales1, j0, j0 + BANK,
+                    [scales[a][:, S + t * P : S + (t + 1) * P] for a in range(PASSES)], v1, scales, j0, j0 + BANK,
                 )
                 nc.scalar.activation(relaxed[t][:, j0 : j0 + BANK], acc[:], COPY, scale=rate_cols[:, t : t + 1])
 
@@ -306,12 +306,21 @@ def tile_list_lattice_boltzmann_step_kernel(
         grouped = {
             m0: placed("page_grouped%d" % m0, [P, m1 - m0, PACK], BF16, 176 + m0 // 128) for m0, m1 in PAGE_CHUNKS
         }
-        for t in range(PACK - 2):
-            for m0, m1 in PAGE_CHUNKS:
-                nc.scalar.copy(out=grouped[m0][:, :, t], in_=page[t][:, m0:m1])
+
+        def round_into_word(t, m0, m1):
+            both = page[t][:, m0:m1].unsqueeze(2).to_broadcast([P, m1 - m0, 2])
+            nc.scalar.copy(out=grouped[m0][:, :, t : t + 2], in_=both)
+
         for m0, m1 in PAGE_CHUNKS:
-            both = page[2][:, m0:m1].unsqueeze(2).to_broadcast([P, m1 - m0, 2])
-            nc.scalar.copy(out=grouped[m0][:, :, 2:4], in_=both)
+            round_into_word(0, m0, m1)
+        for m0, m1 in PAGE_CHUNKS:
+            if m0 < BANK:
+                nc.scalar.copy(out=grouped[m0][:, :, 1], in_=page[1][:, m0:m1])
+            else:
+                both = page[1][:, m0:m1].unsqueeze(2).to_broadcast([P, m1 - m0, 2])
+                nc.gpsimd.tensor_scalar(grouped[m0][:, :, 1:3], both, 1.0, 0.0, MULT, ADD)
+        for m0, m1 in PAGE_CHUNKS:
+            round_into_word(2, m0, m1)
         page_codes = held("page_codes", [P, T2], U32)
         page_s = held("page_s", [P, T2], U8)
         w4_codes = {}

@@ -117,7 +117,7 @@ def tile_list_lattice_boltzmann_step_kernel(
             nc.vector.tensor_copy(picked[:], window[:].bitcast(U8).indirect(offsets[:]))
             stage = held(name, [P, STAGE], U8)
             nc.vector.tensor_copy(out=stage[:, 0:S].bitcast(I32), in_=picked[:].bitcast(I32))
-            nc.gpsimd.tensor_copy(
+            nc.vector.tensor_copy(
                 out=stage[:, S:STAGE].rearrange("p (t m) -> p t m", t=PACK),
                 in_=weight_rows[:, weight, :].bitcast(U8).rearrange("p (m t) -> p t m", t=PACK),
             )
@@ -248,9 +248,10 @@ def tile_list_lattice_boltzmann_step_kernel(
         w1s = held("w1s", [P, PASSES, H], U8)
         for a in range(PASSES):
             quantize(w1_codes[:, a, :], w1s[:, a, :], w1_grouped[a][:])
-        wg1_sb = [load_dealt("wg1_0", 160, wg1, 0, 2, 0, S), load_dealt("wg1_1", 168, wg1, 2, PACK, 0, S)]
+        wg1_sb = [load_dealt("wg1_0", 160, wg1, 0, 2, 0, S)]
         w4_raw = placed("w4_raw", [P, PACK, N], F32, 176)
         nc.sync.dma_start(out=w4_raw[:], in_=w4.rearrange("(p t) n -> p t n", t=PACK))
+        wg1_sb.append(load_dealt("wg1_1", 168, wg1, 2, PACK, 0, S))
 
         v1 = [placed("v1_%d" % a, [P, S], U32, Z + 4 - 4 * a) for a in range(PASSES)]
         gather_words(v1[0][:], tab_sb[0], list1, 0, S)
@@ -292,10 +293,8 @@ def tile_list_lattice_boltzmann_step_kernel(
         halves = [add_terms(0, j0, j0 + BANK, 112 + j0 // 256) for j0 in range(0, S, BANK)]
         for h in range(2):
             weigh(0, h * BANK, (h + 1) * BANK, halves[h][:])
-        middle = [add_terms(1, 0, S, 112), add_terms(2, 0, S, Z + 8)]
-        for t in (1, 2):
-            weigh(t, 0, S, middle[t - 1][:])
-        weigh(3, 0, S, add_terms(3, 0, S, 112)[:])
+        for t in range(1, PACK):
+            weigh(t, 0, S, add_terms(t, 0, S, 112)[:])
         for t in range(PACK):
             scatter(t, list3, 0, S, kept[t][:])
 
@@ -304,23 +303,18 @@ def tile_list_lattice_boltzmann_step_kernel(
             interleave(nc.scalar.copy, w4_grouped[u][:], w4_raw[:, :, u * BANK : (u + 1) * BANK])
 
         grouped = {
-            m0: placed("page_grouped%d" % m0, [P, m1 - m0, PACK], BF16, 176 + m0 // 128) for m0, m1 in PAGE_CHUNKS
+            m0: placed("page_grouped%d" % m0, [P, m1 - m0, PACK], BF16, (176 if m1 < T2 else 160) + m0 // 128) for m0, m1 in PAGE_CHUNKS
         }
 
-        def round_into_word(t, m0, m1):
-            both = page[t][:, m0:m1].unsqueeze(2).to_broadcast([P, m1 - m0, 2])
-            nc.scalar.copy(out=grouped[m0][:, :, t : t + 2], in_=both)
-
-        for m0, m1 in PAGE_CHUNKS:
-            round_into_word(0, m0, m1)
-        for m0, m1 in PAGE_CHUNKS:
-            if m0 < BANK:
-                nc.scalar.copy(out=grouped[m0][:, :, 1], in_=page[1][:, m0:m1])
-            else:
-                both = page[1][:, m0:m1].unsqueeze(2).to_broadcast([P, m1 - m0, 2])
-                nc.gpsimd.tensor_scalar(grouped[m0][:, :, 1:3], both, 1.0, 0.0, MULT, ADD)
-        for m0, m1 in PAGE_CHUNKS:
-            round_into_word(2, m0, m1)
+        for t in range(PACK - 1):
+            width = 2 if t == PACK - 2 else 1
+            for m0, m1 in PAGE_CHUNKS:
+                dst = grouped[m0][:, :, t : t + width]
+                src = page[t][:, m0:m1].unsqueeze(2).to_broadcast([P, m1 - m0, width])
+                if m1 == T2:
+                    nc.gpsimd.tensor_scalar(dst, src, 1.0, 0.0, MULT, ADD)
+                else:
+                    nc.scalar.copy(out=dst, in_=src)
         page_codes = held("page_codes", [P, T2], U32)
         page_s = held("page_s", [P, T2], U8)
         w4_codes = {}
@@ -340,12 +334,12 @@ def tile_list_lattice_boltzmann_step_kernel(
             quantize(page_codes[:, m0:m1], page_s[:, m0:m1], grouped[m0][:])
 
         quantize_w4(0, 256, 112)
-        for chunk in PAGE_CHUNKS[:2]:
-            place_last(*chunk)
+        place_last(*PAGE_CHUNKS[0])
+        quantize_w4(256, 512, 113)
         quantize_page(*PAGE_CHUNKS[0])
-        quantize_w4(256, 512, 176)
+        place_last(*PAGE_CHUNKS[1])
+        quantize_w4(512, 1024, 114)
         quantize_page(*PAGE_CHUNKS[1])
-        quantize_w4(512, 1024, 178)
         place_last(*PAGE_CHUNKS[2])
         for c in range(2, len(PAGE_CHUNKS) - 1):
             place_last(*PAGE_CHUNKS[c + 1])
@@ -371,12 +365,6 @@ def tile_list_lattice_boltzmann_step_kernel(
             last_product(acc[:, 0:NARROW], n, m0, m0 + NARROW)
             engine_copy(out=staged[n // 2][:, n % 2, m0 : m0 + NARROW], in_=acc[:, 0:NARROW])
 
-        def pair_bank(u, m0, engine_copy):
-            acc = fresh_bank()
-            for e in range(2):
-                last_product(acc[:, e * NARROW : (e + 1) * NARROW], 2 * u + e, m0, m0 + NARROW)
-            engine_copy(out=staged[u][:, :, m0 : m0 + NARROW], in_=acc[:].rearrange("p (e m) -> p e m", e=2))
-
         def full_bank(n, m0, engine_copy):
             acc = fresh_bank()
             last_product(acc[:], n, m0, m0 + BANK)
@@ -393,16 +381,20 @@ def tile_list_lattice_boltzmann_step_kernel(
         for n in high:
             full_bank(n, 0, on_scalar)
             store(n, 0, BANK)
-        for u in range(len(low) // 2):
-            pair_bank(u, NARROW, on_scalar)
-            for n in (2 * u, 2 * u + 1):
-                full_bank(n, BANK, on_scalar)
+        for n in low:
+            half_bank(n, NARROW, on_scalar)
+            full_bank(n, BANK, on_scalar)
+            if n in low[:2]:
                 store(n, NARROW, 2 * BANK)
+            else:
+                for m0 in (2 * BANK, 3 * BANK):
+                    full_bank(n, m0, on_vector)
+                store(n, NARROW, T2)
         for n in high:
             for c, m0 in enumerate(range(BANK, T2, BANK)):
                 full_bank(n, m0, on_vector if (n + c) % 2 == 0 else on_scalar)
             store(n, BANK, T2)
-        for n in low:
+        for n in low[:2]:
             full_bank(n, 2 * BANK, on_scalar)
             full_bank(n, 3 * BANK, on_vector)
             store(n, 2 * BANK, T2)

@@ -93,24 +93,33 @@ def tile_list_lattice_boltzmann_step_kernel(
         weight_rows = held("weight_rows", [P, 2, H // 4], I32)
         planes = held("planes", [P, PASSES, STAGE // 4], I32)
         ident = held("ident", [P, P], F32)
-        for filled in (window2, window1, weight_rows, ident, planes):
+        for filled in (window2, weight_rows, ident, window1, planes):
             nc.vector.memset(filled[:], 0)
         make_identity(nc, ident[:], nomemset=True)
 
+        def load_w3(a):
+            raw = held("w3_raw%d" % a, [P, H], I32)
+            nc.sync.dma_start(out=raw[:], in_=w3_words[a].rearrange("p c i -> p (c i)").bitcast(I32))
+            return raw
+
         list2 = load_list("list2", offs2)
-        w3_raw = held("w3_raw", [P, PASSES, H], I32)
-        nc.sync.dma_start(out=w3_raw[:], in_=w3_words.rearrange("a p c i -> p a (c i)").bitcast(I32))
         list1 = load_list("list1", offs)
+        w3_raw = [load_w3(0)]
         wg2_rows = held("wg2_rows", [P, LEAD], F32)
         nc.sync.dma_start(out=wg2_rows[:], in_=wg2[:, 0:LEAD])
         load_spread(window2[0:P:4, :], tab2_scales)
-        load_spread(window1[0:P:4, :], tab_scales)
         load_spread(weight_rows[0:P:4, 0, :], w3_scales)
         load_spread(weight_rows[0:P:4, 1, :], w2_scales)
-        tab2_sb = [load_words("tab2_%d" % a, tab2_words, a, 16 * a) for a in range(PASSES)]
-        list4 = load_list("list4", offs4)
         wall_cols = held("wall_cols", [P, PACK], F32)
         nc.sync.dma_start(out=wall_cols[:], in_=wall.rearrange("(p t) -> p t", t=PACK))
+        tab2_sb = [placed("tab2_0", [P, T], I32, 0)]
+        first_pass = tab2_words[0].rearrange("p t i -> p (t i)").bitcast(I32)
+        nc.sync.dma_start(out=tab2_sb[0][:, 0 : T // 4], in_=first_pass[:, 0 : T // 4])
+        load_spread(window1[0:P:4, :], tab_scales)
+        nc.sync.dma_start(out=tab2_sb[0][:, T // 4 : T], in_=first_pass[:, T // 4 : T])
+        tab2_sb.append(load_words("tab2_1", tab2_words, 1, 16))
+        w3_raw.append(load_w3(1))
+        list4 = load_list("list4", offs4)
         list3 = load_list("list3", offs3)
 
         def stage_scales(name, picked, window, offsets, weight):
@@ -131,10 +140,14 @@ def tile_list_lattice_boltzmann_step_kernel(
 
         scales = [planes[:, a, :].bitcast(U8) for a in range(PASSES)]
         w3_sb = placed("w3_sb", [P, PASSES, H], U32, Y + 4)
-        nc.scalar.copy(
-            out=w3_sb[:].rearrange("p a (t c i) -> p a c t i", t=PACK, i=4),
-            in_=w3_raw[:].bitcast(U32).rearrange("p a (c i t) -> p a c t i", t=PACK, i=4),
-        )
+
+        def sort_w3(a, t0, t1):
+            nc.scalar.copy(
+                out=w3_sb[:, a, t0 * P : t1 * P].rearrange("p (t c i) -> p c t i", t=t1 - t0, i=4),
+                in_=w3_raw[a][:].bitcast(U32).rearrange("p (c i t) -> p c t i", t=PACK, i=4)[:, :, t0:t1, :],
+            )
+
+        sort_w3(0, 0, PACK)
         move_scales(stage_scales("stage2", held("picked2", [P, S], U8), window2, list2, 0))
         stage1 = stage_scales("stage1", placed("picked1", [P, S], U8, X + 22), window1, list1, 1)
 
@@ -172,7 +185,9 @@ def tile_list_lattice_boltzmann_step_kernel(
                 out=wg2_lead[:, 2 * u : 2 * u + 2, :], in_=acc[:].rearrange("p (e j) -> p e j", e=2)
             )
 
-        v2 = [placed("v2_%d" % a, [P, S], U32, Y + 16 * a) for a in range(PASSES)]
+        sort_w3(1, 0, 1)
+        sort_w3(1, 1, PACK)
+        v2 = [placed("v2_%d" % a, [P, S], U32, Y + 19 * a) for a in range(PASSES)]
         gather_words(v2[0][:], tab2_sb[0], list2, 0, S)
         gather_words(v2[1][:, 0:LEAD], tab2_sb[1], list2, 0, LEAD)
         gather_words(v2[1][:, LEAD:S], tab2_sb[1], list2, LEAD, S)
@@ -226,7 +241,7 @@ def tile_list_lattice_boltzmann_step_kernel(
             scatter_weighted(t, list4, LEAD, S, h2[t][:, LEAD:S], wg2_front[:, t, :])
 
         tab_sb.append(load_words("tab_1", tab_words, 1, Y + 2))
-        wg2_back = load_dealt("wg2_back", Y + 18, wg2, 2, PACK, LEAD, S)
+        wg2_back = [load_dealt("wg2_back%d" % t, Y + 27 - 3 * t, wg2, t, t + 1, LEAD, S) for t in range(2, PACK)]
         move_scales(stage1)
         w2_raw = placed("w2_raw", [P, PASSES, H // 2], I32, Y)
         nc.sync.dma_start(out=w2_raw[:], in_=w2_words.bitcast(I32).rearrange("a p c -> p a c"))
@@ -259,7 +274,7 @@ def tile_list_lattice_boltzmann_step_kernel(
             gather_words(v1[1][:, j0 : j0 + BANK], tab_sb[1], list1, j0, j0 + BANK)
         for t in range(2, PACK):
             weighted = placed("weighted%d" % t, [P, REST], F32, X + 3 * (t - 2))
-            nc.gpsimd.tensor_tensor(weighted[:], h2[t][:, LEAD:S], wg2_back[:, t - 2, :], MULT)
+            nc.gpsimd.tensor_tensor(weighted[:], h2[t][:, LEAD:S], wg2_back[t - 2][:, 0, :], MULT)
             scatter(t, list4, LEAD, S, weighted[:])
 
         w2_bytes = w2_sb[:].bitcast(U8)
@@ -390,11 +405,12 @@ def tile_list_lattice_boltzmann_step_kernel(
                 for m0 in (2 * BANK, 3 * BANK):
                     full_bank(n, m0, on_vector)
                 store(n, NARROW, T2)
-        for n in high:
-            for c, m0 in enumerate(range(BANK, T2, BANK)):
-                full_bank(n, m0, on_vector if (n + c) % 2 == 0 else on_scalar)
-            store(n, BANK, T2)
+        for u in (2, 3):
+            for n in (2 * u, 2 * u + 1):
+                for c, m0 in enumerate(range(BANK, T2, BANK)):
+                    full_bank(n, m0, on_vector if (n + c) % 2 == 0 else on_scalar)
+            nc.sync.dma_start(out=out_rows[u][:, :, BANK:T2], in_=staged[u][:, :, BANK:T2])
         for n in low[:2]:
             full_bank(n, 2 * BANK, on_scalar)
             full_bank(n, 3 * BANK, on_vector)
-            store(n, 2 * BANK, T2)
+        nc.sync.dma_start(out=out_rows[0][:, :, 2 * BANK : T2], in_=staged[0][:, :, 2 * BANK : T2])

@@ -246,7 +246,7 @@ def tile_list_lattice_boltzmann_step_kernel(
         w2_raw = placed("w2_raw", [P, PASSES, H // 2], I32, Y)
         nc.sync.dma_start(out=w2_raw[:], in_=w2_words.bitcast(I32).rearrange("a p c -> p a c"))
 
-        w1_grouped = [placed("w1_grouped%d" % a, [P, H, PACK], BF16, 166 + 8 * a) for a in range(PASSES)]
+        w1_grouped = [placed("w1_grouped%d" % a, [P, H, PACK], BF16, 166 + 11 * a) for a in range(PASSES)]
         for a in range(PASSES):
             nc.scalar.copy(
                 out=w1_grouped[a][:].rearrange("p (t m) i -> p m t i", t=PACK),
@@ -264,7 +264,7 @@ def tile_list_lattice_boltzmann_step_kernel(
         for a in range(PASSES):
             quantize(w1_codes[:, a, :], w1s[:, a, :], w1_grouped[a][:])
         wg1_sb = [load_dealt("wg1_0", 160, wg1, 0, 2, 0, S)]
-        w4_raw = placed("w4_raw", [P, PACK, N], F32, 176)
+        w4_raw = placed("w4_raw", [P, PACK, N], F32, 179)
         nc.sync.dma_start(out=w4_raw[:], in_=w4.rearrange("(p t) n -> p t n", t=PACK))
         wg1_sb.append(load_dealt("wg1_1", 168, wg1, 2, PACK, 0, S))
 
@@ -273,7 +273,7 @@ def tile_list_lattice_boltzmann_step_kernel(
         for j0 in range(0, S, BANK):
             gather_words(v1[1][:, j0 : j0 + BANK], tab_sb[1], list1, j0, j0 + BANK)
         for t in range(2, PACK):
-            weighted = placed("weighted%d" % t, [P, REST], F32, X + 3 * (t - 2))
+            weighted = placed("weighted%d" % t, [P, REST], F32, (176, X)[t - 2])
             nc.gpsimd.tensor_tensor(weighted[:], h2[t][:, LEAD:S], wg2_back[t - 2][:, 0, :], MULT)
             scatter(t, list4, LEAD, S, weighted[:])
 
@@ -318,7 +318,7 @@ def tile_list_lattice_boltzmann_step_kernel(
             interleave(nc.scalar.copy, w4_grouped[u][:], w4_raw[:, :, u * BANK : (u + 1) * BANK])
 
         grouped = {
-            m0: placed("page_grouped%d" % m0, [P, m1 - m0, PACK], BF16, (176 if m1 < T2 else 160) + m0 // 128) for m0, m1 in PAGE_CHUNKS
+            m0: placed("page_grouped%d" % m0, [P, m1 - m0, PACK], BF16, (179 if m1 < T2 else 160) + m0 // 128) for m0, m1 in PAGE_CHUNKS
         }
 
         for t in range(PACK - 1):

@@ -93,33 +93,24 @@ def tile_list_lattice_boltzmann_step_kernel(
         weight_rows = held("weight_rows", [P, 2, H // 4], I32)
         planes = held("planes", [P, PASSES, STAGE // 4], I32)
         ident = held("ident", [P, P], F32)
-        for filled in (window2, weight_rows, ident, window1, planes):
+        for filled in (window2, window1, weight_rows, ident, planes):
             nc.vector.memset(filled[:], 0)
         make_identity(nc, ident[:], nomemset=True)
 
-        def load_w3(a):
-            raw = held("w3_raw%d" % a, [P, H], I32)
-            nc.sync.dma_start(out=raw[:], in_=w3_words[a].rearrange("p c i -> p (c i)").bitcast(I32))
-            return raw
-
         list2 = load_list("list2", offs2)
+        w3_raw = held("w3_raw", [P, PASSES, H], I32)
+        nc.sync.dma_start(out=w3_raw[:], in_=w3_words.rearrange("a p c i -> p a (c i)").bitcast(I32))
         list1 = load_list("list1", offs)
-        w3_raw = [load_w3(0)]
         wg2_rows = held("wg2_rows", [P, LEAD], F32)
         nc.sync.dma_start(out=wg2_rows[:], in_=wg2[:, 0:LEAD])
         load_spread(window2[0:P:4, :], tab2_scales)
+        load_spread(window1[0:P:4, :], tab_scales)
         load_spread(weight_rows[0:P:4, 0, :], w3_scales)
         load_spread(weight_rows[0:P:4, 1, :], w2_scales)
+        tab2_sb = [load_words("tab2_%d" % a, tab2_words, a, 16 * a) for a in range(PASSES)]
+        list4 = load_list("list4", offs4)
         wall_cols = held("wall_cols", [P, PACK], F32)
         nc.sync.dma_start(out=wall_cols[:], in_=wall.rearrange("(p t) -> p t", t=PACK))
-        tab2_sb = [placed("tab2_0", [P, T], I32, 0)]
-        first_pass = tab2_words[0].rearrange("p t i -> p (t i)").bitcast(I32)
-        nc.sync.dma_start(out=tab2_sb[0][:, 0 : T // 4], in_=first_pass[:, 0 : T // 4])
-        load_spread(window1[0:P:4, :], tab_scales)
-        nc.sync.dma_start(out=tab2_sb[0][:, T // 4 : T], in_=first_pass[:, T // 4 : T])
-        tab2_sb.append(load_words("tab2_1", tab2_words, 1, 16))
-        w3_raw.append(load_w3(1))
-        list4 = load_list("list4", offs4)
         list3 = load_list("list3", offs3)
 
         def stage_scales(name, picked, window, offsets, weight):
@@ -140,14 +131,10 @@ def tile_list_lattice_boltzmann_step_kernel(
 
         scales = [planes[:, a, :].bitcast(U8) for a in range(PASSES)]
         w3_sb = placed("w3_sb", [P, PASSES, H], U32, Y + 4)
-
-        def sort_w3(a, t0, t1):
-            nc.scalar.copy(
-                out=w3_sb[:, a, t0 * P : t1 * P].rearrange("p (t c i) -> p c t i", t=t1 - t0, i=4),
-                in_=w3_raw[a][:].bitcast(U32).rearrange("p (c i t) -> p c t i", t=PACK, i=4)[:, :, t0:t1, :],
-            )
-
-        sort_w3(0, 0, PACK)
+        nc.scalar.copy(
+            out=w3_sb[:].rearrange("p a (t c i) -> p a c t i", t=PACK, i=4),
+            in_=w3_raw[:].bitcast(U32).rearrange("p a (c i t) -> p a c t i", t=PACK, i=4),
+        )
         move_scales(stage_scales("stage2", held("picked2", [P, S], U8), window2, list2, 0))
         stage1 = stage_scales("stage1", placed("picked1", [P, S], U8, X + 22), window1, list1, 1)
 
@@ -185,8 +172,6 @@ def tile_list_lattice_boltzmann_step_kernel(
                 out=wg2_lead[:, 2 * u : 2 * u + 2, :], in_=acc[:].rearrange("p (e j) -> p e j", e=2)
             )
 
-        sort_w3(1, 0, 1)
-        sort_w3(1, 1, PACK)
         v2 = [placed("v2_%d" % a, [P, S], U32, Y + 19 * a) for a in range(PASSES)]
         gather_words(v2[0][:], tab2_sb[0], list2, 0, S)
         gather_words(v2[1][:, 0:LEAD], tab2_sb[1], list2, 0, LEAD)

@@ -116,26 +116,30 @@ def tile_list_lattice_boltzmann_step_kernel(
         def stage_scales(name, picked, window, offsets, weight):
             nc.vector.tensor_copy(picked[:], window[:].bitcast(U8).indirect(offsets[:]))
             stage = held(name, [P, STAGE], U8)
-            nc.vector.tensor_copy(out=stage[:, 0:S].bitcast(I32), in_=picked[:].bitcast(I32))
+            nc.vector.tensor_copy(out=stage[:, H:STAGE].bitcast(I32), in_=picked[:].bitcast(I32))
             nc.vector.tensor_copy(
-                out=stage[:, S:STAGE].rearrange("p (t m) -> p t m", t=PACK),
+                out=stage[:, 0:H].rearrange("p (t m) -> p t m", t=PACK),
                 in_=weight_rows[:, weight, :].bitcast(U8).rearrange("p (m t) -> p t m", t=PACK),
             )
             return stage
 
-        def move_scales(stage):
+        def move_scales(stage, c0, c1):
             for q in QUADRANTS:
                 nc.sync.dma_start(
-                    out=planes[32 * q : 32 * q + 4], in_=stage[32 * q : 32 * q + 32 : 4, :].bitcast(I32)
+                    out=planes[32 * q : 32 * q + 4, :, c0 // 4 : c1 // 4],
+                    in_=stage[32 * q : 32 * q + 32 : 4, c0:c1].bitcast(I32),
                 )
 
-        scales = [planes[:, a, :].bitcast(U8) for a in range(PASSES)]
+        weight_scales = [planes[:, a, 0 : H // 4].bitcast(U8) for a in range(PASSES)]
+        scales = [planes[:, a, H // 4 : STAGE // 4].bitcast(U8) for a in range(PASSES)]
         w3_sb = placed("w3_sb", [P, PASSES, H], U32, Y + 4)
         nc.scalar.copy(
             out=w3_sb[:].rearrange("p a (t c i) -> p a c t i", t=PACK, i=4),
             in_=w3_raw[:].bitcast(U32).rearrange("p a (c i t) -> p a c t i", t=PACK, i=4),
         )
-        move_scales(stage_scales("stage2", held("picked2", [P, S], U8), window2, list2, 0))
+        stage2 = stage_scales("stage2", held("picked2", [P, S], U8), window2, list2, 0)
+        move_scales(stage2, 0, H + LEAD)
+        move_scales(stage2, H + LEAD, STAGE)
         stage1 = stage_scales("stage1", placed("picked1", [P, S], U8, X + 22), window1, list1, 1)
 
         wg2_front = load_dealt("wg2_front", X, wg2, 0, 2, LEAD, S)
@@ -185,12 +189,12 @@ def tile_list_lattice_boltzmann_step_kernel(
             used.append(len(used))
             return bank(used[-1])
 
-        def product(acc, weights, weight_scales, values, value_scales, j0, j1):
+        def product(acc, weights, weight_planes, values, value_scales, j0, j1):
             for a in range(PASSES):
                 nc.tensor.matmul_mx(
                     out=acc,
                     lhsT=weights[a],
-                    lhsT_scale=weight_scales[a],
+                    lhsT_scale=weight_planes[a],
                     rhs=values[a][:, j0:j1].bitcast(FP8X4),
                     rhs_scale=value_scales[a][:, j0:j1],
                     start=(a == 0),
@@ -202,7 +206,7 @@ def tile_list_lattice_boltzmann_step_kernel(
             product(
                 acc,
                 [w3_sb[:, a, t * P : (t + 1) * P].bitcast(FP8X4) for a in range(PASSES)],
-                [scales[a][:, S + t * P : S + (t + 1) * P] for a in range(PASSES)],
+                [weight_scales[a][:, t * P : (t + 1) * P] for a in range(PASSES)],
                 v2, scales, j0, j1,
             )
             nc.scalar.activation(h2[t][:, j0:j1], acc, IDENTITY, bias=wall_cols[:, t : t + 1], scale=-1.0)
@@ -227,7 +231,7 @@ def tile_list_lattice_boltzmann_step_kernel(
 
         tab_sb.append(load_words("tab_1", tab_words, 1, Y + 2))
         wg2_back = [load_dealt("wg2_back%d" % t, Y + 27 - 3 * t, wg2, t, t + 1, LEAD, S) for t in range(2, PACK)]
-        move_scales(stage1)
+        move_scales(stage1, 0, STAGE)
         w2_raw = placed("w2_raw", [P, PASSES, H // 2], I32, Y)
         nc.sync.dma_start(out=w2_raw[:], in_=w2_words.bitcast(I32).rearrange("a p c -> p a c"))
 
@@ -278,7 +282,7 @@ def tile_list_lattice_boltzmann_step_kernel(
                 acc = bank((step + 1) % 3)
                 product(
                     acc[:], [w2_bytes[:, a, 2 * t * P : 2 * (t + 1) * P].bitcast(FP4X4) for a in range(PASSES)],
-                    [scales[a][:, S + t * P : S + (t + 1) * P] for a in range(PASSES)], v1, scales, j0, j0 + BANK,
+                    [weight_scales[a][:, t * P : (t + 1) * P] for a in range(PASSES)], v1, scales, j0, j0 + BANK,
                 )
                 nc.scalar.activation(relaxed[t][:, j0 : j0 + BANK], acc[:], COPY, scale=rate_cols[:, t : t + 1])
 

@@ -113,12 +113,13 @@ def tile_list_lattice_boltzmann_step_kernel(
         nc.sync.dma_start(out=wall_cols[:], in_=wall.rearrange("(p t) -> p t", t=PACK))
         list3 = load_list("list3", offs3)
 
-        def stage_scales(name, picked, window, offsets, weight):
+        def stage_scales(name, picked, window, offsets, weight, split):
             nc.vector.tensor_copy(picked[:], window[:].bitcast(U8).indirect(offsets[:]))
             stage = held(name, [P, STAGE], U8)
-            nc.vector.tensor_copy(out=stage[:, H:STAGE].bitcast(I32), in_=picked[:].bitcast(I32))
+            nc.vector.tensor_copy(out=stage[:, 0:split].bitcast(I32), in_=picked[:, 0:split].bitcast(I32))
+            nc.vector.tensor_copy(out=stage[:, split + H : STAGE].bitcast(I32), in_=picked[:, split:S].bitcast(I32))
             nc.vector.tensor_copy(
-                out=stage[:, 0:H].rearrange("p (t m) -> p t m", t=PACK),
+                out=stage[:, split : split + H].rearrange("p (t m) -> p t m", t=PACK),
                 in_=weight_rows[:, weight, :].bitcast(U8).rearrange("p (m t) -> p t m", t=PACK),
             )
             return stage
@@ -130,17 +131,16 @@ def tile_list_lattice_boltzmann_step_kernel(
                     in_=stage[32 * q : 32 * q + 32 : 4, c0:c1].bitcast(I32),
                 )
 
-        weight_scales = [planes[:, a, 0 : H // 4].bitcast(U8) for a in range(PASSES)]
-        scales = [planes[:, a, H // 4 : STAGE // 4].bitcast(U8) for a in range(PASSES)]
+        plane_bytes = [planes[:, a, :].bitcast(U8) for a in range(PASSES)]
         w3_sb = placed("w3_sb", [P, PASSES, H], U32, Y + 4)
         nc.scalar.copy(
             out=w3_sb[:].rearrange("p a (t c i) -> p a c t i", t=PACK, i=4),
             in_=w3_raw[:].bitcast(U32).rearrange("p a (c i t) -> p a c t i", t=PACK, i=4),
         )
-        stage2 = stage_scales("stage2", held("picked2", [P, S], U8), window2, list2, 0)
-        move_scales(stage2, 0, H + LEAD)
-        move_scales(stage2, H + LEAD, STAGE)
-        stage1 = stage_scales("stage1", placed("picked1", [P, S], U8, X + 22), window1, list1, 1)
+        stage2 = stage_scales("stage2", held("picked2", [P, S], U8), window2, list2, 0, LEAD)
+        move_scales(stage2, 0, LEAD + P)
+        move_scales(stage2, LEAD + P, STAGE)
+        stage1 = stage_scales("stage1", placed("picked1", [P, S], U8, X + 22), window1, list1, 1, BANK)
 
         wg2_front = load_dealt("wg2_front", X, wg2, 0, 2, LEAD, S)
         rate_cols = placed("rate_cols", [P, PACK], F32, X + 6)
@@ -189,14 +189,14 @@ def tile_list_lattice_boltzmann_step_kernel(
             used.append(len(used))
             return bank(used[-1])
 
-        def product(acc, weights, weight_planes, values, value_scales, j0, j1):
+        def product(acc, weights, weight_planes, values, value_scales, split, j0, j1):
             for a in range(PASSES):
                 nc.tensor.matmul_mx(
                     out=acc,
                     lhsT=weights[a],
                     lhsT_scale=weight_planes[a],
                     rhs=values[a][:, j0:j1].bitcast(FP8X4),
-                    rhs_scale=value_scales[a][:, j0:j1],
+                    rhs_scale=value_scales[a][:, (H if j0 >= split else 0) + j0 : (H if j0 >= split else 0) + j1],
                     start=(a == 0),
                     stop=(a == PASSES - 1),
                 )
@@ -206,8 +206,8 @@ def tile_list_lattice_boltzmann_step_kernel(
             product(
                 acc,
                 [w3_sb[:, a, t * P : (t + 1) * P].bitcast(FP8X4) for a in range(PASSES)],
-                [weight_scales[a][:, t * P : (t + 1) * P] for a in range(PASSES)],
-                v2, scales, j0, j1,
+                [plane_bytes[a][:, LEAD + t * P : LEAD + (t + 1) * P] for a in range(PASSES)],
+                v2, plane_bytes, LEAD, j0, j1,
             )
             nc.scalar.activation(h2[t][:, j0:j1], acc, IDENTITY, bias=wall_cols[:, t : t + 1], scale=-1.0)
 
@@ -276,13 +276,14 @@ def tile_list_lattice_boltzmann_step_kernel(
                 acc = bank(step % 3)
                 product(
                     acc[:], [w1_codes[:, a, rows].bitcast(FP8X4) for a in range(PASSES)],
-                    [w1s[:, a, rows] for a in range(PASSES)], v1, scales, j0, j0 + BANK,
+                    [w1s[:, a, rows] for a in range(PASSES)], v1, plane_bytes, BANK, j0, j0 + BANK,
                 )
                 nc.scalar.activation(kept[t][:, j0 : j0 + BANK], acc[:], COPY, scale=kept_cols[:, t : t + 1])
                 acc = bank((step + 1) % 3)
                 product(
                     acc[:], [w2_bytes[:, a, 2 * t * P : 2 * (t + 1) * P].bitcast(FP4X4) for a in range(PASSES)],
-                    [weight_scales[a][:, t * P : (t + 1) * P] for a in range(PASSES)], v1, scales, j0, j0 + BANK,
+                    [plane_bytes[a][:, BANK + t * P : BANK + (t + 1) * P] for a in range(PASSES)],
+                    v1, plane_bytes, BANK, j0, j0 + BANK,
                 )
                 nc.scalar.activation(relaxed[t][:, j0 : j0 + BANK], acc[:], COPY, scale=rate_cols[:, t : t + 1])
 
@@ -337,6 +338,7 @@ def tile_list_lattice_boltzmann_step_kernel(
         def quantize_page(m0, m1):
             quantize(page_codes[:, m0:m1], page_s[:, m0:m1], grouped[m0][:])
 
+        nc.scalar.copy(out=grouped[BANK][:, :, PACK - 1], in_=page[PACK - 1][:, BANK : 2 * BANK])
         quantize_w4(0, 256, 112)
         place_last(*PAGE_CHUNKS[0])
         quantize_w4(256, 512, 113)
@@ -344,11 +346,11 @@ def tile_list_lattice_boltzmann_step_kernel(
         place_last(*PAGE_CHUNKS[1])
         quantize_w4(512, 1024, 114)
         quantize_page(*PAGE_CHUNKS[1])
-        place_last(*PAGE_CHUNKS[2])
-        for c in range(2, len(PAGE_CHUNKS) - 1):
-            place_last(*PAGE_CHUNKS[c + 1])
-            quantize_page(*PAGE_CHUNKS[c])
-        quantize_page(*PAGE_CHUNKS[-1])
+        quantize_page(*PAGE_CHUNKS[2])
+        for chunk in PAGE_CHUNKS[3:]:
+            place_last(*chunk)
+        for chunk in PAGE_CHUNKS[3:]:
+            quantize_page(*chunk)
 
         staged = [placed("staged%d" % u, [P, 2, T2], F32, (128, 144, X + 6.25, Y + 2)[u]) for u in range(4)]
         out_rows = out.rearrange("(u e p) m -> u p e m", e=2, p=P)
@@ -383,12 +385,16 @@ def tile_list_lattice_boltzmann_step_kernel(
             half_bank(n, 0, on_scalar)
             store(n, 0, NARROW)
         for n in high:
-            full_bank(n, 0, on_scalar)
+            acc = fresh_bank()
+            step = NARROW if n == high[0] else BANK
+            for m0 in range(0, BANK, step):
+                last_product(acc[:, m0 : m0 + step], n, m0, m0 + step)
+            on_scalar(out=staged[n // 2][:, n % 2, 0:BANK], in_=acc[:])
             store(n, 0, BANK)
         for n in low:
             half_bank(n, NARROW, on_scalar)
             full_bank(n, BANK, on_scalar)
-            if n in low[:2]:
+            if n == low[0]:
                 store(n, NARROW, 2 * BANK)
             else:
                 for m0 in (2 * BANK, 3 * BANK):
@@ -399,7 +405,6 @@ def tile_list_lattice_boltzmann_step_kernel(
                 for c, m0 in enumerate(range(BANK, T2, BANK)):
                     full_bank(n, m0, on_vector if (n + c) % 2 == 0 else on_scalar)
             nc.sync.dma_start(out=out_rows[u][:, :, BANK:T2], in_=staged[u][:, :, BANK:T2])
-        for n in low[:2]:
-            full_bank(n, 2 * BANK, on_scalar)
-            full_bank(n, 3 * BANK, on_vector)
-        nc.sync.dma_start(out=out_rows[0][:, :, 2 * BANK : T2], in_=staged[0][:, :, 2 * BANK : T2])
+        full_bank(low[0], 2 * BANK, on_scalar)
+        full_bank(low[0], 3 * BANK, on_vector)
+        store(low[0], 2 * BANK, T2)

@@ -100,28 +100,26 @@ def tile_list_lattice_boltzmann_step_kernel(
         list2 = load_list("list2", offs2)
         w3_raw = held("w3_raw", [P, PASSES, H], I32)
         nc.sync.dma_start(out=w3_raw[:], in_=w3_words.rearrange("a p c i -> p a (c i)").bitcast(I32))
+        load_spread(window2[0:P:4, :], tab2_scales)
         list1 = load_list("list1", offs)
         wg2_rows = held("wg2_rows", [P, LEAD], F32)
         nc.sync.dma_start(out=wg2_rows[:], in_=wg2[:, 0:LEAD])
-        load_spread(window2[0:P:4, :], tab2_scales)
         load_spread(window1[0:P:4, :], tab_scales)
         load_spread(weight_rows[0:P:4, 0, :], w3_scales)
         load_spread(weight_rows[0:P:4, 1, :], w2_scales)
         tab2_sb = [load_words("tab2_%d" % a, tab2_words, a, 16 * a) for a in range(PASSES)]
         list4 = load_list("list4", offs4)
-        wall_cols = held("wall_cols", [P, PACK], F32)
-        nc.sync.dma_start(out=wall_cols[:], in_=wall.rearrange("(p t) -> p t", t=PACK))
         list3 = load_list("list3", offs3)
 
         def stage_scales(name, picked, window, offsets, weight, split):
             nc.vector.tensor_copy(picked[:], window[:].bitcast(U8).indirect(offsets[:]))
             stage = held(name, [P, STAGE], U8)
-            nc.vector.tensor_copy(out=stage[:, 0:split].bitcast(I32), in_=picked[:, 0:split].bitcast(I32))
-            nc.vector.tensor_copy(out=stage[:, split + H : STAGE].bitcast(I32), in_=picked[:, split:S].bitcast(I32))
             nc.vector.tensor_copy(
                 out=stage[:, split : split + H].rearrange("p (t m) -> p t m", t=PACK),
                 in_=weight_rows[:, weight, :].bitcast(U8).rearrange("p (m t) -> p t m", t=PACK),
             )
+            nc.vector.tensor_copy(out=stage[:, 0:split].bitcast(I32), in_=picked[:, 0:split].bitcast(I32))
+            nc.vector.tensor_copy(out=stage[:, split + H : STAGE].bitcast(I32), in_=picked[:, split:S].bitcast(I32))
             return stage
 
         def move_scales(stage, c0, c1):
@@ -137,9 +135,11 @@ def tile_list_lattice_boltzmann_step_kernel(
             out=w3_sb[:].rearrange("p a (t c i) -> p a c t i", t=PACK, i=4),
             in_=w3_raw[:].bitcast(U32).rearrange("p a (c i t) -> p a c t i", t=PACK, i=4),
         )
-        stage2 = stage_scales("stage2", held("picked2", [P, S], U8), window2, list2, 0, LEAD)
-        move_scales(stage2, 0, LEAD + P)
-        move_scales(stage2, LEAD + P, STAGE)
+        stage2 = stage_scales("stage2", placed("picked2", [P, S], U8, Y - 1.5), window2, list2, 0, LEAD)
+        move_scales(stage2, 0, LEAD + 2 * P)
+        wall_cols = placed("wall_cols", [P, PACK], F32, Y - 1.5)
+        nc.sync.dma_start(out=wall_cols[:], in_=wall.rearrange("(p t) -> p t", t=PACK))
+        move_scales(stage2, LEAD + 2 * P, STAGE)
         stage1 = stage_scales("stage1", placed("picked1", [P, S], U8, X + 22), window1, list1, 1, BANK)
 
         wg2_front = load_dealt("wg2_front", X, wg2, 0, 2, LEAD, S)

@@ -333,12 +333,12 @@ def tile_list_lattice_boltzmann_step_kernel(
             quantize(codes[:], w4s[:, n0:n1], w4_grouped[u][:, n0 - u * BANK : n1 - u * BANK, :])
 
         def place_last(m0, m1):
-            nc.vector.tensor_copy(out=grouped[m0][:, :, PACK - 1], in_=page[PACK - 1][:, m0:m1])
+            nc.vector.tensor_copy(out=grouped[m0][:, 0 : m1 - m0, PACK - 1], in_=page[PACK - 1][:, m0:m1])
 
         def quantize_page(m0, m1):
             quantize(page_codes[:, m0:m1], page_s[:, m0:m1], grouped[m0][:])
 
-        nc.scalar.copy(out=grouped[BANK][:, :, PACK - 1], in_=page[PACK - 1][:, BANK : 2 * BANK])
+        nc.scalar.copy(out=grouped[BANK][:, P:BANK, PACK - 1], in_=page[PACK - 1][:, BANK + P : 2 * BANK])
         quantize_w4(0, 256, 112)
         place_last(*PAGE_CHUNKS[0])
         quantize_w4(256, 512, 113)
@@ -346,11 +346,11 @@ def tile_list_lattice_boltzmann_step_kernel(
         place_last(*PAGE_CHUNKS[1])
         quantize_w4(512, 1024, 114)
         quantize_page(*PAGE_CHUNKS[1])
-        quantize_page(*PAGE_CHUNKS[2])
-        for chunk in PAGE_CHUNKS[3:]:
-            place_last(*chunk)
-        for chunk in PAGE_CHUNKS[3:]:
-            quantize_page(*chunk)
+        place_last(BANK, BANK + P)
+        for c in range(2, len(PAGE_CHUNKS) - 1):
+            place_last(*PAGE_CHUNKS[c + 1])
+            quantize_page(*PAGE_CHUNKS[c])
+        quantize_page(*PAGE_CHUNKS[-1])
 
         staged = [placed("staged%d" % u, [P, 2, T2], F32, (128, 144, X + 6.25, Y + 2)[u]) for u in range(4)]
         out_rows = out.rearrange("(u e p) m -> u p e m", e=2, p=P)
@@ -394,7 +394,7 @@ def tile_list_lattice_boltzmann_step_kernel(
         for n in low:
             half_bank(n, NARROW, on_scalar)
             full_bank(n, BANK, on_scalar)
-            if n == low[0]:
+            if n in low[:2]:
                 store(n, NARROW, 2 * BANK)
             else:
                 for m0 in (2 * BANK, 3 * BANK):
@@ -405,6 +405,7 @@ def tile_list_lattice_boltzmann_step_kernel(
                 for c, m0 in enumerate(range(BANK, T2, BANK)):
                     full_bank(n, m0, on_vector if (n + c) % 2 == 0 else on_scalar)
             nc.sync.dma_start(out=out_rows[u][:, :, BANK:T2], in_=staged[u][:, :, BANK:T2])
-        full_bank(low[0], 2 * BANK, on_scalar)
-        full_bank(low[0], 3 * BANK, on_vector)
-        store(low[0], 2 * BANK, T2)
+        for n in low[:2]:
+            full_bank(n, 2 * BANK, on_scalar)
+            full_bank(n, 3 * BANK, on_vector)
+        nc.sync.dma_start(out=out_rows[0][:, :, 2 * BANK : T2], in_=staged[0][:, :, 2 * BANK : T2])

@@ -25,7 +25,7 @@ PASSES = K // (P * PACK)
 BANK = 512
 KIB = 1024
 QUADRANTS = (0, 2, 1, 3)
-PAGE_CHUNKS = ((0, 256), (256, 512), (512, 1024), (1024, 1536), (1536, 2048))
+PAGE_CHUNKS = ((0, 256), (256, 512), (512, 1024), (1024, 1280), (1280, 2048))
 NARROW = PAGE_CHUNKS[0][1]
 LEAD = 256
 REST = S - LEAD
@@ -336,7 +336,9 @@ def tile_list_lattice_boltzmann_step_kernel(
             nc.vector.tensor_copy(out=grouped[m0][:, 0 : m1 - m0, PACK - 1], in_=page[PACK - 1][:, m0:m1])
 
         def quantize_page(m0, m1):
-            quantize(page_codes[:, m0:m1], page_s[:, m0:m1], grouped[m0][:])
+            cuts = [m0] + list(range((m0 // BANK + 1) * BANK, m1, BANK)) + [m1]
+            for c0, c1 in zip(cuts, cuts[1:]):
+                quantize(page_codes[:, c0:c1], page_s[:, c0:c1], grouped[m0][:, c0 - m0 : c1 - m0, :])
 
         nc.scalar.copy(out=grouped[BANK][:, P:BANK, PACK - 1], in_=page[PACK - 1][:, BANK + P : 2 * BANK])
         quantize_w4(0, 256, 112)

from contextlib import ExitStack

import concourse.mybir as mybir
from concourse.masks import make_identity

K, T, S, H, N, T2 = 1024, 4096, 1024, 512, 1024, 2048
FLOPS = 2 * (3 * K * H * S + H * N * T2)

F32 = mybir.dt.float32
BF16 = mybir.dt.bfloat16
I32 = mybir.dt.int32
U32 = mybir.dt.uint32
U16 = mybir.dt.uint16
U8 = mybir.dt.uint8
FP8X4 = mybir.dt.float8_e4m3fn_x4
FP4X4 = mybir.dt.float4_e2m1fn_x4
MULT = mybir.AluOpType.mult
ADD = mybir.AluOpType.add
COPY = mybir.ActivationFunctionType.Copy
IDENTITY = mybir.ActivationFunctionType.Identity

P = 128
PACK = 4
PASSES = K // (P * PACK)
BANK = 512
KIB = 1024
QUADRANTS = (0, 2, 1, 3)
PAGE_CHUNKS = ((0, 256), (256, 512), (512, 1024), (1024, 1280), (1280, 2048))
NARROW = PAGE_CHUNKS[0][1]
LEAD = 256
REST = S - LEAD
STAGE = S + H


def tile_list_lattice_boltzmann_step_kernel(
    tc, tab_words, tab_scales, tab2_words, tab2_scales, offs, offs2, offs3, offs4, w1,
    w2_words, w2_scales, w3_words, w3_scales, rate, wall, wg1, wg2, w4, out,
):
    nc = tc.nc
    with ExitStack() as ctx:
        lists = ctx.enter_context(tc.tile_pool(name="lists", bufs=1))
        keep = ctx.enter_context(tc.tile_pool(name="keep", bufs=1))
        arena = ctx.enter_context(tc.tile_pool(name="arena", bufs=1))
        psum = ctx.enter_context(tc.psum_pool(name="psum", bufs=1))

        def held(name, shape, dtype):
            return keep.tile(shape, dtype, name=name, align_bytes=64)

        def placed(name, shape, dtype, kib):
            return arena.tile(shape, dtype, name=name, offset=int(kib * KIB), align_bytes=64)

        def bank(i):
            return psum.tile([P, BANK], F32, name="bank%d" % (i % 8))

        def load_list(name, src):
            dst = lists.tile([P, S // 16], U16, name=name)
            nc.sync.dma_start(dst[:], src)
            return dst

        def load_words(name, words, a, kib):
            dst = placed(name, [P, T], I32, kib)
            nc.sync.dma_start(out=dst[:], in_=words[a].rearrange("p t i -> p (t i)").bitcast(I32))
            return dst

        def load_spread(dst, scales):
            nc.sync.dma_start(out=dst, in_=scales.bitcast(I32).rearrange("a q t -> q a t"))

        def load_dealt(name, kib, weights, t0, t1, j0, j1):
            dst = placed(name, [P, t1 - t0, j1 - j0], F32, kib)
            rows = weights.rearrange("(p t) j -> p t j", t=PACK)
            for q in QUADRANTS:
                nc.sync.dma_start(out=dst[32 * q : 32 * q + 32], in_=rows[:, t0:t1, j0:j1])
            return dst

        def gather_words(dst, window, offsets, j0, j1):
            nc.vector.tensor_copy(dst, window[:].bitcast(U32).indirect(offsets[:, j0 // 16 : j1 // 16]))

        def interleave(engine_copy, dst, src):
            engine_copy(
                out=dst.rearrange("p (c i) t -> p c t i", i=4),
                in_=src.rearrange("p t (c i) -> p c t i", i=4),
            )

        def quantize(codes, scales, grouped):
            nc.vector.quantize_mx(
                out=codes.bitcast(FP8X4), scales=scales, in_=grouped.rearrange("p c t -> p (c t)")
            )

        X, Y, Z = 32, 72, 96

        window2 = placed("window2", [P, T // 4], I32, Y + 11)
        window1 = placed("window1", [P, T // 4], I32, X + 4)
        weight_rows = held("weight_rows", [P, 2, H // 4], I32)
        planes = held("planes", [P, PASSES, STAGE // 4], I32)
        ident = held("ident", [P, P], F32)
        for filled in (window2, window1, weight_rows, ident, planes):
            nc.vector.memset(filled[:], 0)
        make_identity(nc, ident[:], nomemset=True)

        list2 = load_list("list2", offs2)
        w3_raw = held("w3_raw", [P, PASSES, H], I32)
        nc.sync.dma_start(out=w3_raw[:], in_=w3_words.rearrange("a p c i -> p a (c i)").bitcast(I32))
        load_spread(window2[0:P:4, :], tab2_scales)
        list1 = load_list("list1", offs)
        wg2_rows = held("wg2_rows", [P, LEAD], F32)
        nc.sync.dma_start(out=wg2_rows[:], in_=wg2[:, 0:LEAD])
        load_spread(window1[0:P:4, :], tab_scales)
        load_spread(weight_rows[0:P:4, 0, :], w3_scales)
        load_spread(weight_rows[0:P:4, 1, :], w2_scales)
        tab2_sb = [load_words("tab2_%d" % a, tab2_words, a, 16 * a) for a in range(PASSES)]
        list4 = load_list("list4", offs4)
        list3 = load_list("list3", offs3)

        def stage_scales(name, picked, window, offsets, weight, split):
            nc.vector.tensor_copy(picked[:], window[:].bitcast(U8).indirect(offsets[:]))
            stage = held(name, [P, STAGE], U8)
            nc.vector.tensor_copy(
                out=stage[:, split : split + H].rearrange("p (t m) -> p t m", t=PACK),
                in_=weight_rows[:, weight, :].bitcast(U8).rearrange("p (m t) -> p t m", t=PACK),
            )
            nc.vector.tensor_copy(out=stage[:, 0:split].bitcast(I32), in_=picked[:, 0:split].bitcast(I32))
            nc.vector.tensor_copy(out=stage[:, split + H : STAGE].bitcast(I32), in_=picked[:, split:S].bitcast(I32))
            return stage

        def move_scales(stage, c0, c1):
            for q in QUADRANTS:
                nc.sync.dma_start(
                    out=planes[32 * q : 32 * q + 4, :, c0 // 4 : c1 // 4],
                    in_=stage[32 * q : 32 * q + 32 : 4, c0:c1].bitcast(I32),
                )

        plane_bytes = [planes[:, a, :].bitcast(U8) for a in range(PASSES)]
        w3_sb = placed("w3_sb", [P, PASSES, H], U32, Y + 4)
        nc.scalar.copy(
            out=w3_sb[:].rearrange("p a (t c i) -> p a c t i", t=PACK, i=4),
            in_=w3_raw[:].bitcast(U32).rearrange("p a (c i t) -> p a c t i", t=PACK, i=4),
        )
        stage2 = stage_scales("stage2", placed("picked2", [P, S], U8, Y - 1.5), window2, list2, 0, LEAD)
        move_scales(stage2, 0, LEAD + 2 * P)
        wall_cols = placed("wall_cols", [P, PACK], F32, Y - 1.5)
        nc.sync.dma_start(out=wall_cols[:], in_=wall.rearrange("(p t) -> p t", t=PACK))
        move_scales(stage2, LEAD + 2 * P, STAGE)
        stage1 = stage_scales("stage1", placed("picked1", [P, S], U8, X + 22), window1, list1, 1, BANK)

        wg2_front = load_dealt("wg2_front", X, wg2, 0, 2, LEAD, S)
        rate_cols = placed("rate_cols", [P, PACK], F32, X + 6)
        nc.sync.dma_start(out=rate_cols[:], in_=rate.rearrange("(p t) -> p t", t=PACK))
        w1_raw = placed("w1_raw", [P, PASSES, PACK, H], F32, X + 6.25)
        for a in range(PASSES):
            nc.sync.dma_start(
                out=w1_raw[:, a], in_=w1[512 * a : 512 * (a + 1), :].rearrange("(p t) c -> p t c", t=PACK)
            )
        tab_sb = [load_words("tab_0", tab_words, 0, X + 22.25)]

        wg2_lead = held("wg2_lead", [P, PACK, LEAD], F32)
        acc = bank(4)
        turned = []
        for b in range(LEAD // P):
            nc.tensor.transpose(acc[:, b * P : (b + 1) * P], wg2_rows[:, b * P : (b + 1) * P], ident[:])
        for b in range(LEAD // P):
            sorted_rows = held("wg2_turned%d" % b, [P, PACK, 4, 32], F32)
            rows = acc[:, b * P : (b + 1) * P].rearrange("p (m u e) -> p u m e", u=2, e=2)
            nc.scalar.copy(
                out=sorted_rows[:].rearrange("p (u e) q m -> p u q m e", e=2),
                in_=rows.unsqueeze(2).to_broadcast([P, 2, 4, 32, 2]),
            )
            turned.append(sorted_rows)
        for u in range(2):
            acc = bank(5 + u)
            for e in range(2):
                for b in range(LEAD // P):
                    j0 = e * LEAD + b * P
                    source = turned[b][:, 2 * u + e].rearrange("p q m -> p (q m)")
                    nc.tensor.transpose(acc[:, j0 : j0 + P], source, ident[:])
            nc.scalar.copy(
                out=wg2_lead[:, 2 * u : 2 * u + 2, :], in_=acc[:].rearrange("p (e j) -> p e j", e=2)
            )

        v2 = [placed("v2_%d" % a, [P, S], U32, Y + 19 * a) for a in range(PASSES)]
        gather_words(v2[0][:], tab2_sb[0], list2, 0, S)
        gather_words(v2[1][:, 0:LEAD], tab2_sb[1], list2, 0, LEAD)
        gather_words(v2[1][:, LEAD:S], tab2_sb[1], list2, LEAD, S)

        page = [placed("page%d" % t, [P, T2], F32, 8 * t) for t in range(PACK)]
        h2 = [placed("h2_%d" % t, [P, S], F32, Z + 4 * t) for t in range(PACK)]
        used = []

        def fresh_bank():
            used.append(len(used))
            return bank(used[-1])

        def product(acc, weights, weight_planes, values, value_scales, split, j0, j1):
            for a in range(PASSES):
                nc.tensor.matmul_mx(
                    out=acc,
                    lhsT=weights[a],
                    lhsT_scale=weight_planes[a],
                    rhs=values[a][:, j0:j1].bitcast(FP8X4),
                    rhs_scale=value_scales[a][:, (H if j0 >= split else 0) + j0 : (H if j0 >= split else 0) + j1],
                    start=(a == 0),
                    stop=(a == PASSES - 1),
                )

        def wall_term(t, j0, j1):
            acc = fresh_bank()[:, 0 : j1 - j0]
            product(
                acc,
                [w3_sb[:, a, t * P : (t + 1) * P].bitcast(FP8X4) for a in range(PASSES)],
                [plane_bytes[a][:, LEAD + t * P : LEAD + (t + 1) * P] for a in range(PASSES)],
                v2, plane_bytes, LEAD, j0, j1,
            )
            nc.scalar.activation(h2[t][:, j0:j1], acc, IDENTITY, bias=wall_cols[:, t : t + 1], scale=-1.0)

        def scatter_weighted(t, offsets, j0, j1, values, weights):
            nc.vector.tensor_tensor(
                page[t][:].indirect(offsets[:, j0 // 16 : j1 // 16]), values, weights, MULT
            )

        def scatter(t, offsets, j0, j1, values):
            nc.vector.tensor_copy(page[t][:].indirect(offsets[:, j0 // 16 : j1 // 16]), values)

        for t in range(PACK):
            wall_term(t, 0, LEAD)
        for t in range(PACK):
            wall_term(t, LEAD, BANK)
            wall_term(t, BANK, S)
        for t in range(PACK):
            scatter_weighted(t, list4, 0, LEAD, h2[t][:, 0:LEAD], wg2_lead[:, t, :])
        for t in range(2):
            scatter_weighted(t, list4, LEAD, S, h2[t][:, LEAD:S], wg2_front[:, t, :])

        tab_sb.append(load_words("tab_1", tab_words, 1, Y + 2))
        wg2_back = [load_dealt("wg2_back%d" % t, Y + 27 - 3 * t, wg2, t, t + 1, LEAD, S) for t in range(2, PACK)]
        move_scales(stage1, 0, STAGE)
        w2_raw = placed("w2_raw", [P, PASSES, H // 2], I32, Y)
        nc.sync.dma_start(out=w2_raw[:], in_=w2_words.bitcast(I32).rearrange("a p c -> p a c"))

        w1_grouped = [placed("w1_grouped%d" % a, [P, H, PACK], BF16, 166 + 11 * a) for a in range(PASSES)]
        for a in range(PASSES):
            nc.scalar.copy(
                out=w1_grouped[a][:].rearrange("p (t m) i -> p m t i", t=PACK),
                in_=w1_raw[:, a].rearrange("p i (m t) -> p m t i", t=PACK),
            )
        kept_cols = held("kept_cols", [P, PACK], F32)
        nc.scalar.activation(kept_cols[:], rate_cols[:], COPY, bias=1.0, scale=-1.0)
        w2_sb = held("w2_sb", [P, PASSES, H], U16)
        nc.scalar.copy(
            out=w2_sb[:].rearrange("p a (t m) -> p a m t", t=PACK),
            in_=w2_raw[:].bitcast(U16).rearrange("p a (m t) -> p a m t", t=PACK),
        )
        w1_codes = held("w1_codes", [P, PASSES, H], U32)
        w1s = held("w1s", [P, PASSES, H], U8)
        for a in range(PASSES):
            quantize(w1_codes[:, a, :], w1s[:, a, :], w1_grouped[a][:])
        wg1_sb = [load_dealt("wg1_0", 160, wg1, 0, 2, 0, S)]
        w4_raw = placed("w4_raw", [P, PACK, N], F32, 179)
        nc.sync.dma_start(out=w4_raw[:], in_=w4.rearrange("(p t) n -> p t n", t=PACK))
        wg1_sb.append(load_dealt("wg1_1", 168, wg1, 2, PACK, 0, S))

        v1 = [placed("v1_%d" % a, [P, S], U32, Z + 4 - 4 * a) for a in range(PASSES)]
        gather_words(v1[0][:], tab_sb[0], list1, 0, S)
        for j0 in range(0, S, BANK):
            gather_words(v1[1][:, j0 : j0 + BANK], tab_sb[1], list1, j0, j0 + BANK)
        for t in range(2, PACK):
            weighted = placed("weighted%d" % t, [P, REST], F32, (176, X)[t - 2])
            nc.gpsimd.tensor_tensor(weighted[:], h2[t][:, LEAD:S], wg2_back[t - 2][:, 0, :], MULT)
            scatter(t, list4, LEAD, S, weighted[:])

        w2_bytes = w2_sb[:].bitcast(U8)
        kept = [placed("kept%d" % t, [P, S], F32, X + 22.25 + 4 * t) for t in range(PACK)]
        relaxed = [placed("relaxed%d" % t, [P, S], F32, (Y + 18, Z + 8, Z + 12, Y + 2)[t]) for t in range(PACK)]
        for t in range(PACK):
            rows = slice(t * P, (t + 1) * P)
            for j0 in range(0, S, BANK):
                step = 2 * (2 * t + j0 // BANK)
                acc = bank(step % 3)
                product(
                    acc[:], [w1_codes[:, a, rows].bitcast(FP8X4) for a in range(PASSES)],
                    [w1s[:, a, rows] for a in range(PASSES)], v1, plane_bytes, BANK, j0, j0 + BANK,
                )
                nc.scalar.activation(kept[t][:, j0 : j0 + BANK], acc[:], COPY, scale=kept_cols[:, t : t + 1])
                acc = bank((step + 1) % 3)
                product(
                    acc[:], [w2_bytes[:, a, 2 * t * P : 2 * (t + 1) * P].bitcast(FP4X4) for a in range(PASSES)],
                    [plane_bytes[a][:, BANK + t * P : BANK + (t + 1) * P] for a in range(PASSES)],
                    v1, plane_bytes, BANK, j0, j0 + BANK,
                )
                nc.scalar.activation(relaxed[t][:, j0 : j0 + BANK], acc[:], COPY, scale=rate_cols[:, t : t + 1])

        def add_terms(t, j0, j1, kib):
            summed = placed("summed%d_%d" % (t, j0), [P, j1 - j0], F32, kib)
            nc.gpsimd.tensor_tensor(summed[:], kept[t][:, j0:j1], relaxed[t][:, j0:j1], ADD)
            return summed

        def weigh(t, j0, j1, summed):
            nc.gpsimd.tensor_tensor(kept[t][:, j0:j1], summed, wg1_sb[t // 2][:, t % 2, j0:j1], MULT)

        halves = [add_terms(0, j0, j0 + BANK, 112 + j0 // 256) for j0 in range(0, S, BANK)]
        for h in range(2):
            weigh(0, h * BANK, (h + 1) * BANK, halves[h][:])
        for t in range(1, PACK):
            weigh(t, 0, S, add_terms(t, 0, S, 112)[:])
        for t in range(PACK):
            scatter(t, list3, 0, S, kept[t][:])

        w4_grouped = [placed("w4_grouped%d" % u, [P, BANK, PACK], BF16, Z + 4 * u) for u in range(2)]
        for u in range(2):
            interleave(nc.scalar.copy, w4_grouped[u][:], w4_raw[:, :, u * BANK : (u + 1) * BANK])

        grouped = {
            m0: placed("page_grouped%d" % m0, [P, m1 - m0, PACK], BF16, (179 if m1 < T2 else 160) + m0 // 128) for m0, m1 in PAGE_CHUNKS
        }

        for t in range(PACK - 1):
            width = 2 if t == PACK - 2 else 1
            for m0, m1 in PAGE_CHUNKS:
                dst = grouped[m0][:, :, t : t + width]
                src = page[t][:, m0:m1].unsqueeze(2).to_broadcast([P, m1 - m0, width])
                if m1 == T2:
                    nc.gpsimd.tensor_scalar(dst, src, 1.0, 0.0, MULT, ADD)
                else:
                    nc.scalar.copy(out=dst, in_=src)
        page_codes = held("page_codes", [P, T2], U32)
        page_s = held("page_s", [P, T2], U8)
        w4_codes = {}
        w4s = held("w4s", [P, N], U8)

        def quantize_w4(n0, n1, kib):
            u = n0 // BANK
            codes = placed("w4_codes%d" % n0, [P, n1 - n0], U32, kib)
            for n in range(n0, n1, P):
                w4_codes[n // P] = codes[:, n - n0 : n - n0 + P]
            quantize(codes[:], w4s[:, n0:n1], w4_grouped[u][:, n0 - u * BANK : n1 - u * BANK, :])

        def place_last(m0, m1):
            nc.vector.tensor_copy(out=grouped[m0][:, 0 : m1 - m0, PACK - 1], in_=page[PACK - 1][:, m0:m1])

        def quantize_page(m0, m1):
            cuts = [m0] + list(range((m0 // BANK + 1) * BANK, m1, BANK)) + [m1]
            for c0, c1 in zip(cuts, cuts[1:]):
                quantize(page_codes[:, c0:c1], page_s[:, c0:c1], grouped[m0][:, c0 - m0 : c1 - m0, :])

        nc.scalar.copy(out=grouped[BANK][:, P:BANK, PACK - 1], in_=page[PACK - 1][:, BANK + P : 2 * BANK])
        quantize_w4(0, 256, 112)
        place_last(*PAGE_CHUNKS[0])
        quantize_w4(256, 512, 113)
        quantize_page(*PAGE_CHUNKS[0])
        place_last(*PAGE_CHUNKS[1])
        quantize_w4(512, 1024, 114)
        quantize_page(*PAGE_CHUNKS[1])
        place_last(BANK, BANK + P)
        for c in range(2, len(PAGE_CHUNKS) - 1):
            place_last(*PAGE_CHUNKS[c + 1])
            quantize_page(*PAGE_CHUNKS[c])
        quantize_page(*PAGE_CHUNKS[-1])

        staged = [placed("staged%d" % u, [P, 2, T2], F32, (128, 144, X + 6.25, Y + 2)[u]) for u in range(4)]
        out_rows = out.rearrange("(u e p) m -> u p e m", e=2, p=P)

        def last_product(dst, n, m0, m1):
            nc.tensor.matmul_mx(
                out=dst,
                lhsT=w4_codes[n].bitcast(FP8X4),
                lhsT_scale=w4s[:, n * P : (n + 1) * P],
                rhs=page_codes[:, m0:m1].bitcast(FP8X4),
                rhs_scale=page_s[:, m0:m1],
                start=True,
                stop=True,
            )

        def half_bank(n, m0, engine_copy):
            acc = fresh_bank()
            last_product(acc[:, 0:NARROW], n, m0, m0 + NARROW)
            engine_copy(out=staged[n // 2][:, n % 2, m0 : m0 + NARROW], in_=acc[:, 0:NARROW])

        def full_bank(n, m0, engine_copy):
            acc = fresh_bank()
            last_product(acc[:], n, m0, m0 + BANK)
            engine_copy(out=staged[n // 2][:, n % 2, m0 : m0 + BANK], in_=acc[:])

        def store(n, m0, m1):
            nc.sync.dma_start(out=out_rows[n // 2][:, n % 2, m0:m1], in_=staged[n // 2][:, n % 2, m0:m1])

        on_scalar, on_vector = nc.scalar.copy, nc.vector.tensor_copy
        low, high = range(N // P // 2), range(N // P // 2, N // P)
        for n in low:
            half_bank(n, 0, on_scalar)
            store(n, 0, NARROW)
        for n in high:
            acc = fresh_bank()
            step = NARROW if n == high[0] else BANK
            for m0 in range(0, BANK, step):
                last_product(acc[:, m0 : m0 + step], n, m0, m0 + step)
            on_scalar(out=staged[n // 2][:, n % 2, 0:BANK], in_=acc[:])
            store(n, 0, BANK)
        for n in low:
            half_bank(n, NARROW, on_scalar)
            full_bank(n, BANK, on_scalar)
            if n in low[:2]:
                store(n, NARROW, 2 * BANK)
            else:
                for m0 in (2 * BANK, 3 * BANK):
                    full_bank(n, m0, on_vector)
                store(n, NARROW, T2)
        for u in (2, 3):
            for n in (2 * u, 2 * u + 1):
                for c, m0 in enumerate(range(BANK, T2, BANK)):
                    full_bank(n, m0, on_vector if (n + c) % 2 == 0 else on_scalar)
            nc.sync.dma_start(out=out_rows[u][:, :, BANK:T2], in_=staged[u][:, :, BANK:T2])
        for n in low[:2]:
            full_bank(n, 2 * BANK, on_scalar)
            full_bank(n, 3 * BANK, on_vector)
        nc.sync.dma_start(out=out_rows[0][:, :, 2 * BANK : T2], in_=staged[0][:, :, 2 * BANK : T2])
